import numpy as np
import ml_dtypes


def mxq(x, axis, fmt="e4m3"):
    dtype, down = {"e4m3": (ml_dtypes.float8_e4m3fn, 7), "e5m2": (ml_dtypes.float8_e5m2, 14)}[fmt]
    v = np.moveaxis(np.asarray(x, np.float32).astype(ml_dtypes.bfloat16).astype(np.float64), axis, -1)
    blocks = v.reshape(v.shape[:-1] + (-1, 32))
    amax = np.abs(blocks).max(-1, keepdims=True)
    byte = np.maximum(np.where(amax > 0, np.frexp(amax)[1] - 1 + 127, 0) - down, 1)
    scale = np.exp2(byte - 127.0)
    codes = (blocks / scale).astype(np.float32).astype(dtype).astype(np.float64)
    return np.moveaxis((codes * scale).reshape(v.shape), -1, axis)


WIDE = False


def mx_kscale(k):
    if not WIDE:
        return np.ones(k)
    levels = np.array([30, -30])
    if k % 512:
        return np.exp2(np.random.permutation(np.resize(levels, k // 32))).repeat(32)
    a = np.empty((k // 512, 16))
    for p in range(k // 512):
        a[p, :8] = np.random.permutation(np.resize(levels, 8))
        for g in range(8):
            far = levels[np.abs(levels - a[p, g]) >= 10]
            a[p, g + 8] = far[np.random.randint(len(far))]
    return np.exp2(a.ravel()).repeat(32)


def f64(x):
    return np.asarray(x).astype(np.float64)


def striped(idx):
    return np.tile(idx.reshape(-1, 16).T, (8, 1)).astype(np.uint16)


def unstriped(offs):
    return offs[:16].T.reshape(-1).astype(np.int64)


def bf(x):
    return np.asarray(x, np.float32).astype(ml_dtypes.bfloat16)


E2M1 = np.array([0.0, 0.5, 1.0, 1.5, 2.0, 3.0, 4.0, 6.0, -0.0, -0.5, -1.0, -1.5, -2.0, -3.0, -4.0, -6.0])


def pack_weight(w, fmt):
    k, n = w.shape
    w = f64(bf(w)).reshape(k // 32, 32, n)
    amax = np.abs(w).max(1)
    if fmt in ("e4m3", "e5m2"):
        byte = np.frexp(amax)[1] - 1 + 127 - (7 if fmt == "e4m3" else 14)
    else:
        mant, ex = np.frexp(amax / 6.0)
        byte = np.where(mant > 0.5, ex, ex - 1) + 127
    byte = np.clip(np.where(amax > 0, byte, 1), 1, 254)
    scaled = (w * np.exp2(127.0 - byte)[:, None, :]).reshape(k, n).astype(np.float32)
    by_word = np.ascontiguousarray(scaled.reshape(k // 512, 128, 4, n).transpose(0, 1, 3, 2))
    if fmt in ("e4m3", "e5m2"):
        words = by_word.astype(ml_dtypes.float8_e4m3fn if fmt == "e4m3" else ml_dtypes.float8_e5m2).view(np.uint8)
    else:
        c = by_word.astype(ml_dtypes.float4_e2m1fn).view(np.uint8) & 0xF
        words = c[..., 0::2] | (c[..., 1::2] << 4)
    return np.ascontiguousarray(words), np.ascontiguousarray(byte.astype(np.uint8).reshape(k // 512, 16, n))


def unpack_weight(words, scales, fmt):
    g, p, n, _ = words.shape
    if fmt in ("e4m3", "e5m2"):
        vals = np.ascontiguousarray(words).view(ml_dtypes.float8_e4m3fn if fmt == "e4m3" else ml_dtypes.float8_e5m2).astype(np.float64)
    else:
        nib = np.empty((g, p, n, 4), np.uint8)
        nib[..., 0::2] = words & 0xF
        nib[..., 1::2] = words >> 4
        vals = E2M1[nib]
    vals = vals * np.repeat(np.exp2(scales.astype(np.float64) - 127.0), 8, axis=1)[..., None]
    return vals.transpose(0, 1, 3, 2).reshape(g * 512, n)


K, H, N, T, S, T2 = 1024, 512, 1024, 2048, 1024, 2048

def setup_inputs():
    n = np.random.standard_normal
    s = mx_kscale(K)[:, None]
    u = mx_kscale(H)[:, None]
    tab = n((K, T)) * np.exp(1.0 * n((1, T))) * s
    tab_words, tab_scales = pack_weight(tab, "e5m2")
    wa = n((K, H)) / np.sqrt(K) / s * u.T
    wb_words, wb_scales = pack_weight(n((K, H)) / np.sqrt(K) / s, "e4m3")
    wo = n((H, N)) * np.sqrt(2 / H) / u
    return {
        "tab_words": tab_words, "tab_scales": tab_scales,
        "offs": striped(np.random.permutation(T)[:S]),
        "sT": n((H, T)).astype(np.float32),
        "wa": wa.astype(np.float32),
        "wb_words": wb_words, "wb_scales": wb_scales,
        "wo": wo.astype(np.float32),
        "wgo": np.exp(0.3 * n((128, S))).astype(np.float32),
        "offs2": striped(np.random.permutation(T2)[:S]),
    }

def reference(tab_words, tab_scales, offs, sT, wa, wb_words, wb_scales, wo, wgo, offs2):
    v = unpack_weight(tab_words, tab_scales, "e5m2")[:, unstriped(offs)]
    s_ = f64(sT)[:, unstriped(offs)]
    wb = unpack_weight(wb_words, wb_scales, "e4m3")
    a = mxq(f64(wa), 0, "e4m3").T @ v
    b = wb.T @ v
    h = a / (1.0 + np.abs(b)) * (s_ > 0)
    y = mxq(f64(wo), 0, "e4m3").T @ mxq(h, 0, "e4m3")
    out = np.zeros((N, T2))
    out[:, unstriped(offs2)] = np.tile(f64(wgo), (N // 128, 1)) * y
    return out

@@ -1,0 +1,207 @@
+from contextlib import ExitStack
+
+import concourse.mybir as mybir
+
+K, H, N, T, S, T2 = 1024, 512, 1024, 2048, 1024, 2048
+FLOPS = 2 * (2 * K * H * S + H * N * S)
+
+F32 = mybir.dt.float32
+BF16 = mybir.dt.bfloat16
+I32 = mybir.dt.int32
+U32 = mybir.dt.uint32
+U16 = mybir.dt.uint16
+U8 = mybir.dt.uint8
+E4M3 = mybir.dt.float8_e4m3fn_x4
+E5M2 = mybir.dt.float8_e5m2_x4
+ACT = mybir.ActivationFunctionType
+ALU = mybir.AluOpType
+
+P = 128
+PACK = 4
+PASSES = K // (P * PACK)
+CHUNK = 512
+CHUNKS = S // CHUNK
+LIST_ROWS = 16
+WO_PIECE = 256
+WINDOWS = 2
+
+
+def tile_list_spill_damped_grad_kernel(tc, tab_words, tab_scales, offs, sT, wa, wb_words, wb_scales, wo, wgo, offs2, out):
+    nc = tc.nc
+    with ExitStack() as ctx:
+        keep = ctx.enter_context(tc.tile_pool(name="keep", bufs=1))
+        ring = ctx.enter_context(tc.tile_pool(name="ring", bufs=2))
+        psum = ctx.enter_context(tc.psum_pool(name="psum", bufs=1))
+
+        def held(shape, dtype, name):
+            return keep.tile(shape, dtype, name=name, align_bytes=64)
+
+        picks = keep.tile([P, S // LIST_ROWS], U16, name="picks")
+        places = keep.tile([P, S // LIST_ROWS], U16, name="places")
+
+        tab_sc = held([P, T], U8, "tab_sc")
+        picked_sc = held([P, S], U8, "picked_sc")
+        v_sc = held([P, PASSES, S], U8, "v_sc")
+        wb_sc_raw = held([P, PASSES, H], U8, "wb_sc_raw")
+        wb_sc = held([P, PASSES, H], U8, "wb_sc")
+        windows = [held([P, T2], F32, "window0")]
+        warm = held([P, 8], F32, "warm")
+
+        nc.vector.memset(tab_sc[32:64, :].bitcast(I32), 0)
+        nc.vector.memset(tab_sc[64:128, :].bitcast(I32), 0)
+        nc.vector.memset(v_sc[:].rearrange("p a c -> p (a c)").bitcast(I32), 0)
+        nc.vector.memset(wb_sc[:].rearrange("p a c -> p (a c)").bitcast(I32), 0)
+        nc.vector.memset(windows[0][:], 0.0)
+        nc.gpsimd.memset(warm[:], 0.0)
+        nc.scalar.activation(warm[:], warm[:], ACT.Abs_reciprocal_sqrt, bias=1.0)
+
+        def shared(shape, dtype, name, tag):
+            return keep.tile(shape, dtype, name=name, tag=tag, align_bytes=64)
+
+        tab_w = [shared([P, T], I32, f"tab_w{a}", f"buffer{a}") for a in range(PASSES)]
+        wb_w_raw = shared([P, PASSES, H], I32, "wb_w_raw", "buffer2")
+        wa_raw = [held([P, PACK, H], F32, "wa_raw0")]
+        s_by_slot = sT.rearrange("(g t q) c -> t g q c", t=PACK, q=8)
+        s_rows = [shared([P, T], F32, "s_rows0", "buffer3")]
+
+        nc.sync.dma_start(picks[:], offs)
+        nc.sync.dma_start(places[:], offs2)
+        nc.sync.dma_start(tab_sc[0:32, :].bitcast(I32), tab_scales.rearrange("a q c -> q a c").bitcast(I32))
+        nc.sync.dma_start(tab_w[0][:], tab_words[0].rearrange("p c i -> p (c i)").bitcast(I32))
+        for q in range(4):
+            nc.sync.dma_start(
+                wb_sc_raw[32 * q : 32 * q + 4, :, :].bitcast(I32),
+                wb_scales[:, 4 * q : 4 * q + 4, :].rearrange("a r c -> r a c").bitcast(I32),
+            )
+        nc.sync.dma_start(tab_w[1][:], tab_words[1].rearrange("p c i -> p (c i)").bitcast(I32))
+        nc.sync.dma_start(wb_w_raw[:], wb_words.rearrange("a p c i -> p a (c i)").bitcast(I32))
+        nc.sync.dma_start(wa_raw[0][:], wa[0:512, :].rearrange("(p j) c -> p j c", j=PACK))
+        nc.sync.dma_start(s_rows[0][:], s_by_slot[0])
+
+        nc.vector.tensor_copy(picked_sc[:], tab_sc[:].indirect(picks[:]))
+        for q in range(4):
+            nc.scalar.dma_start(v_sc[32 * q : 32 * q + 4, :, :].bitcast(I32), picked_sc[8 * q : 8 * q + 8, :].bitcast(I32))
+        v_w = [held([P, S], U32, f"v_w{a}") for a in range(PASSES)]
+        nc.vector.tensor_copy(v_w[0][:], tab_w[0][:].bitcast(U32).indirect(picks[:]))
+        for q in range(4):
+            rows = slice(32 * q, 32 * q + 4)
+            nc.vector.tensor_copy(
+                wb_sc[rows].bitcast(I32).rearrange("p a (t g w) -> p a g t w", t=PACK, w=2),
+                wb_sc_raw[rows].bitcast(I32).rearrange("p a (g t w) -> p a g t w", t=PACK, w=2),
+            )
+        nc.vector.tensor_copy(v_w[1][:], tab_w[1][:].bitcast(U32).indirect(picks[:]))
+        wb_w = held([P, PASSES, H], I32, "wb_w")
+        nc.vector.tensor_copy(
+            wb_w[:].rearrange("p a (t g q) -> p a g t q", t=PACK, q=8),
+            wb_w_raw[:].rearrange("p a (g t q) -> p a g t q", t=PACK, q=8),
+        )
+        wa_raw.append(shared([P, PACK, H], F32, "wa_raw1", "buffer0"))
+        nc.sync.dma_start(wa_raw[1][:], wa[512:1024, :].rearrange("(p j) c -> p j c", j=PACK))
+        for t in (1, 2):
+            s_rows.append(shared([P, T], F32, f"s_rows{t}", f"buffer{t}"))
+            nc.sync.dma_start(s_rows[t][:], s_by_slot[t])
+
+        wa_w, wa_sc = [], []
+        for a in range(PASSES):
+            grouped = ring.tile([P, H * PACK], BF16, name="wa_grouped", align_bytes=64)
+            nc.scalar.copy(
+                grouped[:].rearrange("p (t g q j) -> p g t q j", t=PACK, q=8, j=PACK),
+                wa_raw[a][:].rearrange("p j (g t q) -> p g t q j", t=PACK, q=8),
+            )
+            wa_w.append(held([P, H], U32, f"wa_w{a}"))
+            wa_sc.append(held([P, H], U8, f"wa_sc{a}"))
+            nc.vector.quantize_mx(out=wa_w[a][:].bitcast(E4M3), scales=wa_sc[a][:], in_=grouped[:])
+
+        wo_raw = shared([P, PACK, N], F32, "wo_raw", "buffer0")
+        wo_by_slot = wo.rearrange("(g t q) c -> t g q c", t=PACK, q=8)
+        for t in range(PACK):
+            nc.sync.dma_start(wo_raw[:, t, :], wo_by_slot[t])
+
+        def project(acc, words, scales, c, t):
+            cols = slice(c * CHUNK, (c + 1) * CHUNK)
+            rows = slice(t * P, (t + 1) * P)
+            for a in range(PASSES):
+                nc.tensor.matmul_mx(
+                    out=acc[:],
+                    lhsT=words(a)[:, rows].bitcast(E4M3),
+                    lhsT_scale=scales(a)[:, rows],
+                    rhs=v_w[a][:, cols].bitcast(E5M2),
+                    rhs_scale=v_sc[:, a, cols],
+                    start=(a == 0),
+                    stop=(a == PASSES - 1),
+                )
+
+        damp = [held([P, PACK, CHUNK], F32, f"damp{c}") for c in range(CHUNKS)]
+        for c in range(CHUNKS):
+            for t in range(PACK):
+                b_acc = psum.tile([P, CHUNK], F32, name="b_acc", bufs=2)
+                project(b_acc, lambda a: wb_w[:, a, :], lambda a: wb_sc[:, a, :], c, t)
+                nc.scalar.activation(damp[c][:, t, :], b_acc[:], ACT.Abs)
+            flat = damp[c][:].rearrange("p t c -> p (t c)")
+            nc.scalar.activation(flat, flat, ACT.Abs_reciprocal_sqrt, bias=1.0)
+            nc.scalar.activation(flat, flat, ACT.Square)
+
+        masked = [held([P, PACK, CHUNK], F32, f"masked{c}") for c in range(CHUNKS)]
+        for t in range(PACK):
+            saved = ring.tile([P, S], F32, name="saved")
+            nc.vector.tensor_copy(saved[:], s_rows[t][:].indirect(picks[:]))
+            if t == 0:
+                s_rows.append(shared([P, T], F32, "s_rows3", "buffer3"))
+                nc.sync.dma_start(s_rows[3][:], s_by_slot[3])
+            if t == 1:
+                gains = shared([P, S], F32, "gains", "buffer1")
+                nc.sync.dma_start(gains[:], wgo)
+            if t == 3:
+                windows.append(shared([P, T2], F32, "window1", "buffer3"))
+                nc.gpsimd.memset(windows[1][:], 0.0)
+            for c in range(CHUNKS):
+                a_acc = psum.tile([P, CHUNK], F32, name="a_acc", bufs=4)
+                project(a_acc, lambda a: wa_w[a][:], lambda a: wa_sc[a][:], c, t)
+                nc.vector.scalar_tensor_tensor(
+                    masked[c][:, t, :], saved[:, c * CHUNK : (c + 1) * CHUNK], 0.0, a_acc[:], ALU.is_gt, ALU.mult
+                )
+
+        wo_w, wo_sc = [], []
+        for u in range(N // WO_PIECE):
+            grouped = keep.tile([P, WO_PIECE, PACK], BF16, name=f"wo_grouped{u}", align_bytes=64)
+            nc.scalar.copy(grouped[:], wo_raw[:, :, u * WO_PIECE : (u + 1) * WO_PIECE].rearrange("p j c -> p c j"))
+            wo_w.append(held([P, WO_PIECE], U32, f"wo_w{u}"))
+            wo_sc.append(held([P, WO_PIECE], U8, f"wo_sc{u}"))
+            nc.vector.quantize_mx(out=wo_w[u][:].bitcast(E4M3), scales=wo_sc[u][:], in_=grouped[:].rearrange("p c j -> p (c j)"))
+
+        h_w, h_sc = [], []
+        for c in range(CHUNKS):
+            grouped = ring.tile([P, CHUNK * PACK], BF16, name="h_grouped", align_bytes=64)
+            nc.vector.tensor_tensor(
+                grouped[:].rearrange("p (c i t) -> p c t i", i=2, t=PACK),
+                masked[c][:].rearrange("p t (c i) -> p c t i", i=2),
+                damp[c][:].rearrange("p t (c i) -> p c t i", i=2),
+                ALU.mult,
+            )
+            h_w.append(held([P, CHUNK], U32, f"h_w{c}"))
+            h_sc.append(held([P, CHUNK], U8, f"h_sc{c}"))
+            nc.vector.quantize_mx(out=h_w[c][:].bitcast(E4M3), scales=h_sc[c][:], in_=grouped[:])
+
+        for n in range(N // P):
+            y = ring.tile([P, S], F32, name="y")
+            u, first = divmod(n * P, WO_PIECE)
+            window = windows[n % WINDOWS]
+            for c in range(CHUNKS):
+                cols = slice(c * CHUNK, (c + 1) * CHUNK)
+                y_acc = psum.tile([P, CHUNK], F32, name="y_acc", bufs=2)
+                nc.tensor.matmul_mx(
+                    out=y_acc[:],
+                    lhsT=wo_w[u][:, first : first + P].bitcast(E4M3),
+                    lhsT_scale=wo_sc[u][:, first : first + P],
+                    rhs=h_w[c][:].bitcast(E4M3),
+                    rhs_scale=h_sc[c][:],
+                    start=True,
+                    stop=True,
+                )
+                nc.scalar.copy(y[:, cols], y_acc[:])
+                if n == 0:
+                    entries = slice(c * CHUNK // LIST_ROWS, (c + 1) * CHUNK // LIST_ROWS)
+                    nc.vector.tensor_tensor(window[:].indirect(places[:, entries]), y[:, cols], gains[:, cols], ALU.mult)
+            if n > 0:
+                nc.vector.tensor_tensor(window[:].indirect(places[:]), y[:], gains[:], ALU.mult)
+            nc.sync.dma_start(out[n * P : (n + 1) * P, :], window[:])

@@ -39,19 +39,18 @@ def tile_list_spill_damped_grad_kernel(tc, tab_words, tab_scales, offs, sT, wa, 
         picks = keep.tile([P, S // LIST_ROWS], U16, name="picks")
         places = keep.tile([P, S // LIST_ROWS], U16, name="places")
 
-        tab_sc = held([P, T], U8, "tab_sc")
+        tab_sc = keep.tile([P, T], U8, name="tab_sc", tag="buffer5", align_bytes=64)
         picked_sc = held([P, S], U8, "picked_sc")
         v_sc = held([P, PASSES, S], U8, "v_sc")
-        wb_sc_raw = held([P, PASSES, H], U8, "wb_sc_raw")
+        wb_sc_raw = keep.tile([P, PASSES, H], U8, name="wb_sc_raw", tag="buffer4", align_bytes=64)
         wb_sc = held([P, PASSES, H], U8, "wb_sc")
         windows = [held([P, T2], F32, "window0")]
         warm = held([P, 8], F32, "warm")
 
-        nc.vector.memset(tab_sc[32:64, :].bitcast(I32), 0)
-        nc.vector.memset(tab_sc[64:128, :].bitcast(I32), 0)
+        nc.vector.memset(tab_sc[0:96, :].bitcast(I32), 0)
         nc.vector.memset(v_sc[:].rearrange("p a c -> p (a c)").bitcast(I32), 0)
         nc.vector.memset(wb_sc[:].rearrange("p a c -> p (a c)").bitcast(I32), 0)
-        nc.vector.memset(windows[0][:], 0.0)
+        nc.vector.memset(windows[0][:].bitcast(I32), 0)
         nc.gpsimd.memset(warm[:], 0.0)
         nc.scalar.activation(warm[:], warm[:], ACT.Abs_reciprocal_sqrt, bias=1.0)
 
@@ -62,25 +61,25 @@ def tile_list_spill_damped_grad_kernel(tc, tab_words, tab_scales, offs, sT, wa, 
         wb_w_raw = shared([P, PASSES, H], I32, "wb_w_raw", "buffer2")
         wa_raw = [held([P, PACK, H], F32, "wa_raw0")]
         s_by_slot = sT.rearrange("(g t q) c -> t g q c", t=PACK, q=8)
-        s_rows = [shared([P, T], F32, "s_rows0", "buffer3")]
+        s_rows = [held([P, T], F32, "s_rows0")]
 
         nc.sync.dma_start(picks[:], offs)
-        nc.sync.dma_start(places[:], offs2)
-        nc.sync.dma_start(tab_sc[0:32, :].bitcast(I32), tab_scales.rearrange("a q c -> q a c").bitcast(I32))
-        nc.sync.dma_start(tab_w[0][:], tab_words[0].rearrange("p c i -> p (c i)").bitcast(I32))
+        nc.sync.dma_start(tab_sc[96:128, :].bitcast(I32), tab_scales.rearrange("a q c -> q a c").bitcast(I32))
+        for a in range(PASSES):
+            nc.sync.dma_start(tab_w[a][:], tab_words[a].rearrange("p c i -> p (c i)").bitcast(I32))
         for q in range(4):
             nc.sync.dma_start(
                 wb_sc_raw[32 * q : 32 * q + 4, :, :].bitcast(I32),
                 wb_scales[:, 4 * q : 4 * q + 4, :].rearrange("a r c -> r a c").bitcast(I32),
             )
-        nc.sync.dma_start(tab_w[1][:], tab_words[1].rearrange("p c i -> p (c i)").bitcast(I32))
         nc.sync.dma_start(wb_w_raw[:], wb_words.rearrange("a p c i -> p a (c i)").bitcast(I32))
         nc.sync.dma_start(wa_raw[0][:], wa[0:512, :].rearrange("(p j) c -> p j c", j=PACK))
         nc.sync.dma_start(s_rows[0][:], s_by_slot[0])
+        nc.sync.dma_start(places[:], offs2)
 
         nc.vector.tensor_copy(picked_sc[:], tab_sc[:].indirect(picks[:]))
         for q in range(4):
-            nc.scalar.dma_start(v_sc[32 * q : 32 * q + 4, :, :].bitcast(I32), picked_sc[8 * q : 8 * q + 8, :].bitcast(I32))
+            nc.scalar.dma_start(v_sc[32 * q : 32 * q + 4, :, :].bitcast(I32), picked_sc[96 + 8 * q : 96 + 8 * q + 8, :].bitcast(I32))
         v_w = [held([P, S], U32, f"v_w{a}") for a in range(PASSES)]
         nc.vector.tensor_copy(v_w[0][:], tab_w[0][:].bitcast(U32).indirect(picks[:]))
         for q in range(4):
@@ -95,10 +94,12 @@ def tile_list_spill_damped_grad_kernel(tc, tab_words, tab_scales, offs, sT, wa, 
             wb_w[:].rearrange("p a (t g q) -> p a g t q", t=PACK, q=8),
             wb_w_raw[:].rearrange("p a (g t q) -> p a g t q", t=PACK, q=8),
         )
-        wa_raw.append(shared([P, PACK, H], F32, "wa_raw1", "buffer0"))
+        windows.append(shared([P, T2], F32, "window1", "buffer4"))
+        nc.vector.memset(windows[1][:].bitcast(I32), 0)
+        wa_raw.append(shared([P, PACK, H], F32, "wa_raw1", "buffer5"))
         nc.sync.dma_start(wa_raw[1][:], wa[512:1024, :].rearrange("(p j) c -> p j c", j=PACK))
-        for t in (1, 2):
-            s_rows.append(shared([P, T], F32, f"s_rows{t}", f"buffer{t}"))
+        for t in (1, 2, 3):
+            s_rows.append(shared([P, T], F32, f"s_rows{t}", f"buffer{t - 1}"))
             nc.sync.dma_start(s_rows[t][:], s_by_slot[t])
 
         wa_w, wa_sc = [], []
@@ -112,10 +113,6 @@ def tile_list_spill_damped_grad_kernel(tc, tab_words, tab_scales, offs, sT, wa, 
             wa_sc.append(held([P, H], U8, f"wa_sc{a}"))
             nc.vector.quantize_mx(out=wa_w[a][:].bitcast(E4M3), scales=wa_sc[a][:], in_=grouped[:])
 
-        wo_raw = shared([P, PACK, N], F32, "wo_raw", "buffer0")
-        wo_by_slot = wo.rearrange("(g t q) c -> t g q c", t=PACK, q=8)
-        for t in range(PACK):
-            nc.sync.dma_start(wo_raw[:, t, :], wo_by_slot[t])
 
         def project(acc, words, scales, c, t):
             cols = slice(c * CHUNK, (c + 1) * CHUNK)
@@ -141,28 +138,20 @@ def tile_list_spill_damped_grad_kernel(tc, tab_words, tab_scales, offs, sT, wa, 
             nc.scalar.activation(flat, flat, ACT.Abs_reciprocal_sqrt, bias=1.0)
             nc.scalar.activation(flat, flat, ACT.Square)
 
-        masked = [held([P, PACK, CHUNK], F32, f"masked{c}") for c in range(CHUNKS)]
+        saved = []
         for t in range(PACK):
-            saved = ring.tile([P, S], F32, name="saved")
-            nc.vector.tensor_copy(saved[:], s_rows[t][:].indirect(picks[:]))
-            if t == 0:
-                s_rows.append(shared([P, T], F32, "s_rows3", "buffer3"))
-                nc.sync.dma_start(s_rows[3][:], s_by_slot[3])
-            if t == 1:
-                gains = shared([P, S], F32, "gains", "buffer1")
-                nc.sync.dma_start(gains[:], wgo)
-            if t == 3:
-                windows.append(shared([P, T2], F32, "window1", "buffer3"))
-                nc.gpsimd.memset(windows[1][:], 0.0)
-            for c in range(CHUNKS):
-                a_acc = psum.tile([P, CHUNK], F32, name="a_acc", bufs=4)
-                project(a_acc, lambda a: wa_w[a][:], lambda a: wa_sc[a][:], c, t)
-                nc.vector.scalar_tensor_tensor(
-                    masked[c][:, t, :], saved[:, c * CHUNK : (c + 1) * CHUNK], 0.0, a_acc[:], ALU.is_gt, ALU.mult
-                )
+            saved.append(held([P, S], F32, f"saved{t}"))
+            nc.vector.tensor_copy(saved[t][:], s_rows[t][:].indirect(picks[:]))
 
+        wo_raw = shared([P, PACK, N], F32, "wo_raw", "buffer0")
+        wo_by_slot = wo.rearrange("(g t q) c -> t g q c", t=PACK, q=8)
+        for t in range(PACK):
+            nc.sync.dma_start(wo_raw[:, t, :], wo_by_slot[t])
+        gains = shared([P, S], F32, "gains", "buffer1")
+        nc.sync.dma_start(gains[:], wgo)
         wo_w, wo_sc = [], []
-        for u in range(N // WO_PIECE):
+
+        def quantize_wo(u):
             grouped = keep.tile([P, WO_PIECE, PACK], BF16, name=f"wo_grouped{u}", align_bytes=64)
             nc.scalar.copy(grouped[:], wo_raw[:, :, u * WO_PIECE : (u + 1) * WO_PIECE].rearrange("p j c -> p c j"))
             wo_w.append(held([P, WO_PIECE], U32, f"wo_w{u}"))
@@ -170,38 +159,60 @@ def tile_list_spill_damped_grad_kernel(tc, tab_words, tab_scales, offs, sT, wa, 
             nc.vector.quantize_mx(out=wo_w[u][:].bitcast(E4M3), scales=wo_sc[u][:], in_=grouped[:].rearrange("p c j -> p (c j)"))
 
         h_w, h_sc = [], []
-        for c in range(CHUNKS):
-            grouped = ring.tile([P, CHUNK * PACK], BF16, name="h_grouped", align_bytes=64)
-            nc.vector.tensor_tensor(
-                grouped[:].rearrange("p (c i t) -> p c t i", i=2, t=PACK),
-                masked[c][:].rearrange("p t (c i) -> p c t i", i=2),
-                damp[c][:].rearrange("p t (c i) -> p c t i", i=2),
-                ALU.mult,
-            )
+
+        def hidden(c):
+            planes = ring.tile([P, PACK, CHUNK], BF16, name="h_planes")
+            for t in range(PACK):
+                a_acc = psum.tile([P, CHUNK], F32, name="a_acc", bufs=4)
+                project(a_acc, lambda a: wa_w[a][:], lambda a: wa_sc[a][:], c, t)
+                damped = ring.tile([P, CHUNK], F32, name="damped", bufs=4)
+                nc.vector.tensor_tensor(damped[:], a_acc[:], damp[c][:, t, :], ALU.mult)
+                nc.vector.scalar_tensor_tensor(
+                    planes[:, t, :], saved[t][:, c * CHUNK : (c + 1) * CHUNK], 0.0, damped[:], ALU.is_gt, ALU.mult
+                )
+            grouped = ring.tile([P, CHUNK, PACK], BF16, name="h_grouped", align_bytes=64)
+            nc.scalar.copy(grouped[:], planes[:].rearrange("p t c -> p c t"))
             h_w.append(held([P, CHUNK], U32, f"h_w{c}"))
             h_sc.append(held([P, CHUNK], U8, f"h_sc{c}"))
-            nc.vector.quantize_mx(out=h_w[c][:].bitcast(E4M3), scales=h_sc[c][:], in_=grouped[:])
+            nc.vector.quantize_mx(out=h_w[c][:].bitcast(E4M3), scales=h_sc[c][:], in_=grouped[:].rearrange("p c t -> p (c t)"))
 
-        for n in range(N // P):
-            y = ring.tile([P, S], F32, name="y")
+        def embed(y, n, c):
             u, first = divmod(n * P, WO_PIECE)
-            window = windows[n % WINDOWS]
+            y_acc = psum.tile([P, CHUNK], F32, name="y_acc", bufs=2)
+            nc.tensor.matmul_mx(
+                out=y_acc[:],
+                lhsT=wo_w[u][:, first : first + P].bitcast(E4M3),
+                lhsT_scale=wo_sc[u][:, first : first + P],
+                rhs=h_w[c][:].bitcast(E4M3),
+                rhs_scale=h_sc[c][:],
+                start=True,
+                stop=True,
+            )
+            nc.scalar.copy(y[:, c * CHUNK : (c + 1) * CHUNK], y_acc[:])
+
+        def place(y, n, first, count):
+            cols = slice(first, first + count)
+            entries = slice(first // LIST_ROWS, (first + count) // LIST_ROWS)
+            nc.vector.tensor_tensor(windows[n % WINDOWS][:].indirect(places[:, entries]), y[:, cols], gains[:, cols], ALU.mult)
+
+        def store(n):
+            nc.sync.dma_start(out[n * P : (n + 1) * P, :], windows[n % WINDOWS][:])
+
+        hidden(0)
+        quantize_wo(0)
+        hidden(1)
+        early = [ring.tile([P, S], F32, name="y", bufs=3) for n in range(WINDOWS)]
+        for c in range(CHUNKS):
+            for n in range(WINDOWS):
+                embed(early[n], n, c)
+                place(early[n], n, c * CHUNK, CHUNK)
+                if c == CHUNKS - 1:
+                    store(n)
+        for u in range(1, N // WO_PIECE):
+            quantize_wo(u)
+        for n in range(WINDOWS, N // P):
+            y = ring.tile([P, S], F32, name="y", bufs=3)
             for c in range(CHUNKS):
-                cols = slice(c * CHUNK, (c + 1) * CHUNK)
-                y_acc = psum.tile([P, CHUNK], F32, name="y_acc", bufs=2)
-                nc.tensor.matmul_mx(
-                    out=y_acc[:],
-                    lhsT=wo_w[u][:, first : first + P].bitcast(E4M3),
-                    lhsT_scale=wo_sc[u][:, first : first + P],
-                    rhs=h_w[c][:].bitcast(E4M3),
-                    rhs_scale=h_sc[c][:],
-                    start=True,
-                    stop=True,
-                )
-                nc.scalar.copy(y[:, cols], y_acc[:])
-                if n == 0:
-                    entries = slice(c * CHUNK // LIST_ROWS, (c + 1) * CHUNK // LIST_ROWS)
-                    nc.vector.tensor_tensor(window[:].indirect(places[:, entries]), y[:, cols], gains[:, cols], ALU.mult)
-            if n > 0:
-                nc.vector.tensor_tensor(window[:].indirect(places[:]), y[:], gains[:], ALU.mult)
-            nc.sync.dma_start(out[n * P : (n + 1) * P, :], window[:])
+                embed(y, n, c)
+            place(y, n, 0, S)
+            store(n)

@@ -23,7 +23,8 @@ CHUNK = 512
 CHUNKS = S // CHUNK
 LIST_ROWS = 16
 WO_PIECE = 256
-WINDOWS = 2
+WINDOWS = 3
+EARLY = 2
 
 
 def tile_list_spill_damped_grad_kernel(tc, tab_words, tab_scales, offs, sT, wa, wb_words, wb_scales, wo, wgo, offs2, out):
@@ -39,66 +40,59 @@ def tile_list_spill_damped_grad_kernel(tc, tab_words, tab_scales, offs, sT, wa, 
         picks = keep.tile([P, S // LIST_ROWS], U16, name="picks")
         places = keep.tile([P, S // LIST_ROWS], U16, name="places")
 
-        tab_sc = keep.tile([P, T], U8, name="tab_sc", tag="buffer5", align_bytes=64)
-        picked_sc = held([P, S], U8, "picked_sc")
-        v_sc = held([P, PASSES, S], U8, "v_sc")
-        wb_sc_raw = keep.tile([P, PASSES, H], U8, name="wb_sc_raw", tag="buffer4", align_bytes=64)
-        wb_sc = held([P, PASSES, H], U8, "wb_sc")
+        def shared(shape, dtype, name, tag):
+            return keep.tile(shape, dtype, name=name, tag=tag, align_bytes=64)
+
+        tab_sc = held([P, T], U8, "tab_sc")
+        picked_sc = shared([P, S], U8, "picked_sc", "buffer4")
+        wb_sc_raw = held([P, H], U8, "wb_sc_raw")
+        staged = shared([P, S + H], U8, "staged", "buffer5")
+        planes_sc = held([P, PASSES, S + H], U8, "planes_sc")
         windows = [held([P, T2], F32, "window0")]
         warm = held([P, 8], F32, "warm")
+        live = slice(96, 128)
 
         nc.vector.memset(tab_sc[0:96, :].bitcast(I32), 0)
-        nc.vector.memset(v_sc[:].rearrange("p a c -> p (a c)").bitcast(I32), 0)
-        nc.vector.memset(wb_sc[:].rearrange("p a c -> p (a c)").bitcast(I32), 0)
+        nc.vector.memset(planes_sc[:].rearrange("p a c -> p (a c)").bitcast(I32), 0)
         nc.vector.memset(windows[0][:].bitcast(I32), 0)
         nc.gpsimd.memset(warm[:], 0.0)
         nc.scalar.activation(warm[:], warm[:], ACT.Abs_reciprocal_sqrt, bias=1.0)
 
-        def shared(shape, dtype, name, tag):
-            return keep.tile(shape, dtype, name=name, tag=tag, align_bytes=64)
-
         tab_w = [shared([P, T], I32, f"tab_w{a}", f"buffer{a}") for a in range(PASSES)]
         wb_w_raw = shared([P, PASSES, H], I32, "wb_w_raw", "buffer2")
-        wa_raw = [held([P, PACK, H], F32, "wa_raw0")]
+        wa_raw = [shared([P, PACK, H], F32, "wa_raw0", "buffer3")]
         s_by_slot = sT.rearrange("(g t q) c -> t g q c", t=PACK, q=8)
-        s_rows = [held([P, T], F32, "s_rows0")]
 
         nc.sync.dma_start(picks[:], offs)
-        nc.sync.dma_start(tab_sc[96:128, :].bitcast(I32), tab_scales.rearrange("a q c -> q a c").bitcast(I32))
+        nc.sync.dma_start(tab_sc[live, :].bitcast(I32), tab_scales.rearrange("a q c -> q a c").bitcast(I32))
+        nc.sync.dma_start(wb_sc_raw[live, :].bitcast(I32), wb_scales.rearrange("a q c -> q a c").bitcast(I32))
         for a in range(PASSES):
             nc.sync.dma_start(tab_w[a][:], tab_words[a].rearrange("p c i -> p (c i)").bitcast(I32))
-        for q in range(4):
-            nc.sync.dma_start(
-                wb_sc_raw[32 * q : 32 * q + 4, :, :].bitcast(I32),
-                wb_scales[:, 4 * q : 4 * q + 4, :].rearrange("a r c -> r a c").bitcast(I32),
-            )
-        nc.sync.dma_start(wb_w_raw[:], wb_words.rearrange("a p c i -> p a (c i)").bitcast(I32))
         nc.sync.dma_start(wa_raw[0][:], wa[0:512, :].rearrange("(p j) c -> p j c", j=PACK))
-        nc.sync.dma_start(s_rows[0][:], s_by_slot[0])
+        nc.sync.dma_start(wb_w_raw[:], wb_words.rearrange("a p c i -> p a (c i)").bitcast(I32))
         nc.sync.dma_start(places[:], offs2)
 
+        nc.vector.tensor_copy(
+            staged[live, S:].bitcast(I32).rearrange("p (t g w) -> p g t w", t=PACK, w=2),
+            wb_sc_raw[live, :].bitcast(I32).rearrange("p (g t w) -> p g t w", t=PACK, w=2),
+        )
         nc.vector.tensor_copy(picked_sc[:], tab_sc[:].indirect(picks[:]))
+        nc.vector.tensor_copy(staged[live, 0:S].bitcast(I32), picked_sc[live, :].bitcast(I32))
         for q in range(4):
-            nc.scalar.dma_start(v_sc[32 * q : 32 * q + 4, :, :].bitcast(I32), picked_sc[96 + 8 * q : 96 + 8 * q + 8, :].bitcast(I32))
+            nc.sync.dma_start(planes_sc[32 * q : 32 * q + 4, :, :].bitcast(I32), staged[96 + 8 * q : 96 + 8 * q + 8, :].bitcast(I32))
+        s_rows = [shared([P, T], F32, "s_rows0", "buffer4")]
+        nc.sync.dma_start(s_rows[0][:], s_by_slot[0])
         v_w = [held([P, S], U32, f"v_w{a}") for a in range(PASSES)]
-        nc.vector.tensor_copy(v_w[0][:], tab_w[0][:].bitcast(U32).indirect(picks[:]))
-        for q in range(4):
-            rows = slice(32 * q, 32 * q + 4)
-            nc.vector.tensor_copy(
-                wb_sc[rows].bitcast(I32).rearrange("p a (t g w) -> p a g t w", t=PACK, w=2),
-                wb_sc_raw[rows].bitcast(I32).rearrange("p a (g t w) -> p a g t w", t=PACK, w=2),
-            )
-        nc.vector.tensor_copy(v_w[1][:], tab_w[1][:].bitcast(U32).indirect(picks[:]))
+        for a in range(PASSES):
+            nc.vector.tensor_copy(v_w[a][:], tab_w[a][:].bitcast(U32).indirect(picks[:]))
         wb_w = held([P, PASSES, H], I32, "wb_w")
         nc.vector.tensor_copy(
             wb_w[:].rearrange("p a (t g q) -> p a g t q", t=PACK, q=8),
             wb_w_raw[:].rearrange("p a (g t q) -> p a g t q", t=PACK, q=8),
         )
-        windows.append(shared([P, T2], F32, "window1", "buffer4"))
-        nc.vector.memset(windows[1][:].bitcast(I32), 0)
         wa_raw.append(shared([P, PACK, H], F32, "wa_raw1", "buffer5"))
         nc.sync.dma_start(wa_raw[1][:], wa[512:1024, :].rearrange("(p j) c -> p j c", j=PACK))
-        for t in (1, 2, 3):
+        for t in (1, 2):
             s_rows.append(shared([P, T], F32, f"s_rows{t}", f"buffer{t - 1}"))
             nc.sync.dma_start(s_rows[t][:], s_by_slot[t])
 
@@ -112,6 +106,9 @@ def tile_list_spill_damped_grad_kernel(tc, tab_words, tab_scales, offs, sT, wa, 
             wa_w.append(held([P, H], U32, f"wa_w{a}"))
             wa_sc.append(held([P, H], U8, f"wa_sc{a}"))
             nc.vector.quantize_mx(out=wa_w[a][:].bitcast(E4M3), scales=wa_sc[a][:], in_=grouped[:])
+            if a == 0:
+                s_rows.append(shared([P, T], F32, "s_rows3", "buffer3"))
+                nc.sync.dma_start(s_rows[3][:], s_by_slot[3])
 
 
         def project(acc, words, scales, c, t):
@@ -123,20 +120,11 @@ def tile_list_spill_damped_grad_kernel(tc, tab_words, tab_scales, offs, sT, wa, 
                     lhsT=words(a)[:, rows].bitcast(E4M3),
                     lhsT_scale=scales(a)[:, rows],
                     rhs=v_w[a][:, cols].bitcast(E5M2),
-                    rhs_scale=v_sc[:, a, cols],
+                    rhs_scale=planes_sc[:, a, cols],
                     start=(a == 0),
                     stop=(a == PASSES - 1),
                 )
 
-        damp = [held([P, PACK, CHUNK], F32, f"damp{c}") for c in range(CHUNKS)]
-        for c in range(CHUNKS):
-            for t in range(PACK):
-                b_acc = psum.tile([P, CHUNK], F32, name="b_acc", bufs=2)
-                project(b_acc, lambda a: wb_w[:, a, :], lambda a: wb_sc[:, a, :], c, t)
-                nc.scalar.activation(damp[c][:, t, :], b_acc[:], ACT.Abs)
-            flat = damp[c][:].rearrange("p t c -> p (t c)")
-            nc.scalar.activation(flat, flat, ACT.Abs_reciprocal_sqrt, bias=1.0)
-            nc.scalar.activation(flat, flat, ACT.Square)
 
         saved = []
         for t in range(PACK):
@@ -149,6 +137,9 @@ def tile_list_spill_damped_grad_kernel(tc, tab_words, tab_scales, offs, sT, wa, 
             nc.sync.dma_start(wo_raw[:, t, :], wo_by_slot[t])
         gains = shared([P, S], F32, "gains", "buffer1")
         nc.sync.dma_start(gains[:], wgo)
+        for i, tag in ((1, "buffer2"), (2, "buffer4")):
+            windows.append(shared([P, T2], F32, f"window{i}", tag))
+            nc.vector.memset(windows[i][:].bitcast(I32), 0)
         wo_w, wo_sc = [], []
 
         def quantize_wo(u):
@@ -161,14 +152,20 @@ def tile_list_spill_damped_grad_kernel(tc, tab_words, tab_scales, offs, sT, wa, 
         h_w, h_sc = [], []
 
         def hidden(c):
-            planes = ring.tile([P, PACK, CHUNK], BF16, name="h_planes")
+            planes = shared([P, PACK, CHUNK], BF16, f"h_planes{c}", f"buffer{6 + c}")
+            damped = shared([P, PACK, CHUNK], F32, f"damped{c}", "buffer3" if c else "buffer8")
             for t in range(PACK):
+                b_acc = psum.tile([P, CHUNK], F32, name="b_acc", bufs=2)
+                project(b_acc, lambda a: wb_w[:, a, :], lambda a: planes_sc[:, a, S:], c, t)
+                damp = ring.tile([P, CHUNK], F32, name="damp", bufs=CHUNKS * PACK)
+                nc.scalar.activation(damp[:], b_acc[:], ACT.Abs)
+                nc.scalar.activation(damp[:], damp[:], ACT.Abs_reciprocal_sqrt, bias=1.0)
+                nc.scalar.activation(damp[:], damp[:], ACT.Square)
                 a_acc = psum.tile([P, CHUNK], F32, name="a_acc", bufs=4)
                 project(a_acc, lambda a: wa_w[a][:], lambda a: wa_sc[a][:], c, t)
-                damped = ring.tile([P, CHUNK], F32, name="damped", bufs=4)
-                nc.vector.tensor_tensor(damped[:], a_acc[:], damp[c][:, t, :], ALU.mult)
+                nc.vector.tensor_tensor(damped[:, t, :], a_acc[:], damp[:], ALU.mult)
                 nc.vector.scalar_tensor_tensor(
-                    planes[:, t, :], saved[t][:, c * CHUNK : (c + 1) * CHUNK], 0.0, damped[:], ALU.is_gt, ALU.mult
+                    planes[:, t, :], saved[t][:, c * CHUNK : (c + 1) * CHUNK], 0.0, damped[:, t, :], ALU.is_gt, ALU.mult
                 )
             grouped = ring.tile([P, CHUNK, PACK], BF16, name="h_grouped", align_bytes=64)
             nc.scalar.copy(grouped[:], planes[:].rearrange("p t c -> p c t"))
@@ -201,16 +198,16 @@ def tile_list_spill_damped_grad_kernel(tc, tab_words, tab_scales, offs, sT, wa, 
         hidden(0)
         quantize_wo(0)
         hidden(1)
-        early = [ring.tile([P, S], F32, name="y", bufs=3) for n in range(WINDOWS)]
+        early = [shared([P, S], F32, f"y_early{n}", f"buffer{6 + n}") for n in range(EARLY)]
         for c in range(CHUNKS):
-            for n in range(WINDOWS):
+            for n in range(EARLY):
                 embed(early[n], n, c)
                 place(early[n], n, c * CHUNK, CHUNK)
                 if c == CHUNKS - 1:
                     store(n)
         for u in range(1, N // WO_PIECE):
             quantize_wo(u)
-        for n in range(WINDOWS, N // P):
+        for n in range(EARLY, N // P):
             y = ring.tile([P, S], F32, name="y", bufs=3)
             for c in range(CHUNKS):
                 embed(y, n, c)

@@ -24,92 +24,123 @@ CHUNKS = S // CHUNK
 LIST_ROWS = 16
 WO_PIECE = 256
 WINDOWS = 3
-EARLY = 2
 
 
 def tile_list_spill_damped_grad_kernel(tc, tab_words, tab_scales, offs, sT, wa, wb_words, wb_scales, wo, wgo, offs2, out):
     nc = tc.nc
     with ExitStack() as ctx:
         keep = ctx.enter_context(tc.tile_pool(name="keep", bufs=1))
-        ring = ctx.enter_context(tc.tile_pool(name="ring", bufs=2))
+        ring = ctx.enter_context(tc.tile_pool(name="ring", bufs=3))
         psum = ctx.enter_context(tc.psum_pool(name="psum", bufs=1))
 
-        def held(shape, dtype, name):
-            return keep.tile(shape, dtype, name=name, align_bytes=64)
+        def held(shape, dtype, name, tag=None):
+            return keep.tile(shape, dtype, name=name, tag=tag or name, align_bytes=64)
 
         picks = keep.tile([P, S // LIST_ROWS], U16, name="picks")
         places = keep.tile([P, S // LIST_ROWS], U16, name="places")
 
-        def shared(shape, dtype, name, tag):
-            return keep.tile(shape, dtype, name=name, tag=tag, align_bytes=64)
-
         tab_sc = held([P, T], U8, "tab_sc")
-        picked_sc = shared([P, S], U8, "picked_sc", "buffer4")
         wb_sc_raw = held([P, H], U8, "wb_sc_raw")
-        staged = shared([P, S + H], U8, "staged", "buffer5")
+        picked_sc = held([P, S], U8, "picked_sc")
+        staged = held([P, S + H], U8, "staged")
         planes_sc = held([P, PASSES, S + H], U8, "planes_sc")
         windows = [held([P, T2], F32, "window0")]
         warm = held([P, 8], F32, "warm")
         live = slice(96, 128)
 
         nc.vector.memset(tab_sc[0:96, :].bitcast(I32), 0)
+        nc.vector.memset(wb_sc_raw[0:96, :].bitcast(I32), 0)
         nc.vector.memset(planes_sc[:].rearrange("p a c -> p (a c)").bitcast(I32), 0)
         nc.vector.memset(windows[0][:].bitcast(I32), 0)
         nc.gpsimd.memset(warm[:], 0.0)
         nc.scalar.activation(warm[:], warm[:], ACT.Abs_reciprocal_sqrt, bias=1.0)
 
-        tab_w = [shared([P, T], I32, f"tab_w{a}", f"buffer{a}") for a in range(PASSES)]
-        wb_w_raw = shared([P, PASSES, H], I32, "wb_w_raw", "buffer2")
-        wa_raw = [shared([P, PACK, H], F32, "wa_raw0", "buffer3")]
-        s_by_slot = sT.rearrange("(g t q) c -> t g q c", t=PACK, q=8)
+        tab_w = [held([P, T], I32, f"tab_w{a}") for a in range(PASSES)]
+        wb_w_raw = held([P, PASSES, H], I32, "wb_w_raw")
+        wa_raw = [held([P, PACK, H], F32, "wa_raw0")]
+        s_by_slot = sT.rearrange("(p t) c -> t p c", t=PACK)
+        wa_by_pass = wa.rearrange("(a p j) c -> a p j c", a=PASSES, j=PACK)
 
         nc.sync.dma_start(picks[:], offs)
         nc.sync.dma_start(tab_sc[live, :].bitcast(I32), tab_scales.rearrange("a q c -> q a c").bitcast(I32))
         nc.sync.dma_start(wb_sc_raw[live, :].bitcast(I32), wb_scales.rearrange("a q c -> q a c").bitcast(I32))
+        nc.sync.dma_start(places[:], offs2)
         for a in range(PASSES):
             nc.sync.dma_start(tab_w[a][:], tab_words[a].rearrange("p c i -> p (c i)").bitcast(I32))
-        nc.sync.dma_start(wa_raw[0][:], wa[0:512, :].rearrange("(p j) c -> p j c", j=PACK))
+        nc.sync.dma_start(wa_raw[0][:], wa_by_pass[0])
         nc.sync.dma_start(wb_w_raw[:], wb_words.rearrange("a p c i -> p a (c i)").bitcast(I32))
-        nc.sync.dma_start(places[:], offs2)
 
         nc.vector.tensor_copy(
-            staged[live, S:].bitcast(I32).rearrange("p (t g w) -> p g t w", t=PACK, w=2),
-            wb_sc_raw[live, :].bitcast(I32).rearrange("p (g t w) -> p g t w", t=PACK, w=2),
+            staged[:, S:].rearrange("p (t m i) -> p m t i", t=PACK, i=16),
+            wb_sc_raw[:].rearrange("p (m i t) -> p m t i", t=PACK, i=16),
         )
         nc.vector.tensor_copy(picked_sc[:], tab_sc[:].indirect(picks[:]))
         nc.vector.tensor_copy(staged[live, 0:S].bitcast(I32), picked_sc[live, :].bitcast(I32))
         for q in range(4):
-            nc.sync.dma_start(planes_sc[32 * q : 32 * q + 4, :, :].bitcast(I32), staged[96 + 8 * q : 96 + 8 * q + 8, :].bitcast(I32))
-        s_rows = [shared([P, T], F32, "s_rows0", "buffer4")]
+            nc.scalar.dma_start(planes_sc[32 * q : 32 * q + 4, :, :].bitcast(I32), staged[96 + 8 * q : 96 + 8 * q + 8, :].bitcast(I32))
+        s_rows = [held([P, T], F32, "s_rows0", "picked_sc")]
         nc.sync.dma_start(s_rows[0][:], s_by_slot[0])
         v_w = [held([P, S], U32, f"v_w{a}") for a in range(PASSES)]
         for a in range(PASSES):
             nc.vector.tensor_copy(v_w[a][:], tab_w[a][:].bitcast(U32).indirect(picks[:]))
         wb_w = held([P, PASSES, H], I32, "wb_w")
         nc.vector.tensor_copy(
-            wb_w[:].rearrange("p a (t g q) -> p a g t q", t=PACK, q=8),
-            wb_w_raw[:].rearrange("p a (g t q) -> p a g t q", t=PACK, q=8),
+            wb_w[:].rearrange("p a (t m i) -> p a m t i", t=PACK, i=4),
+            wb_w_raw[:].rearrange("p a (m i t) -> p a m t i", t=PACK, i=4),
         )
-        wa_raw.append(shared([P, PACK, H], F32, "wa_raw1", "buffer5"))
-        nc.sync.dma_start(wa_raw[1][:], wa[512:1024, :].rearrange("(p j) c -> p j c", j=PACK))
-        for t in (1, 2):
-            s_rows.append(shared([P, T], F32, f"s_rows{t}", f"buffer{t - 1}"))
+        wa_raw.append(held([P, PACK, H], F32, "wa_raw1", "tab_w0"))
+        nc.sync.dma_start(wa_raw[1][:], wa_by_pass[1])
+        for t, tag in ((1, "tab_w1"), (2, "wb_w_raw")):
+            s_rows.append(held([P, T], F32, f"s_rows{t}", tag))
             nc.sync.dma_start(s_rows[t][:], s_by_slot[t])
+        windows.append(held([P, T2], F32, "window1", "staged"))
+        nc.vector.memset(windows[1][:].bitcast(I32), 0)
 
         wa_w, wa_sc = [], []
         for a in range(PASSES):
-            grouped = ring.tile([P, H * PACK], BF16, name="wa_grouped", align_bytes=64)
+            grouped = held([P, H * PACK], BF16, f"wa_grouped{a}")
             nc.scalar.copy(
-                grouped[:].rearrange("p (t g q j) -> p g t q j", t=PACK, q=8, j=PACK),
-                wa_raw[a][:].rearrange("p j (g t q) -> p g t q j", t=PACK, q=8),
+                grouped[:].rearrange("p (t m j) -> p m t j", t=PACK, j=PACK),
+                wa_raw[a][:].rearrange("p j (m t) -> p m t j", t=PACK),
             )
             wa_w.append(held([P, H], U32, f"wa_w{a}"))
             wa_sc.append(held([P, H], U8, f"wa_sc{a}"))
             nc.vector.quantize_mx(out=wa_w[a][:].bitcast(E4M3), scales=wa_sc[a][:], in_=grouped[:])
-            if a == 0:
-                s_rows.append(shared([P, T], F32, "s_rows3", "buffer3"))
-                nc.sync.dma_start(s_rows[3][:], s_by_slot[3])
+        s_rows.append(held([P, T], F32, "s_rows3", "wa_raw0"))
+        nc.sync.dma_start(s_rows[3][:], s_by_slot[3])
+        windows.append(held([P, T2], F32, "window2", "wa_grouped0"))
+        nc.vector.memset(windows[2][:].bitcast(I32), 0)
 
+        def entries(first, count):
+            return slice(first // LIST_ROWS, (first + count) // LIST_ROWS)
+
+        saved = {}
+
+        def pick_saved(t, c, tag=None):
+            saved[t, c] = held([P, CHUNK], F32, f"saved{t}_{c}", tag)
+            nc.vector.tensor_copy(saved[t, c][:], s_rows[t][:].indirect(picks[:, entries(c * CHUNK, CHUNK)]))
+
+        for t in range(PACK):
+            pick_saved(t, 0)
+            if t < 2:
+                pick_saved(t, 1)
+
+        wo_by_row = wo.rearrange("(p j) c -> p j c", j=PACK)
+        wo_first = held([P, PACK, WO_PIECE], F32, "wo_first", "picked_sc")
+        nc.sync.dma_start(wo_first[:], wo_by_row[:, :, 0:WO_PIECE])
+        gains = held([P, S], F32, "gains", "tab_w1")
+        nc.sync.dma_start(gains[:], wgo)
+        wo_rest = held([P, PACK, N - WO_PIECE], F32, "wo_rest", "tab_w0")
+        nc.sync.dma_start(wo_rest[:], wo_by_row[:, :, WO_PIECE:])
+        wo_w, wo_sc = [], []
+
+        def quantize_wo(u):
+            raw = wo_first[:] if u == 0 else wo_rest[:, :, (u - 1) * WO_PIECE : u * WO_PIECE]
+            grouped = held([P, WO_PIECE, PACK], BF16, f"wo_grouped{u}")
+            nc.scalar.copy(grouped[:], raw.rearrange("p j c -> p c j"))
+            wo_w.append(held([P, WO_PIECE], U32, f"wo_w{u}"))
+            wo_sc.append(held([P, WO_PIECE], U8, f"wo_sc{u}"))
+            nc.vector.quantize_mx(out=wo_w[u][:].bitcast(E4M3), scales=wo_sc[u][:], in_=grouped[:].rearrange("p c j -> p (c j)"))
 
         def project(acc, words, scales, c, t):
             cols = slice(c * CHUNK, (c + 1) * CHUNK)
@@ -125,50 +156,25 @@ def tile_list_spill_damped_grad_kernel(tc, tab_words, tab_scales, offs, sT, wa, 
                     stop=(a == PASSES - 1),
                 )
 
-
-        saved = []
-        for t in range(PACK):
-            saved.append(held([P, S], F32, f"saved{t}"))
-            nc.vector.tensor_copy(saved[t][:], s_rows[t][:].indirect(picks[:]))
-
-        wo_raw = shared([P, PACK, N], F32, "wo_raw", "buffer0")
-        wo_by_slot = wo.rearrange("(g t q) c -> t g q c", t=PACK, q=8)
-        for t in range(PACK):
-            nc.sync.dma_start(wo_raw[:, t, :], wo_by_slot[t])
-        gains = shared([P, S], F32, "gains", "buffer1")
-        nc.sync.dma_start(gains[:], wgo)
-        for i, tag in ((1, "buffer2"), (2, "buffer4")):
-            windows.append(shared([P, T2], F32, f"window{i}", tag))
-            nc.vector.memset(windows[i][:].bitcast(I32), 0)
-        wo_w, wo_sc = [], []
-
-        def quantize_wo(u):
-            grouped = keep.tile([P, WO_PIECE, PACK], BF16, name=f"wo_grouped{u}", align_bytes=64)
-            nc.scalar.copy(grouped[:], wo_raw[:, :, u * WO_PIECE : (u + 1) * WO_PIECE].rearrange("p j c -> p c j"))
-            wo_w.append(held([P, WO_PIECE], U32, f"wo_w{u}"))
-            wo_sc.append(held([P, WO_PIECE], U8, f"wo_sc{u}"))
-            nc.vector.quantize_mx(out=wo_w[u][:].bitcast(E4M3), scales=wo_sc[u][:], in_=grouped[:].rearrange("p c j -> p (c j)"))
-
         h_w, h_sc = [], []
 
         def hidden(c):
-            planes = shared([P, PACK, CHUNK], BF16, f"h_planes{c}", f"buffer{6 + c}")
-            damped = shared([P, PACK, CHUNK], F32, f"damped{c}", "buffer3" if c else "buffer8")
+            planes = held([P, PACK, CHUNK], BF16, f"h_planes{c}")
+            damped = held([P, PACK, CHUNK], F32, f"damped{c}")
             for t in range(PACK):
                 b_acc = psum.tile([P, CHUNK], F32, name="b_acc", bufs=2)
                 project(b_acc, lambda a: wb_w[:, a, :], lambda a: planes_sc[:, a, S:], c, t)
-                damp = ring.tile([P, CHUNK], F32, name="damp", bufs=CHUNKS * PACK)
+                damp = held([P, CHUNK], F32, f"damp{t}_{c}")
                 nc.scalar.activation(damp[:], b_acc[:], ACT.Abs)
                 nc.scalar.activation(damp[:], damp[:], ACT.Abs_reciprocal_sqrt, bias=1.0)
                 nc.scalar.activation(damp[:], damp[:], ACT.Square)
                 a_acc = psum.tile([P, CHUNK], F32, name="a_acc", bufs=4)
                 project(a_acc, lambda a: wa_w[a][:], lambda a: wa_sc[a][:], c, t)
                 nc.vector.tensor_tensor(damped[:, t, :], a_acc[:], damp[:], ALU.mult)
-                nc.vector.scalar_tensor_tensor(
-                    planes[:, t, :], saved[t][:, c * CHUNK : (c + 1) * CHUNK], 0.0, damped[:, t, :], ALU.is_gt, ALU.mult
-                )
-            grouped = ring.tile([P, CHUNK, PACK], BF16, name="h_grouped", align_bytes=64)
-            nc.scalar.copy(grouped[:], planes[:].rearrange("p t c -> p c t"))
+                nc.vector.scalar_tensor_tensor(planes[:, t, :], saved[t, c][:], 0.0, damped[:, t, :], ALU.is_gt, ALU.mult)
+            grouped = held([P, CHUNK, PACK], BF16, f"h_grouped{c}")
+            interleave = nc.scalar.copy if c else nc.vector.tensor_copy
+            interleave(grouped[:], planes[:].rearrange("p t c -> p c t"))
             h_w.append(held([P, CHUNK], U32, f"h_w{c}"))
             h_sc.append(held([P, CHUNK], U8, f"h_sc{c}"))
             nc.vector.quantize_mx(out=h_w[c][:].bitcast(E4M3), scales=h_sc[c][:], in_=grouped[:].rearrange("p c t -> p (c t)"))
@@ -185,31 +191,37 @@ def tile_list_spill_damped_grad_kernel(tc, tab_words, tab_scales, offs, sT, wa, 
                 start=True,
                 stop=True,
             )
-            nc.scalar.copy(y[:, c * CHUNK : (c + 1) * CHUNK], y_acc[:])
+            nc.scalar.copy(y, y_acc[:])
 
         def place(y, n, first, count):
-            cols = slice(first, first + count)
-            entries = slice(first // LIST_ROWS, (first + count) // LIST_ROWS)
-            nc.vector.tensor_tensor(windows[n % WINDOWS][:].indirect(places[:, entries]), y[:, cols], gains[:, cols], ALU.mult)
+            window = windows[n % WINDOWS][:].indirect(places[:, entries(first, count)])
+            nc.vector.tensor_tensor(window, y, gains[:, first : first + count], ALU.mult)
 
         def store(n):
             nc.sync.dma_start(out[n * P : (n + 1) * P, :], windows[n % WINDOWS][:])
 
+        def half(n, c, tag=None):
+            y = held([P, CHUNK], F32, f"y{n}_{c}", tag)
+            embed(y[:], n, c)
+            place(y[:], n, c * CHUNK, CHUNK)
+
         hidden(0)
         quantize_wo(0)
+        half(0, 0)
+        pick_saved(2, 1, "damped0")
+        pick_saved(3, 1, "saved3_0")
         hidden(1)
-        early = [shared([P, S], F32, f"y_early{n}", f"buffer{6 + n}") for n in range(EARLY)]
-        for c in range(CHUNKS):
-            for n in range(EARLY):
-                embed(early[n], n, c)
-                place(early[n], n, c * CHUNK, CHUNK)
-                if c == CHUNKS - 1:
-                    store(n)
-        for u in range(1, N // WO_PIECE):
+        quantize_wo(1)
+        half(1, 0, "damp3_1")
+        half(2, 0, "h_planes1")
+        for n in range(WINDOWS):
+            half(n, 1)
+            store(n)
+        for u in range(2, N // WO_PIECE):
             quantize_wo(u)
-        for n in range(EARLY, N // P):
-            y = ring.tile([P, S], F32, name="y", bufs=3)
+        for n in range(WINDOWS, N // P):
+            y = ring.tile([P, S], F32, name="y")
             for c in range(CHUNKS):
-                embed(y, n, c)
-            place(y, n, 0, S)
+                embed(y[:, c * CHUNK : (c + 1) * CHUNK], n, c)
+            place(y[:], n, 0, S)
             store(n)

@@ -56,8 +56,8 @@ def tile_list_spill_damped_grad_kernel(tc, tab_words, tab_scales, offs, sT, wa, 
         nc.scalar.activation(warm[:], warm[:], ACT.Abs_reciprocal_sqrt, bias=1.0)
 
         tab_w = [held([P, T], I32, f"tab_w{a}") for a in range(PASSES)]
-        wb_w_raw = held([P, PASSES, H], I32, "wb_w_raw")
         wa_raw = [held([P, PACK, H], F32, "wa_raw0")]
+        wb_w_raw = held([P, PASSES, H], I32, "wb_w_raw")
         s_by_slot = sT.rearrange("(p t) c -> t p c", t=PACK)
         wa_by_pass = wa.rearrange("(a p j) c -> a p j c", a=PASSES, j=PACK)
 
@@ -78,8 +78,8 @@ def tile_list_spill_damped_grad_kernel(tc, tab_words, tab_scales, offs, sT, wa, 
         nc.vector.tensor_copy(staged[live, 0:S].bitcast(I32), picked_sc[live, :].bitcast(I32))
         for q in range(4):
             nc.scalar.dma_start(planes_sc[32 * q : 32 * q + 4, :, :].bitcast(I32), staged[96 + 8 * q : 96 + 8 * q + 8, :].bitcast(I32))
-        s_rows = [held([P, T], F32, "s_rows0", "picked_sc")]
-        nc.sync.dma_start(s_rows[0][:], s_by_slot[0])
+        wa_raw.append(held([P, PACK, H], F32, "wa_raw1", "picked_sc"))
+        nc.sync.dma_start(wa_raw[1][:], wa_by_pass[1])
         v_w = [held([P, S], U32, f"v_w{a}") for a in range(PASSES)]
         for a in range(PASSES):
             nc.vector.tensor_copy(v_w[a][:], tab_w[a][:].bitcast(U32).indirect(picks[:]))
@@ -88,12 +88,11 @@ def tile_list_spill_damped_grad_kernel(tc, tab_words, tab_scales, offs, sT, wa, 
             wb_w[:].rearrange("p a (t m i) -> p a m t i", t=PACK, i=4),
             wb_w_raw[:].rearrange("p a (m i t) -> p a m t i", t=PACK, i=4),
         )
-        wa_raw.append(held([P, PACK, H], F32, "wa_raw1", "tab_w0"))
-        nc.sync.dma_start(wa_raw[1][:], wa_by_pass[1])
-        for t, tag in ((1, "tab_w1"), (2, "wb_w_raw")):
+        s_rows = []
+        for t, tag in ((0, "tab_w0"), (1, "tab_w1")):
             s_rows.append(held([P, T], F32, f"s_rows{t}", tag))
             nc.sync.dma_start(s_rows[t][:], s_by_slot[t])
-        windows.append(held([P, T2], F32, "window1", "staged"))
+        windows.append(held([P, T2], F32, "window1", "wb_w_raw"))
         nc.vector.memset(windows[1][:].bitcast(I32), 0)
 
         wa_w, wa_sc = [], []
@@ -106,10 +105,9 @@ def tile_list_spill_damped_grad_kernel(tc, tab_words, tab_scales, offs, sT, wa, 
             wa_w.append(held([P, H], U32, f"wa_w{a}"))
             wa_sc.append(held([P, H], U8, f"wa_sc{a}"))
             nc.vector.quantize_mx(out=wa_w[a][:].bitcast(E4M3), scales=wa_sc[a][:], in_=grouped[:])
-        s_rows.append(held([P, T], F32, "s_rows3", "wa_raw0"))
-        nc.sync.dma_start(s_rows[3][:], s_by_slot[3])
-        windows.append(held([P, T2], F32, "window2", "wa_grouped0"))
-        nc.vector.memset(windows[2][:].bitcast(I32), 0)
+        for t, tag in ((2, "wa_raw0"), (3, "wa_grouped0")):
+            s_rows.append(held([P, T], F32, f"s_rows{t}", tag))
+            nc.sync.dma_start(s_rows[t][:], s_by_slot[t])
 
         def entries(first, count):
             return slice(first // LIST_ROWS, (first + count) // LIST_ROWS)
@@ -128,9 +126,9 @@ def tile_list_spill_damped_grad_kernel(tc, tab_words, tab_scales, offs, sT, wa, 
         wo_by_row = wo.rearrange("(p j) c -> p j c", j=PACK)
         wo_first = held([P, PACK, WO_PIECE], F32, "wo_first", "picked_sc")
         nc.sync.dma_start(wo_first[:], wo_by_row[:, :, 0:WO_PIECE])
-        gains = held([P, S], F32, "gains", "tab_w1")
+        gains = held([P, S], F32, "gains", "tab_w0")
         nc.sync.dma_start(gains[:], wgo)
-        wo_rest = held([P, PACK, N - WO_PIECE], F32, "wo_rest", "tab_w0")
+        wo_rest = held([P, PACK, N - WO_PIECE], F32, "wo_rest", "tab_w1")
         nc.sync.dma_start(wo_rest[:], wo_by_row[:, :, WO_PIECE:])
         wo_w, wo_sc = [], []
 
@@ -158,23 +156,34 @@ def tile_list_spill_damped_grad_kernel(tc, tab_words, tab_scales, offs, sT, wa, 
 
         h_w, h_sc = [], []
 
-        def hidden(c):
-            planes = held([P, PACK, CHUNK], BF16, f"h_planes{c}")
-            damped = held([P, PACK, CHUNK], F32, f"damped{c}")
-            for t in range(PACK):
+        damp, planes, damped = {}, {}, {}
+
+        def damping(c, pair):
+            for t in pair:
                 b_acc = psum.tile([P, CHUNK], F32, name="b_acc", bufs=2)
                 project(b_acc, lambda a: wb_w[:, a, :], lambda a: planes_sc[:, a, S:], c, t)
-                damp = held([P, CHUNK], F32, f"damp{t}_{c}")
-                nc.scalar.activation(damp[:], b_acc[:], ACT.Abs)
-                nc.scalar.activation(damp[:], damp[:], ACT.Abs_reciprocal_sqrt, bias=1.0)
-                nc.scalar.activation(damp[:], damp[:], ACT.Square)
+                damp[t, c] = held([P, CHUNK], F32, f"damp{t}_{c}")
+                nc.scalar.activation(damp[t, c][:], b_acc[:], ACT.Abs)
+            for t in pair:
+                nc.scalar.activation(damp[t, c][:], damp[t, c][:], ACT.Abs_reciprocal_sqrt, bias=1.0)
+            for t in pair:
+                nc.scalar.activation(damp[t, c][:], damp[t, c][:], ACT.Square)
+
+        def products(c, pair):
+            for t in pair:
                 a_acc = psum.tile([P, CHUNK], F32, name="a_acc", bufs=4)
                 project(a_acc, lambda a: wa_w[a][:], lambda a: wa_sc[a][:], c, t)
-                nc.vector.tensor_tensor(damped[:, t, :], a_acc[:], damp[:], ALU.mult)
-                nc.vector.scalar_tensor_tensor(planes[:, t, :], saved[t, c][:], 0.0, damped[:, t, :], ALU.is_gt, ALU.mult)
+                nc.vector.tensor_tensor(damped[c][:, t, :], a_acc[:], damp[t, c][:], ALU.mult)
+            for t in pair:
+                nc.vector.scalar_tensor_tensor(planes[c][:, t, :], saved[t, c][:], 0.0, damped[c][:, t, :], ALU.is_gt, ALU.mult)
+
+        def open_chunk(c, tag=None):
+            planes[c] = held([P, PACK, CHUNK], BF16, f"h_planes{c}")
+            damped[c] = held([P, PACK, CHUNK], F32, f"damped{c}", tag)
+
+        def quantize_h(c):
             grouped = held([P, CHUNK, PACK], BF16, f"h_grouped{c}")
-            interleave = nc.scalar.copy if c else nc.vector.tensor_copy
-            interleave(grouped[:], planes[:].rearrange("p t c -> p c t"))
+            nc.scalar.copy(grouped[:], planes[c][:].rearrange("p t c -> p c t"))
             h_w.append(held([P, CHUNK], U32, f"h_w{c}"))
             h_sc.append(held([P, CHUNK], U8, f"h_sc{c}"))
             nc.vector.quantize_mx(out=h_w[c][:].bitcast(E4M3), scales=h_sc[c][:], in_=grouped[:].rearrange("p c t -> p (c t)"))
@@ -205,14 +214,27 @@ def tile_list_spill_damped_grad_kernel(tc, tab_words, tab_scales, offs, sT, wa, 
             embed(y[:], n, c)
             place(y[:], n, c * CHUNK, CHUNK)
 
-        hidden(0)
+        low, high = (0, 1), (2, 3)
+        open_chunk(0)
+        for pair in (low, high):
+            damping(0, pair)
+        for pair in (low, high):
+            products(0, pair)
+        damping(1, low)
         quantize_wo(0)
-        half(0, 0)
+        quantize_h(0)
         pick_saved(2, 1, "damped0")
         pick_saved(3, 1, "saved3_0")
-        hidden(1)
+        open_chunk(1, "h_grouped0")
+        products(1, low)
+        half(0, 0)
+        windows.append(held([P, T2], F32, "window2", "y0_0"))
+        nc.gpsimd.memset(windows[2][:].bitcast(I32), 0)
+        damping(1, high)
+        products(1, high)
         quantize_wo(1)
         half(1, 0, "damp3_1")
+        quantize_h(1)
         half(2, 0, "h_planes1")
         for n in range(WINDOWS):
             half(n, 1)

@@ -99,8 +99,8 @@ def tile_list_spill_damped_grad_kernel(tc, tab_words, tab_scales, offs, sT, wa, 
         for a in range(PASSES):
             grouped = held([P, H * PACK], BF16, f"wa_grouped{a}")
             nc.scalar.copy(
-                grouped[:].rearrange("p (t m j) -> p m t j", t=PACK, j=PACK),
-                wa_raw[a][:].rearrange("p j (m t) -> p m t j", t=PACK),
+                grouped[:].rearrange("p (t m j) -> p m j t", t=PACK, j=PACK),
+                wa_raw[a][:].rearrange("p j (m t) -> p m j t", t=PACK),
             )
             wa_w.append(held([P, H], U32, f"wa_w{a}"))
             wa_sc.append(held([P, H], U8, f"wa_sc{a}"))
@@ -135,7 +135,7 @@ def tile_list_spill_damped_grad_kernel(tc, tab_words, tab_scales, offs, sT, wa, 
         def quantize_wo(u):
             raw = wo_first[:] if u == 0 else wo_rest[:, :, (u - 1) * WO_PIECE : u * WO_PIECE]
             grouped = held([P, WO_PIECE, PACK], BF16, f"wo_grouped{u}")
-            nc.scalar.copy(grouped[:], raw.rearrange("p j c -> p c j"))
+            nc.scalar.copy(grouped[:].rearrange("p (c i) j -> p c j i", i=4), raw.rearrange("p j (c i) -> p c j i", i=4))
             wo_w.append(held([P, WO_PIECE], U32, f"wo_w{u}"))
             wo_sc.append(held([P, WO_PIECE], U8, f"wo_sc{u}"))
             nc.vector.quantize_mx(out=wo_w[u][:].bitcast(E4M3), scales=wo_sc[u][:], in_=grouped[:].rearrange("p c j -> p (c j)"))
@@ -183,7 +183,7 @@ def tile_list_spill_damped_grad_kernel(tc, tab_words, tab_scales, offs, sT, wa, 
 
         def quantize_h(c):
             grouped = held([P, CHUNK, PACK], BF16, f"h_grouped{c}")
-            nc.scalar.copy(grouped[:], planes[c][:].rearrange("p t c -> p c t"))
+            nc.scalar.copy(grouped[:].rearrange("p (c i) t -> p c t i", i=4), planes[c][:].rearrange("p t (c i) -> p c t i", i=4))
             h_w.append(held([P, CHUNK], U32, f"h_w{c}"))
             h_sc.append(held([P, CHUNK], U8, f"h_sc{c}"))
             nc.vector.quantize_mx(out=h_w[c][:].bitcast(E4M3), scales=h_sc[c][:], in_=grouped[:].rearrange("p c t -> p (c t)"))

@@ -45,15 +45,12 @@ def tile_list_spill_damped_grad_kernel(tc, tab_words, tab_scales, offs, sT, wa, 
         staged = held([P, S + H], U8, "staged")
         planes_sc = held([P, PASSES, S + H], U8, "planes_sc")
         windows = [held([P, T2], F32, "window0")]
-        warm = held([P, 8], F32, "warm")
         live = slice(96, 128)
 
         nc.vector.memset(tab_sc[0:96, :].bitcast(I32), 0)
         nc.vector.memset(wb_sc_raw[0:96, :].bitcast(I32), 0)
         nc.vector.memset(planes_sc[:].rearrange("p a c -> p (a c)").bitcast(I32), 0)
         nc.vector.memset(windows[0][:].bitcast(I32), 0)
-        nc.gpsimd.memset(warm[:], 0.0)
-        nc.scalar.activation(warm[:], warm[:], ACT.Abs_reciprocal_sqrt, bias=1.0)
 
         tab_w = [held([P, T], I32, f"tab_w{a}") for a in range(PASSES)]
         wa_raw = [held([P, PACK, H], F32, "wa_raw0")]
@@ -92,8 +89,6 @@ def tile_list_spill_damped_grad_kernel(tc, tab_words, tab_scales, offs, sT, wa, 
         for t, tag in ((0, "tab_w0"), (1, "tab_w1")):
             s_rows.append(held([P, T], F32, f"s_rows{t}", tag))
             nc.sync.dma_start(s_rows[t][:], s_by_slot[t])
-        windows.append(held([P, T2], F32, "window1", "wb_w_raw"))
-        nc.vector.memset(windows[1][:].bitcast(I32), 0)
 
         wa_w, wa_sc = [], []
         for a in range(PASSES):
@@ -228,8 +223,9 @@ def tile_list_spill_damped_grad_kernel(tc, tab_words, tab_scales, offs, sT, wa, 
         open_chunk(1, "h_grouped0")
         products(1, low)
         half(0, 0)
-        windows.append(held([P, T2], F32, "window2", "y0_0"))
-        nc.gpsimd.memset(windows[2][:].bitcast(I32), 0)
+        for i, tag in ((1, "damp0_1"), (2, "y0_0")):
+            windows.append(held([P, T2], F32, f"window{i}", tag))
+            nc.gpsimd.memset(windows[i][:].bitcast(I32), 0)
         damping(1, high)
         products(1, high)
         quantize_wo(1)

@@ -23,7 +23,7 @@ CHUNK = 512
 CHUNKS = S // CHUNK
 LIST_ROWS = 16
 WO_PIECE = 256
-WINDOWS = 3
+WINDOWS = 4
 
 
 def tile_list_spill_damped_grad_kernel(tc, tab_words, tab_scales, offs, sT, wa, wb_words, wb_scales, wo, wgo, offs2, out):
@@ -44,13 +44,11 @@ def tile_list_spill_damped_grad_kernel(tc, tab_words, tab_scales, offs, sT, wa, 
         picked_sc = held([P, S], U8, "picked_sc")
         staged = held([P, S + H], U8, "staged")
         planes_sc = held([P, PASSES, S + H], U8, "planes_sc")
-        windows = [held([P, T2], F32, "window0")]
         live = slice(96, 128)
 
         nc.vector.memset(tab_sc[0:96, :].bitcast(I32), 0)
         nc.vector.memset(wb_sc_raw[0:96, :].bitcast(I32), 0)
         nc.vector.memset(planes_sc[:].rearrange("p a c -> p (a c)").bitcast(I32), 0)
-        nc.vector.memset(windows[0][:].bitcast(I32), 0)
 
         tab_w = [held([P, T], I32, f"tab_w{a}") for a in range(PASSES)]
         wa_raw = [held([P, PACK, H], F32, "wa_raw0")]
@@ -75,8 +73,6 @@ def tile_list_spill_damped_grad_kernel(tc, tab_words, tab_scales, offs, sT, wa, 
         nc.vector.tensor_copy(staged[live, 0:S].bitcast(I32), picked_sc[live, :].bitcast(I32))
         for q in range(4):
             nc.scalar.dma_start(planes_sc[32 * q : 32 * q + 4, :, :].bitcast(I32), staged[96 + 8 * q : 96 + 8 * q + 8, :].bitcast(I32))
-        wa_raw.append(held([P, PACK, H], F32, "wa_raw1", "picked_sc"))
-        nc.sync.dma_start(wa_raw[1][:], wa_by_pass[1])
         v_w = [held([P, S], U32, f"v_w{a}") for a in range(PASSES)]
         for a in range(PASSES):
             nc.vector.tensor_copy(v_w[a][:], tab_w[a][:].bitcast(U32).indirect(picks[:]))
@@ -85,8 +81,10 @@ def tile_list_spill_damped_grad_kernel(tc, tab_words, tab_scales, offs, sT, wa, 
             wb_w[:].rearrange("p a (t m i) -> p a m t i", t=PACK, i=4),
             wb_w_raw[:].rearrange("p a (m i t) -> p a m t i", t=PACK, i=4),
         )
+        wa_raw.append(held([P, PACK, H], F32, "wa_raw1", "tab_w0"))
+        nc.sync.dma_start(wa_raw[1][:], wa_by_pass[1])
         s_rows = []
-        for t, tag in ((0, "tab_w0"), (1, "tab_w1")):
+        for t, tag in ((0, "tab_w1"), (1, "wb_w_raw")):
             s_rows.append(held([P, T], F32, f"s_rows{t}", tag))
             nc.sync.dma_start(s_rows[t][:], s_by_slot[t])
 
@@ -115,15 +113,15 @@ def tile_list_spill_damped_grad_kernel(tc, tab_words, tab_scales, offs, sT, wa, 
 
         for t in range(PACK):
             pick_saved(t, 0)
-            if t < 2:
+            if t == 0:
                 pick_saved(t, 1)
 
         wo_by_row = wo.rearrange("(p j) c -> p j c", j=PACK)
-        wo_first = held([P, PACK, WO_PIECE], F32, "wo_first", "picked_sc")
+        wo_first = held([P, PACK, WO_PIECE], F32, "wo_first", "tab_w0")
         nc.sync.dma_start(wo_first[:], wo_by_row[:, :, 0:WO_PIECE])
-        gains = held([P, S], F32, "gains", "tab_w0")
+        gains = held([P, S], F32, "gains", "tab_w1")
         nc.sync.dma_start(gains[:], wgo)
-        wo_rest = held([P, PACK, N - WO_PIECE], F32, "wo_rest", "tab_w1")
+        wo_rest = held([P, PACK, N - WO_PIECE], F32, "wo_rest", "wa_grouped1")
         nc.sync.dma_start(wo_rest[:], wo_by_row[:, :, WO_PIECE:])
         wo_w, wo_sc = [], []
 
@@ -215,23 +213,47 @@ def tile_list_spill_damped_grad_kernel(tc, tab_words, tab_scales, offs, sT, wa, 
             damping(0, pair)
         for pair in (low, high):
             products(0, pair)
+        windows = [held([P, T2], F32, "window0", "damp2_0")]
+        nc.gpsimd.memset(windows[0][:].bitcast(I32), 0)
         damping(1, low)
         quantize_wo(0)
         quantize_h(0)
+        pick_saved(1, 1, "saved3_0")
         pick_saved(2, 1, "damped0")
-        pick_saved(3, 1, "saved3_0")
-        open_chunk(1, "h_grouped0")
-        products(1, low)
+        planes[1] = held([P, PACK, CHUNK], BF16, "h_planes1")
+        rounded = held([P, PACK, CHUNK], BF16, "rounded", "h_grouped0")
+        mask = held([P, PACK, CHUNK], BF16, "mask", "h_planes0")
+
+        def rounded_products(pair):
+            for t in pair:
+                a_acc = psum.tile([P, CHUNK], F32, name="a_acc", bufs=4)
+                project(a_acc, lambda a: wa_w[a][:], lambda a: wa_sc[a][:], 1, t)
+                nc.vector.tensor_tensor(rounded[:, t, :], a_acc[:], damp[t, 1][:], ALU.mult)
+
+        def open_gates(pair):
+            for t in pair:
+                nc.scalar.activation(mask[:, t, :], saved[t, 1][:], ACT.Sign)
+            both = mask[:, pair[0] : pair[1] + 1, :]
+            nc.scalar.activation(both, both, ACT.Relu)
+
+        rounded_products(low)
+        pick_saved(3, 1, "damp1_1")
         half(0, 0)
         for i, tag in ((1, "damp0_1"), (2, "y0_0")):
             windows.append(held([P, T2], F32, f"window{i}", tag))
             nc.gpsimd.memset(windows[i][:].bitcast(I32), 0)
         damping(1, high)
-        products(1, high)
+        half(1, 0)
+        windows.append(held([P, T2], F32, "window3", "y1_0"))
+        nc.gpsimd.memset(windows[3][:].bitcast(I32), 0)
         quantize_wo(1)
-        half(1, 0, "damp3_1")
+        for pair in (low, high):
+            open_gates(pair)
+        rounded_products(high)
+        nc.vector.tensor_tensor(planes[1][:], mask[:], rounded[:], ALU.mult)
+        half(2, 0, "damp1_1")
         quantize_h(1)
-        half(2, 0, "h_planes1")
+        half(3, 0, "h_planes1")
         for n in range(WINDOWS):
             half(n, 1)
             store(n)

@@ -22,19 +22,26 @@ PASSES = K // (P * PACK)
 CHUNK = 512
 CHUNKS = S // CHUNK
 LIST_ROWS = 16
+QUADRANT = 32
+SCALE_ROWS = 4
+LINE = 16
+WORDS_A_LINE = LINE // 4
 WO_PIECE = 256
 WINDOWS = 4
+Y_TILES = 3
+A_BANKS, B_BANKS, Y_BANKS = 4, 2, 2
+LOW, HIGH = (0, 1), (2, 3)
 
 
 def tile_list_spill_damped_grad_kernel(tc, tab_words, tab_scales, offs, sT, wa, wb_words, wb_scales, wo, wgo, offs2, out):
     nc = tc.nc
     with ExitStack() as ctx:
         keep = ctx.enter_context(tc.tile_pool(name="keep", bufs=1))
-        ring = ctx.enter_context(tc.tile_pool(name="ring", bufs=3))
+        ring = ctx.enter_context(tc.tile_pool(name="ring", bufs=Y_TILES))
         psum = ctx.enter_context(tc.psum_pool(name="psum", bufs=1))
 
-        def held(shape, dtype, name, tag=None):
-            return keep.tile(shape, dtype, name=name, tag=tag or name, align_bytes=64)
+        def held(shape, dtype, name, after=None):
+            return keep.tile(shape, dtype, name=name, tag=after or name, align_bytes=64)
 
         picks = keep.tile([P, S // LIST_ROWS], U16, name="picks")
         places = keep.tile([P, S // LIST_ROWS], U16, name="places")
@@ -44,11 +51,15 @@ def tile_list_spill_damped_grad_kernel(tc, tab_words, tab_scales, offs, sT, wa, 
         picked_sc = held([P, S], U8, "picked_sc")
         staged = held([P, S + H], U8, "staged")
         planes_sc = held([P, PASSES, S + H], U8, "planes_sc")
-        live = slice(96, 128)
+        warm = held([P, 8], F32, "warm")
+        rest, last = slice(0, P - QUADRANT), slice(P - QUADRANT, P)
 
-        nc.vector.memset(tab_sc[0:96, :].bitcast(I32), 0)
-        nc.vector.memset(wb_sc_raw[0:96, :].bitcast(I32), 0)
+        nc.vector.memset(tab_sc[rest, :].bitcast(I32), 0)
+        nc.vector.memset(wb_sc_raw[rest, :].bitcast(I32), 0)
         nc.vector.memset(planes_sc[:].rearrange("p a c -> p (a c)").bitcast(I32), 0)
+
+        nc.vector.memset(warm[:], 0.0)
+        nc.scalar.activation(warm[:], warm[:], ACT.Abs_reciprocal_sqrt, bias=1.0)
 
         tab_w = [held([P, T], I32, f"tab_w{a}") for a in range(PASSES)]
         wa_raw = [held([P, PACK, H], F32, "wa_raw0")]
@@ -57,8 +68,8 @@ def tile_list_spill_damped_grad_kernel(tc, tab_words, tab_scales, offs, sT, wa, 
         wa_by_pass = wa.rearrange("(a p j) c -> a p j c", a=PASSES, j=PACK)
 
         nc.sync.dma_start(picks[:], offs)
-        nc.sync.dma_start(tab_sc[live, :].bitcast(I32), tab_scales.rearrange("a q c -> q a c").bitcast(I32))
-        nc.sync.dma_start(wb_sc_raw[live, :].bitcast(I32), wb_scales.rearrange("a q c -> q a c").bitcast(I32))
+        nc.sync.dma_start(tab_sc[last, :].bitcast(I32), tab_scales.rearrange("a q c -> q a c").bitcast(I32))
+        nc.sync.dma_start(wb_sc_raw[last, :].bitcast(I32), wb_scales.rearrange("a q c -> q a c").bitcast(I32))
         nc.sync.dma_start(places[:], offs2)
         for a in range(PASSES):
             nc.sync.dma_start(tab_w[a][:], tab_words[a].rearrange("p c i -> p (c i)").bitcast(I32))
@@ -66,95 +77,113 @@ def tile_list_spill_damped_grad_kernel(tc, tab_words, tab_scales, offs, sT, wa, 
         nc.sync.dma_start(wb_w_raw[:], wb_words.rearrange("a p c i -> p a (c i)").bitcast(I32))
 
         nc.vector.tensor_copy(
-            staged[:, S:].rearrange("p (t m i) -> p m t i", t=PACK, i=16),
-            wb_sc_raw[:].rearrange("p (m i t) -> p m t i", t=PACK, i=16),
+            staged[:, S:].rearrange("p (t m i) -> p m t i", t=PACK, i=LINE),
+            wb_sc_raw[:].rearrange("p (m i t) -> p m t i", t=PACK, i=LINE),
         )
         nc.vector.tensor_copy(picked_sc[:], tab_sc[:].indirect(picks[:]))
-        nc.vector.tensor_copy(staged[live, 0:S].bitcast(I32), picked_sc[live, :].bitcast(I32))
-        for q in range(4):
-            nc.scalar.dma_start(planes_sc[32 * q : 32 * q + 4, :, :].bitcast(I32), staged[96 + 8 * q : 96 + 8 * q + 8, :].bitcast(I32))
+        nc.vector.tensor_copy(staged[last, 0:S].bitcast(I32), picked_sc[last, :].bitcast(I32))
+        for q in range(P // QUADRANT):
+            first = last.start + q * SCALE_ROWS * PASSES
+            nc.scalar.dma_start(
+                planes_sc[QUADRANT * q : QUADRANT * q + SCALE_ROWS, :, :].bitcast(I32),
+                staged[first : first + SCALE_ROWS * PASSES, :].bitcast(I32),
+            )
         v_w = [held([P, S], U32, f"v_w{a}") for a in range(PASSES)]
         for a in range(PASSES):
             nc.vector.tensor_copy(v_w[a][:], tab_w[a][:].bitcast(U32).indirect(picks[:]))
         wb_w = held([P, PASSES, H], I32, "wb_w")
         nc.vector.tensor_copy(
-            wb_w[:].rearrange("p a (t m i) -> p a m t i", t=PACK, i=4),
-            wb_w_raw[:].rearrange("p a (m i t) -> p a m t i", t=PACK, i=4),
+            wb_w[:].rearrange("p a (t m i) -> p a m t i", t=PACK, i=WORDS_A_LINE),
+            wb_w_raw[:].rearrange("p a (m i t) -> p a m t i", t=PACK, i=WORDS_A_LINE),
         )
-        wa_raw.append(held([P, PACK, H], F32, "wa_raw1", "tab_w0"))
+
+        wa_raw.append(held([P, PACK, H], F32, "wa_raw1", after="tab_w0"))
         nc.sync.dma_start(wa_raw[1][:], wa_by_pass[1])
         s_rows = []
-        for t, tag in ((0, "tab_w1"), (1, "wb_w_raw")):
-            s_rows.append(held([P, T], F32, f"s_rows{t}", tag))
+
+        def load_slot(t, after):
+            s_rows.append(held([P, T], F32, f"s_rows{t}", after))
             nc.sync.dma_start(s_rows[t][:], s_by_slot[t])
+
+        load_slot(0, after="tab_w1")
+        load_slot(1, after="wb_w_raw")
 
         wa_w, wa_sc = [], []
         for a in range(PASSES):
-            grouped = held([P, H * PACK], BF16, f"wa_grouped{a}")
+            wa_grouped = held([P, H * PACK], BF16, f"wa_grouped{a}")
             nc.scalar.copy(
-                grouped[:].rearrange("p (t m j) -> p m j t", t=PACK, j=PACK),
+                wa_grouped[:].rearrange("p (t m j) -> p m j t", t=PACK, j=PACK),
                 wa_raw[a][:].rearrange("p j (m t) -> p m j t", t=PACK),
             )
             wa_w.append(held([P, H], U32, f"wa_w{a}"))
             wa_sc.append(held([P, H], U8, f"wa_sc{a}"))
-            nc.vector.quantize_mx(out=wa_w[a][:].bitcast(E4M3), scales=wa_sc[a][:], in_=grouped[:])
-        for t, tag in ((2, "wa_raw0"), (3, "wa_grouped0")):
-            s_rows.append(held([P, T], F32, f"s_rows{t}", tag))
-            nc.sync.dma_start(s_rows[t][:], s_by_slot[t])
+            nc.vector.quantize_mx(out=wa_w[a][:].bitcast(E4M3), scales=wa_sc[a][:], in_=wa_grouped[:])
+        load_slot(2, after="wa_raw0")
+        load_slot(3, after="wa_grouped0")
 
         def entries(first, count):
             return slice(first // LIST_ROWS, (first + count) // LIST_ROWS)
 
         saved = {}
 
-        def pick_saved(t, c, tag=None):
-            saved[t, c] = held([P, CHUNK], F32, f"saved{t}_{c}", tag)
+        def pick_saved(t, c, after=None):
+            saved[t, c] = held([P, CHUNK], F32, f"saved{t}_{c}", after)
             nc.vector.tensor_copy(saved[t, c][:], s_rows[t][:].indirect(picks[:, entries(c * CHUNK, CHUNK)]))
 
-        for t in range(PACK):
+        pick_saved(0, 0)
+        pick_saved(0, 1)
+        for t in range(1, PACK):
             pick_saved(t, 0)
-            if t == 0:
-                pick_saved(t, 1)
 
         wo_by_row = wo.rearrange("(p j) c -> p j c", j=PACK)
-        wo_first = held([P, PACK, WO_PIECE], F32, "wo_first", "tab_w0")
+        wo_first = held([P, PACK, WO_PIECE], F32, "wo_first", after="tab_w0")
         nc.sync.dma_start(wo_first[:], wo_by_row[:, :, 0:WO_PIECE])
-        gains = held([P, S], F32, "gains", "tab_w1")
+        gains = held([P, S], F32, "gains", after="tab_w1")
         nc.sync.dma_start(gains[:], wgo)
-        wo_rest = held([P, PACK, N - WO_PIECE], F32, "wo_rest", "wa_grouped1")
+        wo_rest = held([P, PACK, N - WO_PIECE], F32, "wo_rest", after="wa_grouped1")
         nc.sync.dma_start(wo_rest[:], wo_by_row[:, :, WO_PIECE:])
-        wo_w, wo_sc = [], []
+
+        def quantize_rows(rows, name):
+            columns = rows.shape[2]
+            grouped = held([P, columns, PACK], BF16, f"{name}_grouped")
+            nc.scalar.copy(
+                grouped[:].rearrange("p (c i) j -> p c j i", i=WORDS_A_LINE),
+                rows.rearrange("p j (c i) -> p c j i", i=WORDS_A_LINE),
+            )
+            words = held([P, columns], U32, f"{name}_words")
+            scales = held([P, columns], U8, f"{name}_scales")
+            nc.vector.quantize_mx(out=words[:].bitcast(E4M3), scales=scales[:], in_=grouped[:].rearrange("p c j -> p (c j)"))
+            return words, scales
+
+        wo_mx, h_mx = [], []
 
         def quantize_wo(u):
-            raw = wo_first[:] if u == 0 else wo_rest[:, :, (u - 1) * WO_PIECE : u * WO_PIECE]
-            grouped = held([P, WO_PIECE, PACK], BF16, f"wo_grouped{u}")
-            nc.scalar.copy(grouped[:].rearrange("p (c i) j -> p c j i", i=4), raw.rearrange("p j (c i) -> p c j i", i=4))
-            wo_w.append(held([P, WO_PIECE], U32, f"wo_w{u}"))
-            wo_sc.append(held([P, WO_PIECE], U8, f"wo_sc{u}"))
-            nc.vector.quantize_mx(out=wo_w[u][:].bitcast(E4M3), scales=wo_sc[u][:], in_=grouped[:].rearrange("p c j -> p (c j)"))
+            rows = wo_first[:] if u == 0 else wo_rest[:, :, (u - 1) * WO_PIECE : u * WO_PIECE]
+            wo_mx.append(quantize_rows(rows, f"wo{u}"))
 
-        def project(acc, words, scales, c, t):
+        def project(name, banks, words, scales, c, t):
+            acc = psum.tile([P, CHUNK], F32, name=name, bufs=banks)
             cols = slice(c * CHUNK, (c + 1) * CHUNK)
             rows = slice(t * P, (t + 1) * P)
             for a in range(PASSES):
                 nc.tensor.matmul_mx(
                     out=acc[:],
-                    lhsT=words(a)[:, rows].bitcast(E4M3),
-                    lhsT_scale=scales(a)[:, rows],
+                    lhsT=words[a][:, rows].bitcast(E4M3),
+                    lhsT_scale=scales[a][:, rows],
                     rhs=v_w[a][:, cols].bitcast(E5M2),
                     rhs_scale=planes_sc[:, a, cols],
                     start=(a == 0),
                     stop=(a == PASSES - 1),
                 )
+            return acc
 
-        h_w, h_sc = [], []
-
-        damp, planes, damped = {}, {}, {}
+        wb_words_by_pass = [wb_w[:, a, :] for a in range(PASSES)]
+        wb_scales_by_pass = [planes_sc[:, a, S:] for a in range(PASSES)]
+        damp = {}
 
         def damping(c, pair):
             for t in pair:
-                b_acc = psum.tile([P, CHUNK], F32, name="b_acc", bufs=2)
-                project(b_acc, lambda a: wb_w[:, a, :], lambda a: planes_sc[:, a, S:], c, t)
+                b_acc = project("b_acc", B_BANKS, wb_words_by_pass, wb_scales_by_pass, c, t)
                 damp[t, c] = held([P, CHUNK], F32, f"damp{t}_{c}")
                 nc.scalar.activation(damp[t, c][:], b_acc[:], ACT.Abs)
             for t in pair:
@@ -162,34 +191,28 @@ def tile_list_spill_damped_grad_kernel(tc, tab_words, tab_scales, offs, sT, wa, 
             for t in pair:
                 nc.scalar.activation(damp[t, c][:], damp[t, c][:], ACT.Square)
 
-        def products(c, pair):
+        def damped_products(c, pair, into):
             for t in pair:
-                a_acc = psum.tile([P, CHUNK], F32, name="a_acc", bufs=4)
-                project(a_acc, lambda a: wa_w[a][:], lambda a: wa_sc[a][:], c, t)
-                nc.vector.tensor_tensor(damped[c][:, t, :], a_acc[:], damp[t, c][:], ALU.mult)
-            for t in pair:
-                nc.vector.scalar_tensor_tensor(planes[c][:, t, :], saved[t, c][:], 0.0, damped[c][:, t, :], ALU.is_gt, ALU.mult)
+                a_acc = project("a_acc", A_BANKS, wa_w, wa_sc, c, t)
+                nc.vector.tensor_tensor(into[:, t, :], a_acc[:], damp[t, c][:], ALU.mult)
 
-        def open_chunk(c, tag=None):
-            planes[c] = held([P, PACK, CHUNK], BF16, f"h_planes{c}")
-            damped[c] = held([P, PACK, CHUNK], F32, f"damped{c}", tag)
+        windows = []
 
-        def quantize_h(c):
-            grouped = held([P, CHUNK, PACK], BF16, f"h_grouped{c}")
-            nc.scalar.copy(grouped[:].rearrange("p (c i) t -> p c t i", i=4), planes[c][:].rearrange("p t (c i) -> p c t i", i=4))
-            h_w.append(held([P, CHUNK], U32, f"h_w{c}"))
-            h_sc.append(held([P, CHUNK], U8, f"h_sc{c}"))
-            nc.vector.quantize_mx(out=h_w[c][:].bitcast(E4M3), scales=h_sc[c][:], in_=grouped[:].rearrange("p c t -> p (c t)"))
+        def open_window(after):
+            window = held([P, T2], F32, f"window{len(windows)}", after)
+            nc.gpsimd.memset(window[:].bitcast(I32), 0)
+            windows.append(window)
 
         def embed(y, n, c):
             u, first = divmod(n * P, WO_PIECE)
-            y_acc = psum.tile([P, CHUNK], F32, name="y_acc", bufs=2)
+            (wo_words, wo_scales), (h_words, h_scales) = wo_mx[u], h_mx[c]
+            y_acc = psum.tile([P, CHUNK], F32, name="y_acc", bufs=Y_BANKS)
             nc.tensor.matmul_mx(
                 out=y_acc[:],
-                lhsT=wo_w[u][:, first : first + P].bitcast(E4M3),
-                lhsT_scale=wo_sc[u][:, first : first + P],
-                rhs=h_w[c][:].bitcast(E4M3),
-                rhs_scale=h_sc[c][:],
+                lhsT=wo_words[:, first : first + P].bitcast(E4M3),
+                lhsT_scale=wo_scales[:, first : first + P],
+                rhs=h_words[:].bitcast(E4M3),
+                rhs_scale=h_scales[:],
                 start=True,
                 stop=True,
             )
@@ -202,62 +225,54 @@ def tile_list_spill_damped_grad_kernel(tc, tab_words, tab_scales, offs, sT, wa, 
         def store(n):
             nc.sync.dma_start(out[n * P : (n + 1) * P, :], windows[n % WINDOWS][:])
 
-        def half(n, c, tag=None):
-            y = held([P, CHUNK], F32, f"y{n}_{c}", tag)
+        def place_chunk(n, c, after=None):
+            y = held([P, CHUNK], F32, f"y{n}_{c}", after)
             embed(y[:], n, c)
             place(y[:], n, c * CHUNK, CHUNK)
 
-        low, high = (0, 1), (2, 3)
-        open_chunk(0)
-        for pair in (low, high):
+        h0 = held([P, PACK, CHUNK], BF16, "h0")
+        damped = held([P, PACK, CHUNK], F32, "damped")
+        for pair in (LOW, HIGH):
             damping(0, pair)
-        for pair in (low, high):
-            products(0, pair)
-        windows = [held([P, T2], F32, "window0", "damp2_0")]
-        nc.gpsimd.memset(windows[0][:].bitcast(I32), 0)
-        damping(1, low)
-        quantize_wo(0)
-        quantize_h(0)
-        pick_saved(1, 1, "saved3_0")
-        pick_saved(2, 1, "damped0")
-        planes[1] = held([P, PACK, CHUNK], BF16, "h_planes1")
-        rounded = held([P, PACK, CHUNK], BF16, "rounded", "h_grouped0")
-        mask = held([P, PACK, CHUNK], BF16, "mask", "h_planes0")
-
-        def rounded_products(pair):
+        for pair in (LOW, HIGH):
+            damped_products(0, pair, damped)
             for t in pair:
-                a_acc = psum.tile([P, CHUNK], F32, name="a_acc", bufs=4)
-                project(a_acc, lambda a: wa_w[a][:], lambda a: wa_sc[a][:], 1, t)
-                nc.vector.tensor_tensor(rounded[:, t, :], a_acc[:], damp[t, 1][:], ALU.mult)
+                nc.vector.scalar_tensor_tensor(h0[:, t, :], saved[t, 0][:], 0.0, damped[:, t, :], ALU.is_gt, ALU.mult)
+        open_window(after="damp2_0")
+        damping(1, LOW)
+        quantize_wo(0)
+        h_mx.append(quantize_rows(h0[:], "h0"))
 
-        def open_gates(pair):
+        pick_saved(1, 1, after="saved3_0")
+        pick_saved(2, 1, after="damped")
+        h1 = held([P, PACK, CHUNK], BF16, "h1")
+        rounded = held([P, PACK, CHUNK], BF16, "rounded", after="h0_grouped")
+        mask = held([P, PACK, CHUNK], BF16, "mask", after="h0")
+        damped_products(1, LOW, rounded)
+        pick_saved(3, 1, after="damp1_1")
+        place_chunk(0, 0)
+        open_window(after="damp0_1")
+        open_window(after="y0_0")
+        damping(1, HIGH)
+        place_chunk(1, 0)
+        open_window(after="y1_0")
+        quantize_wo(1)
+        for pair in (LOW, HIGH):
             for t in pair:
                 nc.scalar.activation(mask[:, t, :], saved[t, 1][:], ACT.Sign)
-            both = mask[:, pair[0] : pair[1] + 1, :]
-            nc.scalar.activation(both, both, ACT.Relu)
+            signs = mask[:, pair[0] : pair[-1] + 1, :]
+            nc.scalar.activation(signs, signs, ACT.Relu)
+        damped_products(1, HIGH, rounded)
+        nc.vector.tensor_tensor(h1[:], mask[:], rounded[:], ALU.mult)
 
-        rounded_products(low)
-        pick_saved(3, 1, "damp1_1")
-        half(0, 0)
-        for i, tag in ((1, "damp0_1"), (2, "y0_0")):
-            windows.append(held([P, T2], F32, f"window{i}", tag))
-            nc.gpsimd.memset(windows[i][:].bitcast(I32), 0)
-        damping(1, high)
-        half(1, 0)
-        windows.append(held([P, T2], F32, "window3", "y1_0"))
-        nc.gpsimd.memset(windows[3][:].bitcast(I32), 0)
-        quantize_wo(1)
-        for pair in (low, high):
-            open_gates(pair)
-        rounded_products(high)
-        nc.vector.tensor_tensor(planes[1][:], mask[:], rounded[:], ALU.mult)
-        half(2, 0, "damp1_1")
-        quantize_h(1)
-        half(3, 0, "h_planes1")
+        place_chunk(2, 0, after="damp1_1")
+        h_mx.append(quantize_rows(h1[:], "h1"))
+        place_chunk(3, 0, after="h1")
         for n in range(WINDOWS):
-            half(n, 1)
+            place_chunk(n, 1)
             store(n)
-        for u in range(2, N // WO_PIECE):
+
+        for u in range(WINDOWS * P // WO_PIECE, N // WO_PIECE):
             quantize_wo(u)
         for n in range(WINDOWS, N // P):
             y = ring.tile([P, S], F32, name="y")

@@ -21,13 +21,14 @@ PACK = 4
 PASSES = K // (P * PACK)
 CHUNK = 512
 CHUNKS = S // CHUNK
+HALF = CHUNK // 2
 LIST_ROWS = 16
 QUADRANT = 32
 SCALE_ROWS = 4
 LINE = 16
 WORDS_A_LINE = LINE // 4
 WO_PIECE = 256
-WINDOWS = 4
+WINDOWS = 5
 Y_TILES = 3
 A_BANKS, B_BANKS, Y_BANKS = 4, 2, 2
 LOW, HIGH = (0, 1), (2, 3)
@@ -97,29 +98,36 @@ def tile_list_spill_damped_grad_kernel(tc, tab_words, tab_scales, offs, sT, wa, 
             wb_w_raw[:].rearrange("p a (m i t) -> p a m t i", t=PACK, i=WORDS_A_LINE),
         )
 
-        wa_raw.append(held([P, PACK, H], F32, "wa_raw1", after="tab_w0"))
-        nc.sync.dma_start(wa_raw[1][:], wa_by_pass[1])
         s_rows = []
 
         def load_slot(t, after):
             s_rows.append(held([P, T], F32, f"s_rows{t}", after))
             nc.sync.dma_start(s_rows[t][:], s_by_slot[t])
 
-        load_slot(0, after="tab_w1")
+        load_slot(0, after="tab_w0")
+        wa_raw.append(held([P, PACK, H], F32, "wa_raw1", after="tab_w1"))
+        nc.sync.dma_start(wa_raw[1][:], wa_by_pass[1])
         load_slot(1, after="wb_w_raw")
 
-        wa_w, wa_sc = [], []
-        for a in range(PASSES):
-            wa_grouped = held([P, H * PACK], BF16, f"wa_grouped{a}")
+        wa_mx = {}
+
+        def quantize_wa(a, slots, after=None):
+            name = f"wa{a}_{slots[0]}"
+            grouped = held([P, len(slots) * P * PACK], BF16, f"{name}_grouped")
             nc.scalar.copy(
-                wa_grouped[:].rearrange("p (t m j) -> p m j t", t=PACK, j=PACK),
-                wa_raw[a][:].rearrange("p j (m t) -> p m j t", t=PACK),
+                grouped[:].rearrange("p (t m j) -> p m j t", t=len(slots), j=PACK),
+                wa_raw[a][:].rearrange("p j (m t) -> p m j t", t=PACK)[:, :, :, slots[0] : slots[-1] + 1],
             )
-            wa_w.append(held([P, H], U32, f"wa_w{a}"))
-            wa_sc.append(held([P, H], U8, f"wa_sc{a}"))
-            nc.vector.quantize_mx(out=wa_w[a][:].bitcast(E4M3), scales=wa_sc[a][:], in_=wa_grouped[:])
+            words = held([P, len(slots) * P], U32, f"{name}_words", after)
+            scales = held([P, len(slots) * P], U8, f"{name}_scales")
+            nc.vector.quantize_mx(out=words[:].bitcast(E4M3), scales=scales[:], in_=grouped[:])
+            for t in slots:
+                rows = slice((t - slots[0]) * P, (t - slots[0] + 1) * P)
+                wa_mx[a, t] = words[:, rows], scales[:, rows]
+
+        quantize_wa(0, LOW + HIGH)
         load_slot(2, after="wa_raw0")
-        load_slot(3, after="wa_grouped0")
+        load_slot(3, after="wa0_0_grouped")
 
         def entries(first, count):
             return slice(first // LIST_ROWS, (first + count) // LIST_ROWS)
@@ -130,46 +138,43 @@ def tile_list_spill_damped_grad_kernel(tc, tab_words, tab_scales, offs, sT, wa, 
             saved[t, c] = held([P, CHUNK], F32, f"saved{t}_{c}", after)
             nc.vector.tensor_copy(saved[t, c][:], s_rows[t][:].indirect(picks[:, entries(c * CHUNK, CHUNK)]))
 
-        pick_saved(0, 0)
-        pick_saved(0, 1)
-        for t in range(1, PACK):
+        for t in LOW:
+            pick_saved(t, 0)
+            pick_saved(t, 1)
+        quantize_wa(1, LOW, after="wb_w_raw")
+        quantize_wa(1, HIGH, after="wa1_0_grouped")
+        for t in HIGH:
             pick_saved(t, 0)
 
         wo_by_row = wo.rearrange("(p j) c -> p j c", j=PACK)
-        wo_first = held([P, PACK, WO_PIECE], F32, "wo_first", after="tab_w0")
-        nc.sync.dma_start(wo_first[:], wo_by_row[:, :, 0:WO_PIECE])
-        gains = held([P, S], F32, "gains", after="tab_w1")
-        nc.sync.dma_start(gains[:], wgo)
-        wo_rest = held([P, PACK, N - WO_PIECE], F32, "wo_rest", after="wa_grouped1")
-        nc.sync.dma_start(wo_rest[:], wo_by_row[:, :, WO_PIECE:])
 
-        def quantize_rows(rows, name):
+        def quantize_rows(rows, name, after=None, words_after=None):
             columns = rows.shape[2]
-            grouped = held([P, columns, PACK], BF16, f"{name}_grouped")
+            grouped = held([P, columns, PACK], BF16, f"{name}_grouped", after)
             nc.scalar.copy(
                 grouped[:].rearrange("p (c i) j -> p c j i", i=WORDS_A_LINE),
                 rows.rearrange("p j (c i) -> p c j i", i=WORDS_A_LINE),
             )
-            words = held([P, columns], U32, f"{name}_words")
+            words = held([P, columns], U32, f"{name}_words", words_after)
             scales = held([P, columns], U8, f"{name}_scales")
             nc.vector.quantize_mx(out=words[:].bitcast(E4M3), scales=scales[:], in_=grouped[:].rearrange("p c j -> p (c j)"))
             return words, scales
 
         wo_mx, h_mx = [], []
 
-        def quantize_wo(u):
+        def quantize_wo(u, after=None, words_after=None):
             rows = wo_first[:] if u == 0 else wo_rest[:, :, (u - 1) * WO_PIECE : u * WO_PIECE]
-            wo_mx.append(quantize_rows(rows, f"wo{u}"))
+            wo_mx.append(quantize_rows(rows, f"wo{u}", after, words_after))
 
-        def project(name, banks, words, scales, c, t):
+        def project(name, banks, weight, c, t):
             acc = psum.tile([P, CHUNK], F32, name=name, bufs=banks)
             cols = slice(c * CHUNK, (c + 1) * CHUNK)
-            rows = slice(t * P, (t + 1) * P)
             for a in range(PASSES):
+                words, scales = weight[a, t]
                 nc.tensor.matmul_mx(
                     out=acc[:],
-                    lhsT=words[a][:, rows].bitcast(E4M3),
-                    lhsT_scale=scales[a][:, rows],
+                    lhsT=words.bitcast(E4M3),
+                    lhsT_scale=scales,
                     rhs=v_w[a][:, cols].bitcast(E5M2),
                     rhs_scale=planes_sc[:, a, cols],
                     start=(a == 0),
@@ -177,23 +182,29 @@ def tile_list_spill_damped_grad_kernel(tc, tab_words, tab_scales, offs, sT, wa, 
                 )
             return acc
 
-        wb_words_by_pass = [wb_w[:, a, :] for a in range(PASSES)]
-        wb_scales_by_pass = [planes_sc[:, a, S:] for a in range(PASSES)]
+        wb_mx = {
+            (a, t): (wb_w[:, a, t * P : (t + 1) * P], planes_sc[:, a, S + t * P : S + (t + 1) * P])
+            for a in range(PASSES)
+            for t in range(PACK)
+        }
         damp = {}
 
-        def damping(c, pair):
+        def damping(c, pair, bank_name="b_acc", banks=B_BANKS, after=None):
+            size = {}
             for t in pair:
-                b_acc = project("b_acc", B_BANKS, wb_words_by_pass, wb_scales_by_pass, c, t)
+                b_acc = project(bank_name, banks, wb_mx, c, t)
+                size[t] = held([P, CHUNK], F32, f"size{t}_{c}", after)
+                after = None
+                nc.scalar.activation(size[t][:], b_acc[:], ACT.Abs)
+            for t in pair:
+                nc.scalar.activation(size[t][:], size[t][:], ACT.Abs_reciprocal_sqrt, bias=1.0)
+            for t in pair:
                 damp[t, c] = held([P, CHUNK], F32, f"damp{t}_{c}")
-                nc.scalar.activation(damp[t, c][:], b_acc[:], ACT.Abs)
-            for t in pair:
-                nc.scalar.activation(damp[t, c][:], damp[t, c][:], ACT.Abs_reciprocal_sqrt, bias=1.0)
-            for t in pair:
-                nc.scalar.activation(damp[t, c][:], damp[t, c][:], ACT.Square)
+                nc.scalar.activation(damp[t, c][:], size[t][:], ACT.Square)
 
         def damped_products(c, pair, into):
             for t in pair:
-                a_acc = project("a_acc", A_BANKS, wa_w, wa_sc, c, t)
+                a_acc = project("a_acc", A_BANKS, wa_mx, c, t)
                 nc.vector.tensor_tensor(into[:, t, :], a_acc[:], damp[t, c][:], ALU.mult)
 
         windows = []
@@ -203,20 +214,20 @@ def tile_list_spill_damped_grad_kernel(tc, tab_words, tab_scales, offs, sT, wa, 
             nc.gpsimd.memset(window[:].bitcast(I32), 0)
             windows.append(window)
 
-        def embed(y, n, c):
+        def embed(y, n, c, part=slice(0, CHUNK)):
             u, first = divmod(n * P, WO_PIECE)
             (wo_words, wo_scales), (h_words, h_scales) = wo_mx[u], h_mx[c]
             y_acc = psum.tile([P, CHUNK], F32, name="y_acc", bufs=Y_BANKS)
             nc.tensor.matmul_mx(
-                out=y_acc[:],
+                out=y_acc[:, part],
                 lhsT=wo_words[:, first : first + P].bitcast(E4M3),
                 lhsT_scale=wo_scales[:, first : first + P],
-                rhs=h_words[:].bitcast(E4M3),
-                rhs_scale=h_scales[:],
+                rhs=h_words[:, part].bitcast(E4M3),
+                rhs_scale=h_scales[:, part],
                 start=True,
                 stop=True,
             )
-            nc.scalar.copy(y, y_acc[:])
+            nc.scalar.copy(y, y_acc[:, part])
 
         def place(y, n, first, count):
             window = windows[n % WINDOWS][:].indirect(places[:, entries(first, count)])
@@ -231,32 +242,54 @@ def tile_list_spill_damped_grad_kernel(tc, tab_words, tab_scales, offs, sT, wa, 
             place(y[:], n, c * CHUNK, CHUNK)
 
         h0 = held([P, PACK, CHUNK], BF16, "h0")
-        damped = held([P, PACK, CHUNK], F32, "damped")
-        for pair in (LOW, HIGH):
-            damping(0, pair)
-        for pair in (LOW, HIGH):
-            damped_products(0, pair, damped)
-            for t in pair:
-                nc.vector.scalar_tensor_tensor(h0[:, t, :], saved[t, 0][:], 0.0, damped[:, t, :], ALU.is_gt, ALU.mult)
-        open_window(after="damp2_0")
+        masked = [held([P, CHUNK], F32, f"masked{t}") for t in range(PACK)]
+        open_window(after="tab_w0")
+        damping(0, LOW)
+        wo_first = held([P, PACK, WO_PIECE], F32, "wo_first", after="size0_0")
+        nc.sync.dma_start(wo_first[:], wo_by_row[:, :, 0:WO_PIECE])
+        gains = held([P, S], F32, "gains", after="tab_w1")
+        nc.sync.dma_start(gains[:], wgo)
+        open_window(after="size1_0")
+        damping(0, HIGH)
+        wo_rest = held([P, PACK, N - WO_PIECE], F32, "wo_rest", after="size2_0")
+        nc.sync.dma_start(wo_rest[:], wo_by_row[:, :, WO_PIECE:])
+        for t in range(PACK):
+            a_acc = project("a_acc", A_BANKS, wa_mx, 0, t)
+            nc.vector.scalar_tensor_tensor(masked[t][:], saved[t, 0][:], 0.0, a_acc[:], ALU.is_gt, ALU.mult)
+            nc.gpsimd.tensor_tensor(h0[:, t, :], masked[t][:], damp[t, 0][:], ALU.mult)
         damping(1, LOW)
-        quantize_wo(0)
-        h_mx.append(quantize_rows(h0[:], "h0"))
-
-        pick_saved(1, 1, after="saved3_0")
-        pick_saved(2, 1, after="damped")
+        pick_saved(2, 1, after="saved3_0")
         h1 = held([P, PACK, CHUNK], BF16, "h1")
-        rounded = held([P, PACK, CHUNK], BF16, "rounded", after="h0_grouped")
-        mask = held([P, PACK, CHUNK], BF16, "mask", after="h0")
+        rounded = held([P, PACK, CHUNK], BF16, "rounded", after="masked2")
         damped_products(1, LOW, rounded)
-        pick_saved(3, 1, after="damp1_1")
-        place_chunk(0, 0)
-        open_window(after="damp0_1")
-        open_window(after="y0_0")
-        damping(1, HIGH)
+        quantize_wo(0, words_after="masked3")
+        h0_words = held([P, CHUNK], U32, "h0_words")
+        h0_scales = held([P, CHUNK], U8, "h0_scales")
+        h_mx.append((h0_words, h0_scales))
+        halves = [slice(u * HALF, (u + 1) * HALF) for u in range(2)]
+        for u, part in enumerate(halves):
+            grouped = held([P, HALF, PACK], BF16, f"h0_grouped{u}", after=f"size{u}_1")
+            nc.scalar.copy(
+                grouped[:].rearrange("p (c i) j -> p c j i", i=WORDS_A_LINE),
+                h0[:, :, part].rearrange("p j (c i) -> p c j i", i=WORDS_A_LINE),
+            )
+            if u == 1:
+                pick_saved(3, 1, after="size0_1")
+            nc.vector.quantize_mx(out=h0_words[:, part].bitcast(E4M3), scales=h0_scales[:, part], in_=grouped[:].rearrange("p c j -> p (c j)"))
+        for u, part in enumerate(halves):
+            y = held([P, HALF], F32, f"y0_half{u}")
+            embed(y[:], 0, 0, part)
+            place(y[:], 0, part.start, HALF)
+
+        open_window(after="y0_half0")
         place_chunk(1, 0)
+        quantize_wo(1, after="size1_1")
+        open_window(after="size1_1")
         open_window(after="y1_0")
-        quantize_wo(1)
+        damping(1, HIGH, "y_acc", Y_BANKS)
+        place_chunk(2, 0)
+        quantize_wo(2, after="size2_1")
+        mask = held([P, PACK, CHUNK], BF16, "mask", after="size3_1")
         for pair in (LOW, HIGH):
             for t in pair:
                 nc.scalar.activation(mask[:, t, :], saved[t, 1][:], ACT.Sign)
@@ -265,15 +298,14 @@ def tile_list_spill_damped_grad_kernel(tc, tab_words, tab_scales, offs, sT, wa, 
         damped_products(1, HIGH, rounded)
         nc.vector.tensor_tensor(h1[:], mask[:], rounded[:], ALU.mult)
 
-        place_chunk(2, 0, after="damp1_1")
+        place_chunk(3, 0, after="size0_1")
         h_mx.append(quantize_rows(h1[:], "h1"))
-        place_chunk(3, 0, after="h1")
+        place_chunk(4, 0, after="h1")
+        quantize_wo(3, after="h1_grouped")
         for n in range(WINDOWS):
             place_chunk(n, 1)
             store(n)
 
-        for u in range(WINDOWS * P // WO_PIECE, N // WO_PIECE):
-            quantize_wo(u)
         for n in range(WINDOWS, N // P):
             y = ring.tile([P, S], F32, name="y")
             for c in range(CHUNKS):

@@ -71,11 +71,11 @@ def tile_list_spill_damped_grad_kernel(tc, tab_words, tab_scales, offs, sT, wa, 
         nc.sync.dma_start(picks[:], offs)
         nc.sync.dma_start(tab_sc[last, :].bitcast(I32), tab_scales.rearrange("a q c -> q a c").bitcast(I32))
         nc.sync.dma_start(wb_sc_raw[last, :].bitcast(I32), wb_scales.rearrange("a q c -> q a c").bitcast(I32))
-        nc.sync.dma_start(places[:], offs2)
         for a in range(PASSES):
             nc.sync.dma_start(tab_w[a][:], tab_words[a].rearrange("p c i -> p (c i)").bitcast(I32))
         nc.sync.dma_start(wa_raw[0][:], wa_by_pass[0])
         nc.sync.dma_start(wb_w_raw[:], wb_words.rearrange("a p c i -> p a (c i)").bitcast(I32))
+        nc.sync.dma_start(places[:], offs2)
 
         nc.vector.tensor_copy(
             staged[:, S:].rearrange("p (t m i) -> p m t i", t=PACK, i=LINE),
@@ -205,7 +205,7 @@ def tile_list_spill_damped_grad_kernel(tc, tab_words, tab_scales, offs, sT, wa, 
         def damped_products(c, pair, into):
             for t in pair:
                 a_acc = project("a_acc", A_BANKS, wa_mx, c, t)
-                nc.vector.tensor_tensor(into[:, t, :], a_acc[:], damp[t, c][:], ALU.mult)
+                nc.vector.tensor_tensor(into[:, t - pair[0], :], a_acc[:], damp[t, c][:], ALU.mult)
 
         windows = []
 
@@ -242,7 +242,8 @@ def tile_list_spill_damped_grad_kernel(tc, tab_words, tab_scales, offs, sT, wa, 
             place(y[:], n, c * CHUNK, CHUNK)
 
         h0 = held([P, PACK, CHUNK], BF16, "h0")
-        masked = [held([P, CHUNK], F32, f"masked{t}") for t in range(PACK)]
+        masked = {}
+
         open_window(after="tab_w0")
         damping(0, LOW)
         wo_first = held([P, PACK, WO_PIECE], F32, "wo_first", after="size0_0")
@@ -253,16 +254,24 @@ def tile_list_spill_damped_grad_kernel(tc, tab_words, tab_scales, offs, sT, wa, 
         damping(0, HIGH)
         wo_rest = held([P, PACK, N - WO_PIECE], F32, "wo_rest", after="size2_0")
         nc.sync.dma_start(wo_rest[:], wo_by_row[:, :, WO_PIECE:])
-        for t in range(PACK):
-            a_acc = project("a_acc", A_BANKS, wa_mx, 0, t)
-            nc.vector.scalar_tensor_tensor(masked[t][:], saved[t, 0][:], 0.0, a_acc[:], ALU.is_gt, ALU.mult)
-            nc.gpsimd.tensor_tensor(h0[:, t, :], masked[t][:], damp[t, 0][:], ALU.mult)
+        def masked_product(c, t):
+            a_acc = project("a_acc", A_BANKS, wa_mx, c, t)
+            masked[t, c] = held([P, CHUNK], F32, f"masked{t}_{c}")
+            nc.vector.scalar_tensor_tensor(masked[t, c][:], saved[t, c][:], 0.0, a_acc[:], ALU.is_gt, ALU.mult)
+
+        for t in range(PACK - 1):
+            masked_product(0, t)
+            nc.gpsimd.tensor_tensor(h0[:, t, :], masked[t, 0][:], damp[t, 0][:], ALU.mult)
+        last_damped = held([P, 1, CHUNK], F32, "last_damped")
+        damped_products(0, (3,), last_damped)
+        nc.vector.scalar_tensor_tensor(h0[:, 3, :], saved[3, 0][:], 0.0, last_damped[:, 0, :], ALU.is_gt, ALU.mult)
         damping(1, LOW)
         pick_saved(2, 1, after="saved3_0")
         h1 = held([P, PACK, CHUNK], BF16, "h1")
-        rounded = held([P, PACK, CHUNK], BF16, "rounded", after="masked2")
-        damped_products(1, LOW, rounded)
-        quantize_wo(0, words_after="masked3")
+        for t in LOW:
+            masked_product(1, t)
+            nc.gpsimd.tensor_tensor(h1[:, t, :], masked[t, 1][:], damp[t, 1][:], ALU.mult)
+        quantize_wo(0, words_after="last_damped")
         h0_words = held([P, CHUNK], U32, "h0_words")
         h0_scales = held([P, CHUNK], U8, "h0_scales")
         h_mx.append((h0_words, h0_scales))
@@ -289,14 +298,13 @@ def tile_list_spill_damped_grad_kernel(tc, tab_words, tab_scales, offs, sT, wa, 
         damping(1, HIGH, "y_acc", Y_BANKS)
         place_chunk(2, 0)
         quantize_wo(2, after="size2_1")
-        mask = held([P, PACK, CHUNK], BF16, "mask", after="size3_1")
-        for pair in (LOW, HIGH):
-            for t in pair:
-                nc.scalar.activation(mask[:, t, :], saved[t, 1][:], ACT.Sign)
-            signs = mask[:, pair[0] : pair[-1] + 1, :]
-            nc.scalar.activation(signs, signs, ACT.Relu)
+        mask = held([P, 2, CHUNK], BF16, "mask", after="size3_1")
+        for t in HIGH:
+            nc.scalar.activation(mask[:, t - HIGH[0], :], saved[t, 1][:], ACT.Sign)
+        nc.scalar.activation(mask[:], mask[:], ACT.Relu)
+        rounded = held([P, 2, CHUNK], BF16, "rounded")
         damped_products(1, HIGH, rounded)
-        nc.vector.tensor_tensor(h1[:], mask[:], rounded[:], ALU.mult)
+        nc.vector.tensor_tensor(h1[:, 2:4, :], mask[:], rounded[:], ALU.mult)
 
         place_chunk(3, 0, after="size0_1")
         h_mx.append(quantize_rows(h1[:], "h1"))

@@ -27,10 +27,10 @@ QUADRANT = 32
 SCALE_ROWS = 4
 LINE = 16
 WORDS_A_LINE = LINE // 4
+EARLY = 4
+WINDOWS = 4
 WO_PIECE = 256
-WINDOWS = 5
 Y_TILES = 3
-A_BANKS, B_BANKS, Y_BANKS = 4, 2, 2
 LOW, HIGH = (0, 1), (2, 3)
 
 
@@ -41,8 +41,11 @@ def tile_list_spill_damped_grad_kernel(tc, tab_words, tab_scales, offs, sT, wa, 
         ring = ctx.enter_context(tc.tile_pool(name="ring", bufs=Y_TILES))
         psum = ctx.enter_context(tc.psum_pool(name="psum", bufs=1))
 
+        tags = {}
+
         def held(shape, dtype, name, after=None):
-            return keep.tile(shape, dtype, name=name, tag=after or name, align_bytes=64)
+            tags[name] = tags[after] if after else name
+            return keep.tile(shape, dtype, name=name, tag=tags[name], align_bytes=64)
 
         picks = keep.tile([P, S // LIST_ROWS], U16, name="picks")
         places = keep.tile([P, S // LIST_ROWS], U16, name="places")
@@ -55,43 +58,55 @@ def tile_list_spill_damped_grad_kernel(tc, tab_words, tab_scales, offs, sT, wa, 
         warm = held([P, 8], F32, "warm")
         rest, last = slice(0, P - QUADRANT), slice(P - QUADRANT, P)
 
-        nc.vector.memset(tab_sc[rest, :].bitcast(I32), 0)
-        nc.vector.memset(wb_sc_raw[rest, :].bitcast(I32), 0)
-        nc.vector.memset(planes_sc[:].rearrange("p a c -> p (a c)").bitcast(I32), 0)
+        nc.gpsimd.memset(tab_sc[rest, :].bitcast(I32), 0)
+        nc.gpsimd.memset(wb_sc_raw[rest, :].bitcast(I32), 0)
+        nc.gpsimd.memset(planes_sc[:].rearrange("p a c -> p (a c)").bitcast(I32), 0)
 
         nc.vector.memset(warm[:], 0.0)
         nc.scalar.activation(warm[:], warm[:], ACT.Abs_reciprocal_sqrt, bias=1.0)
 
         tab_w = [held([P, T], I32, f"tab_w{a}") for a in range(PASSES)]
-        wa_raw = [held([P, PACK, H], F32, "wa_raw0")]
         wb_w_raw = held([P, PASSES, H], I32, "wb_w_raw")
         s_by_slot = sT.rearrange("(p t) c -> t p c", t=PACK)
         wa_by_pass = wa.rearrange("(a p j) c -> a p j c", a=PASSES, j=PACK)
+        wo_by_row = wo.rearrange("(p j) c -> p j c", j=PACK)
 
         nc.sync.dma_start(picks[:], offs)
         nc.sync.dma_start(tab_sc[last, :].bitcast(I32), tab_scales.rearrange("a q c -> q a c").bitcast(I32))
         nc.sync.dma_start(wb_sc_raw[last, :].bitcast(I32), wb_scales.rearrange("a q c -> q a c").bitcast(I32))
-        for a in range(PASSES):
-            nc.sync.dma_start(tab_w[a][:], tab_words[a].rearrange("p c i -> p (c i)").bitcast(I32))
-        nc.sync.dma_start(wa_raw[0][:], wa_by_pass[0])
+        nc.sync.dma_start(tab_w[0][:], tab_words[0].rearrange("p c i -> p (c i)").bitcast(I32))
         nc.sync.dma_start(wb_w_raw[:], wb_words.rearrange("a p c i -> p a (c i)").bitcast(I32))
+        nc.sync.dma_start(tab_w[1][:], tab_words[1].rearrange("p c i -> p (c i)").bitcast(I32))
         nc.sync.dma_start(places[:], offs2)
 
+        windows = []
+
+        def open_window(after=None):
+            window = held([P, T2], F32, f"window{len(windows)}", after)
+            nc.gpsimd.memset(window[:].bitcast(I32), 0)
+            windows.append(window)
+
+        for early in range(WINDOWS - 1):
+            open_window()
+        nc.vector.tensor_copy(picked_sc[:], tab_sc[:].indirect(picks[:]))
         nc.vector.tensor_copy(
             staged[:, S:].rearrange("p (t m i) -> p m t i", t=PACK, i=LINE),
             wb_sc_raw[:].rearrange("p (m i t) -> p m t i", t=PACK, i=LINE),
         )
-        nc.vector.tensor_copy(picked_sc[:], tab_sc[:].indirect(picks[:]))
         nc.vector.tensor_copy(staged[last, 0:S].bitcast(I32), picked_sc[last, :].bitcast(I32))
         for q in range(P // QUADRANT):
             first = last.start + q * SCALE_ROWS * PASSES
-            nc.scalar.dma_start(
+            nc.sync.dma_start(
                 planes_sc[QUADRANT * q : QUADRANT * q + SCALE_ROWS, :, :].bitcast(I32),
                 staged[first : first + SCALE_ROWS * PASSES, :].bitcast(I32),
             )
+        wa_raw = [held([P, PACK, H], F32, "wa_raw0", after="picked_sc")]
+        nc.sync.dma_start(wa_raw[0][:], wa_by_pass[0])
         v_w = [held([P, S], U32, f"v_w{a}") for a in range(PASSES)]
         for a in range(PASSES):
             nc.vector.tensor_copy(v_w[a][:], tab_w[a][:].bitcast(U32).indirect(picks[:]))
+        wa_raw.append(held([P, PACK, H], F32, "wa_raw1", after="tab_w0"))
+        nc.sync.dma_start(wa_raw[1][:], wa_by_pass[1])
         wb_w = held([P, PASSES, H], I32, "wb_w")
         nc.vector.tensor_copy(
             wb_w[:].rearrange("p a (t m i) -> p a m t i", t=PACK, i=WORDS_A_LINE),
@@ -104,70 +119,43 @@ def tile_list_spill_damped_grad_kernel(tc, tab_words, tab_scales, offs, sT, wa, 
             s_rows.append(held([P, T], F32, f"s_rows{t}", after))
             nc.sync.dma_start(s_rows[t][:], s_by_slot[t])
 
-        load_slot(0, after="tab_w0")
-        wa_raw.append(held([P, PACK, H], F32, "wa_raw1", after="tab_w1"))
-        nc.sync.dma_start(wa_raw[1][:], wa_by_pass[1])
-        load_slot(1, after="wb_w_raw")
+        load_slot(0, after="wb_w_raw")
+        load_slot(1, after="tab_w1")
 
         wa_mx = {}
 
-        def quantize_wa(a, slots, after=None):
-            name = f"wa{a}_{slots[0]}"
-            grouped = held([P, len(slots) * P * PACK], BF16, f"{name}_grouped")
-            nc.scalar.copy(
-                grouped[:].rearrange("p (t m j) -> p m j t", t=len(slots), j=PACK),
-                wa_raw[a][:].rearrange("p j (m t) -> p m j t", t=PACK)[:, :, :, slots[0] : slots[-1] + 1],
-            )
-            words = held([P, len(slots) * P], U32, f"{name}_words", after)
-            scales = held([P, len(slots) * P], U8, f"{name}_scales")
+        def quantize_wa(a):
+            grouped = held([P, H * PACK], BF16, f"wa{a}_grouped")
+            into = grouped[:].rearrange("p (t m j) -> p m j t", t=PACK, j=PACK)
+            rows = wa_raw[a][:].rearrange("p j (m t) -> p m j t", t=PACK)
+            if a == 0:
+                nc.scalar.copy(into, rows)
+            else:
+                nc.vector.tensor_copy(into[:, :, :, 0:2], rows[:, :, :, 0:2])
+                nc.scalar.copy(into[:, :, :, 2:4], rows[:, :, :, 2:4])
+            words = held([P, H], U32, f"wa{a}_words")
+            scales = held([P, H], U8, f"wa{a}_scales")
             nc.vector.quantize_mx(out=words[:].bitcast(E4M3), scales=scales[:], in_=grouped[:])
-            for t in slots:
-                rows = slice((t - slots[0]) * P, (t - slots[0] + 1) * P)
-                wa_mx[a, t] = words[:, rows], scales[:, rows]
+            for t in range(PACK):
+                wa_mx[a, t] = words[:, t * P : (t + 1) * P], scales[:, t * P : (t + 1) * P]
 
-        quantize_wa(0, LOW + HIGH)
-        load_slot(2, after="wa_raw0")
-        load_slot(3, after="wa0_0_grouped")
+        quantize_wa(0)
+        load_slot(2, after="wa0_grouped")
+        quantize_wa(1)
+        load_slot(3, after="wa_raw1")
+        open_window(after="wa1_grouped")
+        wo_raw = {}
+
+        def load_wo(first_tile, tiles, after):
+            wo_raw[first_tile] = held([P, PACK, tiles * P], F32, f"wo{first_tile}_raw", after)
+            nc.sync.dma_start(wo_raw[first_tile][:], wo_by_row[:, :, first_tile * P : (first_tile + tiles) * P])
+
 
         def entries(first, count):
             return slice(first // LIST_ROWS, (first + count) // LIST_ROWS)
 
-        saved = {}
-
-        def pick_saved(t, c, after=None):
-            saved[t, c] = held([P, CHUNK], F32, f"saved{t}_{c}", after)
-            nc.vector.tensor_copy(saved[t, c][:], s_rows[t][:].indirect(picks[:, entries(c * CHUNK, CHUNK)]))
-
-        for t in LOW:
-            pick_saved(t, 0)
-            pick_saved(t, 1)
-        quantize_wa(1, LOW, after="wb_w_raw")
-        quantize_wa(1, HIGH, after="wa1_0_grouped")
-        for t in HIGH:
-            pick_saved(t, 0)
-
-        wo_by_row = wo.rearrange("(p j) c -> p j c", j=PACK)
-
-        def quantize_rows(rows, name, after=None, words_after=None):
-            columns = rows.shape[2]
-            grouped = held([P, columns, PACK], BF16, f"{name}_grouped", after)
-            nc.scalar.copy(
-                grouped[:].rearrange("p (c i) j -> p c j i", i=WORDS_A_LINE),
-                rows.rearrange("p j (c i) -> p c j i", i=WORDS_A_LINE),
-            )
-            words = held([P, columns], U32, f"{name}_words", words_after)
-            scales = held([P, columns], U8, f"{name}_scales")
-            nc.vector.quantize_mx(out=words[:].bitcast(E4M3), scales=scales[:], in_=grouped[:].rearrange("p c j -> p (c j)"))
-            return words, scales
-
-        wo_mx, h_mx = [], []
-
-        def quantize_wo(u, after=None, words_after=None):
-            rows = wo_first[:] if u == 0 else wo_rest[:, :, (u - 1) * WO_PIECE : u * WO_PIECE]
-            wo_mx.append(quantize_rows(rows, f"wo{u}", after, words_after))
-
-        def project(name, banks, weight, c, t):
-            acc = psum.tile([P, CHUNK], F32, name=name, bufs=banks)
+        def project(bank, weight, c, t):
+            acc = psum.tile([P, CHUNK], F32, name=bank)
             cols = slice(c * CHUNK, (c + 1) * CHUNK)
             for a in range(PASSES):
                 words, scales = weight[a, t]
@@ -187,134 +175,159 @@ def tile_list_spill_damped_grad_kernel(tc, tab_words, tab_scales, offs, sT, wa, 
             for a in range(PASSES)
             for t in range(PACK)
         }
-        damp = {}
+        roots, damp, saved, masked = {}, {}, {}, {}
 
-        def damping(c, pair, bank_name="b_acc", banks=B_BANKS, after=None):
-            size = {}
-            for t in pair:
-                b_acc = project(bank_name, banks, wb_mx, c, t)
-                size[t] = held([P, CHUNK], F32, f"size{t}_{c}", after)
-                after = None
-                nc.scalar.activation(size[t][:], b_acc[:], ACT.Abs)
-            for t in pair:
-                nc.scalar.activation(size[t][:], size[t][:], ACT.Abs_reciprocal_sqrt, bias=1.0)
-            for t in pair:
-                damp[t, c] = held([P, CHUNK], F32, f"damp{t}_{c}")
-                nc.scalar.activation(damp[t, c][:], size[t][:], ACT.Square)
+        def damping(c, pair, size_after=None):
+            size = held([P, 2, CHUNK], F32, f"size{pair[0]}_{c}", size_after)
+            for i, t in enumerate(pair):
+                nc.scalar.activation(size[:, i, :], project(f"b{i}", wb_mx, c, t)[:], ACT.Abs)
+            for i in range(2):
+                nc.scalar.activation(size[:, i, :], size[:, i, :], ACT.Abs_reciprocal_sqrt, bias=1.0)
+            roots[pair, c] = size
 
-        def damped_products(c, pair, into):
-            for t in pair:
-                a_acc = project("a_acc", A_BANKS, wa_mx, c, t)
-                nc.vector.tensor_tensor(into[:, t - pair[0], :], a_acc[:], damp[t, c][:], ALU.mult)
+        def squares(c, pair, after=None):
+            damp[pair, c] = held([P, 2, CHUNK], F32, f"damp{pair[0]}_{c}", after)
+            for i in range(2):
+                nc.scalar.activation(damp[pair, c][:, i, :], roots[pair, c][:, i, :], ACT.Square)
 
-        windows = []
+        def pick_saved(t, c, into=None):
+            saved[t, c] = held([P, CHUNK], F32, f"saved{t}_{c}")[:] if into is None else into
+            nc.vector.tensor_copy(saved[t, c], s_rows[t][:].indirect(picks[:, entries(c * CHUNK, CHUNK)]))
 
-        def open_window(after):
-            window = held([P, T2], F32, f"window{len(windows)}", after)
-            nc.gpsimd.memset(window[:].bitcast(I32), 0)
-            windows.append(window)
+        def masked_product(pair, c, t, bank, after=None):
+            if t == pair[0]:
+                masked[pair, c] = held([P, 2, CHUNK], F32, f"masked{t}_{c}", after)
+            a_acc = project(bank, wa_mx, c, t)
+            nc.vector.scalar_tensor_tensor(masked[pair, c][:, t - pair[0], :], saved[t, c], 0.0, a_acc[:], ALU.is_gt, ALU.mult)
+
+        h_grouped = [held([P, CHUNK, PACK], BF16, "h0_grouped")]
+
+        def finish_pair(pair, c):
+            nc.gpsimd.tensor_tensor(
+                h_grouped[c][:, :, pair[0] : pair[1] + 1],
+                masked[pair, c][:].rearrange("p t c -> p c t"),
+                damp[pair, c][:].rearrange("p t c -> p c t"),
+                ALU.mult,
+            )
+
+        def finish_slot(pair, c, t):
+            i = t - pair[0]
+            nc.gpsimd.tensor_tensor(h_grouped[c][:, :, t], masked[t, c][:], damp[pair, c][:, i, :], ALU.mult)
+
+        def masked_slot(c, t):
+            masked[t, c] = held([P, CHUNK], F32, f"masked_slot{t}_{c}")
+            a_acc = project(f"a{t}", wa_mx, c, t)
+            nc.vector.scalar_tensor_tensor(masked[t, c][:], saved[t, c], 0.0, a_acc[:], ALU.is_gt, ALU.mult)
+
+        wo_mx = {}
+
+        def quantize_wo(first_tile, after=None, words_after=None):
+            rows = wo_raw[first_tile][:]
+            columns = rows.shape[2]
+            name = f"wo{first_tile}"
+            grouped = held([P, columns, PACK], BF16, f"{name}_grouped", after)
+            nc.scalar.copy(
+                grouped[:].rearrange("p (c i) j -> p c j i", i=WORDS_A_LINE),
+                rows.rearrange("p j (c i) -> p c j i", i=WORDS_A_LINE),
+            )
+            words = held([P, columns], U32, f"{name}_words", words_after)
+            scales = held([P, columns], U8, f"{name}_scales")
+            nc.vector.quantize_mx(out=words[:].bitcast(E4M3), scales=scales[:], in_=grouped[:].rearrange("p c j -> p (c j)"))
+            for i in range(columns // P):
+                wo_mx[first_tile + i] = words[:, i * P : (i + 1) * P], scales[:, i * P : (i + 1) * P]
+
+        h_words = [held([P, CHUNK], U32, f"h{c}_words") for c in range(CHUNKS)]
+        h_scales = [held([P, CHUNK], U8, f"h{c}_scales") for c in range(CHUNKS)]
+
+        def quantize_h(c, part):
+            nc.vector.quantize_mx(
+                out=h_words[c][:, part].bitcast(E4M3),
+                scales=h_scales[c][:, part],
+                in_=h_grouped[c][:, part, :].rearrange("p c j -> p (c j)"),
+            )
+
+        filled = []
 
         def embed(y, n, c, part=slice(0, CHUNK)):
-            u, first = divmod(n * P, WO_PIECE)
-            (wo_words, wo_scales), (h_words, h_scales) = wo_mx[u], h_mx[c]
-            y_acc = psum.tile([P, CHUNK], F32, name="y_acc", bufs=Y_BANKS)
+            y_acc = psum.tile([P, CHUNK], F32, name=f"y{len(filled) % 2}")
+            filled.append(n)
             nc.tensor.matmul_mx(
                 out=y_acc[:, part],
-                lhsT=wo_words[:, first : first + P].bitcast(E4M3),
-                lhsT_scale=wo_scales[:, first : first + P],
-                rhs=h_words[:, part].bitcast(E4M3),
-                rhs_scale=h_scales[:, part],
+                lhsT=wo_mx[n][0].bitcast(E4M3),
+                lhsT_scale=wo_mx[n][1],
+                rhs=h_words[c][:, part].bitcast(E4M3),
+                rhs_scale=h_scales[c][:, part],
                 start=True,
                 stop=True,
             )
             nc.scalar.copy(y, y_acc[:, part])
 
+        def spots(n, first, count):
+            return windows[n % WINDOWS][:].indirect(places[:, entries(first, count)])
+
         def place(y, n, first, count):
-            window = windows[n % WINDOWS][:].indirect(places[:, entries(first, count)])
-            nc.vector.tensor_tensor(window, y, gains[:, first : first + count], ALU.mult)
+            nc.vector.tensor_tensor(spots(n, first, count), y, gains[:, first : first + count], ALU.mult)
+
+        def place_weighted(n, part, name, after=None):
+            count = part.stop - part.start
+            y = held([P, count], F32, name)
+            embed(y[:], n, 0, part)
+            weighted = held([P, count], F32, f"{name}_weighted", after)
+            nc.gpsimd.tensor_tensor(weighted[:], y[:], gains[:, part], ALU.mult)
+            nc.vector.tensor_copy(spots(n, part.start, count), weighted[:])
 
         def store(n):
             nc.sync.dma_start(out[n * P : (n + 1) * P, :], windows[n % WINDOWS][:])
 
-        def place_chunk(n, c, after=None):
-            y = held([P, CHUNK], F32, f"y{n}_{c}", after)
-            embed(y[:], n, c)
-            place(y[:], n, c * CHUNK, CHUNK)
-
-        h0 = held([P, PACK, CHUNK], BF16, "h0")
-        masked = {}
-
-        open_window(after="tab_w0")
-        damping(0, LOW)
-        wo_first = held([P, PACK, WO_PIECE], F32, "wo_first", after="size0_0")
-        nc.sync.dma_start(wo_first[:], wo_by_row[:, :, 0:WO_PIECE])
-        gains = held([P, S], F32, "gains", after="tab_w1")
-        nc.sync.dma_start(gains[:], wgo)
-        open_window(after="size1_0")
+        damping(0, LOW, size_after="wa_raw0")
+        squares(0, LOW)
         damping(0, HIGH)
-        wo_rest = held([P, PACK, N - WO_PIECE], F32, "wo_rest", after="size2_0")
-        nc.sync.dma_start(wo_rest[:], wo_by_row[:, :, WO_PIECE:])
-        def masked_product(c, t):
-            a_acc = project("a_acc", A_BANKS, wa_mx, c, t)
-            masked[t, c] = held([P, CHUNK], F32, f"masked{t}_{c}")
-            nc.vector.scalar_tensor_tensor(masked[t, c][:], saved[t, c][:], 0.0, a_acc[:], ALU.is_gt, ALU.mult)
-
-        for t in range(PACK - 1):
-            masked_product(0, t)
-            nc.gpsimd.tensor_tensor(h0[:, t, :], masked[t, 0][:], damp[t, 0][:], ALU.mult)
-        last_damped = held([P, 1, CHUNK], F32, "last_damped")
-        damped_products(0, (3,), last_damped)
-        nc.vector.scalar_tensor_tensor(h0[:, 3, :], saved[3, 0][:], 0.0, last_damped[:, 0, :], ALU.is_gt, ALU.mult)
+        squares(0, HIGH)
+        for t in range(PACK):
+            pick_saved(t, 0)
+            masked_slot(0, t)
+            finish_slot(LOW if t in LOW else HIGH, 0, t)
+        load_wo(0, 2, after="saved0_0")
+        gains = held([P, S], F32, "gains", after="size0_0")
+        nc.sync.dma_start(gains[:], wgo)
+        load_wo(2, 2, after="masked_slot0_0")
+        load_wo(4, 4, after="size2_0")
+        quantize_wo(0)
+        quantize_wo(2)
         damping(1, LOW)
-        pick_saved(2, 1, after="saved3_0")
-        h1 = held([P, PACK, CHUNK], BF16, "h1")
+        damping(1, HIGH)
+        late = held([P, 2, CHUNK], F32, "late_low", after="saved3_0")
         for t in LOW:
-            masked_product(1, t)
-            nc.gpsimd.tensor_tensor(h1[:, t, :], masked[t, 1][:], damp[t, 1][:], ALU.mult)
-        quantize_wo(0, words_after="last_damped")
-        h0_words = held([P, CHUNK], U32, "h0_words")
-        h0_scales = held([P, CHUNK], U8, "h0_scales")
-        h_mx.append((h0_words, h0_scales))
+            pick_saved(t, 1, late[:, t, :])
+        quantize_h(0, slice(0, CHUNK))
+        late = held([P, 2, CHUNK], F32, "late_high", after="h0_grouped")
+        for t in HIGH:
+            pick_saved(t, 1, late[:, t - HIGH[0], :])
         halves = [slice(u * HALF, (u + 1) * HALF) for u in range(2)]
         for u, part in enumerate(halves):
-            grouped = held([P, HALF, PACK], BF16, f"h0_grouped{u}", after=f"size{u}_1")
-            nc.scalar.copy(
-                grouped[:].rearrange("p (c i) j -> p c j i", i=WORDS_A_LINE),
-                h0[:, :, part].rearrange("p j (c i) -> p c j i", i=WORDS_A_LINE),
-            )
-            if u == 1:
-                pick_saved(3, 1, after="size0_1")
-            nc.vector.quantize_mx(out=h0_words[:, part].bitcast(E4M3), scales=h0_scales[:, part], in_=grouped[:].rearrange("p c j -> p (c j)"))
-        for u, part in enumerate(halves):
-            y = held([P, HALF], F32, f"y0_half{u}")
-            embed(y[:], 0, 0, part)
-            place(y[:], 0, part.start, HALF)
-
-        open_window(after="y0_half0")
-        place_chunk(1, 0)
-        quantize_wo(1, after="size1_1")
-        open_window(after="size1_1")
-        open_window(after="y1_0")
-        damping(1, HIGH, "y_acc", Y_BANKS)
-        place_chunk(2, 0)
-        quantize_wo(2, after="size2_1")
-        mask = held([P, 2, CHUNK], BF16, "mask", after="size3_1")
-        for t in HIGH:
-            nc.scalar.activation(mask[:, t - HIGH[0], :], saved[t, 1][:], ACT.Sign)
-        nc.scalar.activation(mask[:], mask[:], ACT.Relu)
-        rounded = held([P, 2, CHUNK], BF16, "rounded")
-        damped_products(1, HIGH, rounded)
-        nc.vector.tensor_tensor(h1[:, 2:4, :], mask[:], rounded[:], ALU.mult)
-
-        place_chunk(3, 0, after="size0_1")
-        h_mx.append(quantize_rows(h1[:], "h1"))
-        place_chunk(4, 0, after="h1")
-        quantize_wo(3, after="h1_grouped")
-        for n in range(WINDOWS):
-            place_chunk(n, 1)
+            place_weighted(0, part, f"y0_half{u}", after=None if u else "wo2_grouped")
+        masked_product(LOW, 1, 0, "a0", after="wo2_raw")
+        masked_product(LOW, 1, 1, "a1")
+        masked_product(HIGH, 1, 2, "a2", after="s_rows3")
+        masked_product(HIGH, 1, 3, "a3")
+        for n in (1, 2):
+            place_weighted(n, slice(0, CHUNK), f"y{n}_0")
+        h_grouped.append(held([P, CHUNK, PACK], BF16, "h1_grouped", after="y2_0"))
+        squares(1, LOW)
+        finish_pair(LOW, 1)
+        squares(1, HIGH)
+        finish_pair(HIGH, 1)
+        quantize_h(1, slice(0, CHUNK))
+        y = held([P, CHUNK], F32, "y3_0", after="masked2_1")
+        embed(y[:], 3, 0)
+        place(y[:], 3, 0, CHUNK)
+        quantize_wo(4, after="size2_1", words_after="y3_0")
+        for n in range(EARLY):
+            y = held([P, CHUNK], F32, f"y{n}_1")
+            embed(y[:], n, 1)
+            place(y[:], n, CHUNK, CHUNK)
             store(n)
-
-        for n in range(WINDOWS, N // P):
+        for n in range(EARLY, N // P):
             y = ring.tile([P, S], F32, name="y")
             for c in range(CHUNKS):
                 embed(y[:, c * CHUNK : (c + 1) * CHUNK], n, c)

@@ -86,8 +86,8 @@ def tile_list_spill_damped_grad_kernel(tc, tab_words, tab_scales, offs, sT, wa, 
             nc.gpsimd.memset(window[:].bitcast(I32), 0)
             windows.append(window)
 
-        for early in range(WINDOWS - 1):
-            open_window()
+        open_window()
+        open_window()
         nc.vector.tensor_copy(picked_sc[:], tab_sc[:].indirect(picks[:]))
         nc.vector.tensor_copy(
             staged[:, S:].rearrange("p (t m i) -> p m t i", t=PACK, i=LINE),
@@ -96,30 +96,31 @@ def tile_list_spill_damped_grad_kernel(tc, tab_words, tab_scales, offs, sT, wa, 
         nc.vector.tensor_copy(staged[last, 0:S].bitcast(I32), picked_sc[last, :].bitcast(I32))
         for q in range(P // QUADRANT):
             first = last.start + q * SCALE_ROWS * PASSES
-            nc.sync.dma_start(
+            nc.scalar.dma_start(
                 planes_sc[QUADRANT * q : QUADRANT * q + SCALE_ROWS, :, :].bitcast(I32),
                 staged[first : first + SCALE_ROWS * PASSES, :].bitcast(I32),
             )
-        wa_raw = [held([P, PACK, H], F32, "wa_raw0", after="picked_sc")]
-        nc.sync.dma_start(wa_raw[0][:], wa_by_pass[0])
-        v_w = [held([P, S], U32, f"v_w{a}") for a in range(PASSES)]
-        for a in range(PASSES):
-            nc.vector.tensor_copy(v_w[a][:], tab_w[a][:].bitcast(U32).indirect(picks[:]))
-        wa_raw.append(held([P, PACK, H], F32, "wa_raw1", after="tab_w0"))
-        nc.sync.dma_start(wa_raw[1][:], wa_by_pass[1])
-        wb_w = held([P, PASSES, H], I32, "wb_w")
-        nc.vector.tensor_copy(
-            wb_w[:].rearrange("p a (t m i) -> p a m t i", t=PACK, i=WORDS_A_LINE),
-            wb_w_raw[:].rearrange("p a (m i t) -> p a m t i", t=PACK, i=WORDS_A_LINE),
-        )
-
+        open_window(after="picked_sc")
         s_rows = []
 
         def load_slot(t, after):
             s_rows.append(held([P, T], F32, f"s_rows{t}", after))
             nc.sync.dma_start(s_rows[t][:], s_by_slot[t])
 
-        load_slot(0, after="wb_w_raw")
+        load_slot(0, after="tab_sc")
+        v_w = [held([P, S], U32, f"v_w{a}") for a in range(PASSES)]
+        for a in range(PASSES):
+            nc.vector.tensor_copy(v_w[a][:], tab_w[a][:].bitcast(U32).indirect(picks[:]))
+        wa_raw = [held([P, PACK, H], F32, "wa_raw0", after="tab_w0")]
+        nc.sync.dma_start(wa_raw[0][:], wa_by_pass[0])
+        wb_w = held([P, PASSES, H], I32, "wb_w")
+        nc.vector.tensor_copy(
+            wb_w[:].rearrange("p a (t m i) -> p a m t i", t=PACK, i=WORDS_A_LINE),
+            wb_w_raw[:].rearrange("p a (m i t) -> p a m t i", t=PACK, i=WORDS_A_LINE),
+        )
+
+        wa_raw.append(held([P, PACK, H], F32, "wa_raw1", after="wb_w_raw"))
+        nc.sync.dma_start(wa_raw[1][:], wa_by_pass[1])
         load_slot(1, after="tab_w1")
 
         wa_mx = {}
@@ -128,22 +129,14 @@ def tile_list_spill_damped_grad_kernel(tc, tab_words, tab_scales, offs, sT, wa, 
             grouped = held([P, H * PACK], BF16, f"wa{a}_grouped")
             into = grouped[:].rearrange("p (t m j) -> p m j t", t=PACK, j=PACK)
             rows = wa_raw[a][:].rearrange("p j (m t) -> p m j t", t=PACK)
-            if a == 0:
-                nc.scalar.copy(into, rows)
-            else:
-                nc.vector.tensor_copy(into[:, :, :, 0:2], rows[:, :, :, 0:2])
-                nc.scalar.copy(into[:, :, :, 2:4], rows[:, :, :, 2:4])
+            nc.vector.tensor_copy(into[:, :, :, 0:2], rows[:, :, :, 0:2])
+            nc.scalar.copy(into[:, :, :, 2:4], rows[:, :, :, 2:4])
             words = held([P, H], U32, f"wa{a}_words")
             scales = held([P, H], U8, f"wa{a}_scales")
             nc.vector.quantize_mx(out=words[:].bitcast(E4M3), scales=scales[:], in_=grouped[:])
             for t in range(PACK):
                 wa_mx[a, t] = words[:, t * P : (t + 1) * P], scales[:, t * P : (t + 1) * P]
 
-        quantize_wa(0)
-        load_slot(2, after="wa0_grouped")
-        quantize_wa(1)
-        load_slot(3, after="wa_raw1")
-        open_window(after="wa1_grouped")
         wo_raw = {}
 
         def load_wo(first_tile, tiles, after):
@@ -177,13 +170,13 @@ def tile_list_spill_damped_grad_kernel(tc, tab_words, tab_scales, offs, sT, wa, 
         }
         roots, damp, saved, masked = {}, {}, {}, {}
 
-        def damping(c, pair, size_after=None):
+        def damping(c, pair, size_after=None, root_after=None):
             size = held([P, 2, CHUNK], F32, f"size{pair[0]}_{c}", size_after)
             for i, t in enumerate(pair):
                 nc.scalar.activation(size[:, i, :], project(f"b{i}", wb_mx, c, t)[:], ACT.Abs)
+            roots[pair, c] = held([P, 2, CHUNK], F32, f"root{pair[0]}_{c}", root_after) if root_after else size
             for i in range(2):
-                nc.scalar.activation(size[:, i, :], size[:, i, :], ACT.Abs_reciprocal_sqrt, bias=1.0)
-            roots[pair, c] = size
+                nc.scalar.activation(roots[pair, c][:, i, :], size[:, i, :], ACT.Abs_reciprocal_sqrt, bias=1.0)
 
         def squares(c, pair, after=None):
             damp[pair, c] = held([P, 2, CHUNK], F32, f"damp{pair[0]}_{c}", after)
@@ -195,7 +188,7 @@ def tile_list_spill_damped_grad_kernel(tc, tab_words, tab_scales, offs, sT, wa, 
             nc.vector.tensor_copy(saved[t, c], s_rows[t][:].indirect(picks[:, entries(c * CHUNK, CHUNK)]))
 
         def masked_product(pair, c, t, bank, after=None):
-            if t == pair[0]:
+            if (pair, c) not in masked:
                 masked[pair, c] = held([P, 2, CHUNK], F32, f"masked{t}_{c}", after)
             a_acc = project(bank, wa_mx, c, t)
             nc.vector.scalar_tensor_tensor(masked[pair, c][:, t - pair[0], :], saved[t, c], 0.0, a_acc[:], ALU.is_gt, ALU.mult)
@@ -205,19 +198,10 @@ def tile_list_spill_damped_grad_kernel(tc, tab_words, tab_scales, offs, sT, wa, 
         def finish_pair(pair, c):
             nc.gpsimd.tensor_tensor(
                 h_grouped[c][:, :, pair[0] : pair[1] + 1],
-                masked[pair, c][:].rearrange("p t c -> p c t"),
+                masked[pair, c][:, :, :].rearrange("p t c -> p c t"),
                 damp[pair, c][:].rearrange("p t c -> p c t"),
                 ALU.mult,
             )
-
-        def finish_slot(pair, c, t):
-            i = t - pair[0]
-            nc.gpsimd.tensor_tensor(h_grouped[c][:, :, t], masked[t, c][:], damp[pair, c][:, i, :], ALU.mult)
-
-        def masked_slot(c, t):
-            masked[t, c] = held([P, CHUNK], F32, f"masked_slot{t}_{c}")
-            a_acc = project(f"a{t}", wa_mx, c, t)
-            nc.vector.scalar_tensor_tensor(masked[t, c][:], saved[t, c], 0.0, a_acc[:], ALU.is_gt, ALU.mult)
 
         wo_mx = {}
 
@@ -279,37 +263,43 @@ def tile_list_spill_damped_grad_kernel(tc, tab_words, tab_scales, offs, sT, wa, 
         def store(n):
             nc.sync.dma_start(out[n * P : (n + 1) * P, :], windows[n % WINDOWS][:])
 
-        damping(0, LOW, size_after="wa_raw0")
+        for c in range(CHUNKS):
+            pick_saved(0, c)
+        load_slot(2, after="s_rows0")
+        quantize_wa(0)
+        load_slot(3, after="wa0_grouped")
+        quantize_wa(1)
+        open_window(after="wa1_grouped")
+        damping(0, LOW, root_after="wa_raw1")
         squares(0, LOW)
-        damping(0, HIGH)
+        damping(0, HIGH, size_after="size0_0")
         squares(0, HIGH)
-        for t in range(PACK):
-            pick_saved(t, 0)
-            masked_slot(0, t)
-            finish_slot(LOW if t in LOW else HIGH, 0, t)
+        for pair in (LOW, HIGH):
+            for t in pair:
+                if t:
+                    pick_saved(t, 0)
+                masked_product(pair, 0, t, f"a{t}")
+            finish_pair(pair, 0)
         load_wo(0, 2, after="saved0_0")
-        gains = held([P, S], F32, "gains", after="size0_0")
+        gains = held([P, S], F32, "gains", after="saved1_0")
         nc.sync.dma_start(gains[:], wgo)
-        load_wo(2, 2, after="masked_slot0_0")
-        load_wo(4, 4, after="size2_0")
+        load_wo(2, 2, after="saved2_0")
+        load_wo(4, 4, after="masked2_0")
         quantize_wo(0)
-        quantize_wo(2)
         damping(1, LOW)
         damping(1, HIGH)
-        late = held([P, 2, CHUNK], F32, "late_low", after="saved3_0")
-        for t in LOW:
-            pick_saved(t, 1, late[:, t, :])
+        late = held([P, PACK - 1, CHUNK], F32, "late", after="saved3_0")
+        for t in range(1, PACK):
+            pick_saved(t, 1, late[:, t - 1, :])
         quantize_h(0, slice(0, CHUNK))
-        late = held([P, 2, CHUNK], F32, "late_high", after="h0_grouped")
-        for t in HIGH:
-            pick_saved(t, 1, late[:, t - HIGH[0], :])
+        quantize_wo(2, words_after="h0_grouped")
         halves = [slice(u * HALF, (u + 1) * HALF) for u in range(2)]
         for u, part in enumerate(halves):
             place_weighted(0, part, f"y0_half{u}", after=None if u else "wo2_grouped")
-        masked_product(LOW, 1, 0, "a0", after="wo2_raw")
-        masked_product(LOW, 1, 1, "a1")
-        masked_product(HIGH, 1, 2, "a2", after="s_rows3")
-        masked_product(HIGH, 1, 3, "a3")
+        second = held([P, PACK, CHUNK], F32, "masked2_1", after="damp2_0")
+        masked[LOW, 1], masked[HIGH, 1] = second[:, 0:2, :], second[:, 2:4, :]
+        for t in range(PACK):
+            masked_product(LOW if t in LOW else HIGH, 1, t, f"a{t}")
         for n in (1, 2):
             place_weighted(n, slice(0, CHUNK), f"y{n}_0")
         h_grouped.append(held([P, CHUNK, PACK], BF16, "h1_grouped", after="y2_0"))
@@ -321,7 +311,7 @@ def tile_list_spill_damped_grad_kernel(tc, tab_words, tab_scales, offs, sT, wa, 
         y = held([P, CHUNK], F32, "y3_0", after="masked2_1")
         embed(y[:], 3, 0)
         place(y[:], 3, 0, CHUNK)
-        quantize_wo(4, after="size2_1", words_after="y3_0")
+        quantize_wo(4, after="y1_0_weighted", words_after="y3_0")
         for n in range(EARLY):
             y = held([P, CHUNK], F32, f"y{n}_1")
             embed(y[:], n, 1)

@@ -27,8 +27,8 @@ QUADRANT = 32
 SCALE_ROWS = 4
 LINE = 16
 WORDS_A_LINE = LINE // 4
-EARLY = 4
-WINDOWS = 4
+EARLY = 5
+WINDOWS = 5
 WO_PIECE = 256
 Y_TILES = 3
 LOW, HIGH = (0, 1), (2, 3)
@@ -101,6 +101,7 @@ def tile_list_spill_damped_grad_kernel(tc, tab_words, tab_scales, offs, sT, wa, 
                 staged[first : first + SCALE_ROWS * PASSES, :].bitcast(I32),
             )
         open_window(after="picked_sc")
+        open_window(after="staged")
         s_rows = []
 
         def load_slot(t, after):
@@ -129,8 +130,11 @@ def tile_list_spill_damped_grad_kernel(tc, tab_words, tab_scales, offs, sT, wa, 
             grouped = held([P, H * PACK], BF16, f"wa{a}_grouped")
             into = grouped[:].rearrange("p (t m j) -> p m j t", t=PACK, j=PACK)
             rows = wa_raw[a][:].rearrange("p j (m t) -> p m j t", t=PACK)
-            nc.vector.tensor_copy(into[:, :, :, 0:2], rows[:, :, :, 0:2])
-            nc.scalar.copy(into[:, :, :, 2:4], rows[:, :, :, 2:4])
+            if a == 0:
+                nc.vector.tensor_copy(into, rows)
+            else:
+                nc.vector.tensor_copy(into[:, :, :, 0:2], rows[:, :, :, 0:2])
+                nc.scalar.copy(into[:, :, :, 2:4], rows[:, :, :, 2:4])
             words = held([P, H], U32, f"wa{a}_words")
             scales = held([P, H], U8, f"wa{a}_scales")
             nc.vector.quantize_mx(out=words[:].bitcast(E4M3), scales=scales[:], in_=grouped[:])
@@ -168,13 +172,19 @@ def tile_list_spill_damped_grad_kernel(tc, tab_words, tab_scales, offs, sT, wa, 
             for a in range(PASSES)
             for t in range(PACK)
         }
-        roots, damp, saved, masked = {}, {}, {}, {}
+        sizes, roots, damp, saved, masked = {}, {}, {}, {}, {}
 
-        def damping(c, pair, size_after=None, root_after=None):
+        def damping(c, pair, size_after=None, root_after=None, later=False):
             size = held([P, 2, CHUNK], F32, f"size{pair[0]}_{c}", size_after)
             for i, t in enumerate(pair):
                 nc.scalar.activation(size[:, i, :], project(f"b{i}", wb_mx, c, t)[:], ACT.Abs)
-            roots[pair, c] = held([P, 2, CHUNK], F32, f"root{pair[0]}_{c}", root_after) if root_after else size
+            sizes[pair, c] = size
+            if not later:
+                take_roots(c, pair, root_after)
+
+        def take_roots(c, pair, after):
+            size = sizes[pair, c]
+            roots[pair, c] = held([P, 2, CHUNK], F32, f"root{pair[0]}_{c}", after) if after else size
             for i in range(2):
                 nc.scalar.activation(roots[pair, c][:, i, :], size[:, i, :], ACT.Abs_reciprocal_sqrt, bias=1.0)
 
@@ -195,11 +205,11 @@ def tile_list_spill_damped_grad_kernel(tc, tab_words, tab_scales, offs, sT, wa, 
 
         h_grouped = [held([P, CHUNK, PACK], BF16, "h0_grouped")]
 
-        def finish_pair(pair, c):
+        def finish_pair(pair, c, left, right, part=slice(0, CHUNK)):
             nc.gpsimd.tensor_tensor(
-                h_grouped[c][:, :, pair[0] : pair[1] + 1],
-                masked[pair, c][:, :, :].rearrange("p t c -> p c t"),
-                damp[pair, c][:].rearrange("p t c -> p c t"),
+                h_grouped[c][:, part, pair[0] : pair[1] + 1],
+                left[:, :, part].rearrange("p t c -> p c t"),
+                right[:, :, part].rearrange("p t c -> p c t"),
                 ALU.mult,
             )
 
@@ -263,6 +273,7 @@ def tile_list_spill_damped_grad_kernel(tc, tab_words, tab_scales, offs, sT, wa, 
         def store(n):
             nc.sync.dma_start(out[n * P : (n + 1) * P, :], windows[n % WINDOWS][:])
 
+        halves = [slice(u * HALF, (u + 1) * HALF) for u in range(2)]
         for c in range(CHUNKS):
             pick_saved(0, c)
         load_slot(2, after="s_rows0")
@@ -270,8 +281,8 @@ def tile_list_spill_damped_grad_kernel(tc, tab_words, tab_scales, offs, sT, wa, 
         load_slot(3, after="wa0_grouped")
         quantize_wa(1)
         open_window(after="wa1_grouped")
-        damping(0, LOW, root_after="wa_raw1")
-        squares(0, LOW)
+        damping(0, LOW)
+        squares(0, LOW, after="wa_raw1")
         damping(0, HIGH, size_after="size0_0")
         squares(0, HIGH)
         for pair in (LOW, HIGH):
@@ -279,39 +290,46 @@ def tile_list_spill_damped_grad_kernel(tc, tab_words, tab_scales, offs, sT, wa, 
                 if t:
                     pick_saved(t, 0)
                 masked_product(pair, 0, t, f"a{t}")
-            finish_pair(pair, 0)
+            for part in halves if pair == HIGH else [slice(0, CHUNK)]:
+                finish_pair(pair, 0, masked[pair, 0], damp[pair, 0], part)
         load_wo(0, 2, after="saved0_0")
         gains = held([P, S], F32, "gains", after="saved1_0")
         nc.sync.dma_start(gains[:], wgo)
-        load_wo(2, 2, after="saved2_0")
-        load_wo(4, 4, after="masked2_0")
+        load_wo(2, 4, after="saved2_0")
+        load_wo(6, 2, after="masked2_0")
         quantize_wo(0)
-        damping(1, LOW)
-        damping(1, HIGH)
+        damping(1, LOW, size_after="size2_0")
         late = held([P, PACK - 1, CHUNK], F32, "late", after="saved3_0")
         for t in range(1, PACK):
             pick_saved(t, 1, late[:, t - 1, :])
-        quantize_h(0, slice(0, CHUNK))
+        for part in halves:
+            quantize_h(0, part)
         quantize_wo(2, words_after="h0_grouped")
-        halves = [slice(u * HALF, (u + 1) * HALF) for u in range(2)]
         for u, part in enumerate(halves):
             place_weighted(0, part, f"y0_half{u}", after=None if u else "wo2_grouped")
-        second = held([P, PACK, CHUNK], F32, "masked2_1", after="damp2_0")
-        masked[LOW, 1], masked[HIGH, 1] = second[:, 0:2, :], second[:, 2:4, :]
-        for t in range(PACK):
-            masked_product(LOW if t in LOW else HIGH, 1, t, f"a{t}")
-        for n in (1, 2):
+        masked_product(LOW, 1, 0, "a0", after="damp2_0")
+        masked_product(LOW, 1, 1, "a1")
+        for n in range(1, EARLY - 1):
             place_weighted(n, slice(0, CHUNK), f"y{n}_0")
-        h_grouped.append(held([P, CHUNK, PACK], BF16, "h1_grouped", after="y2_0"))
-        squares(1, LOW)
-        finish_pair(LOW, 1)
+        h_grouped.append(held([P, CHUNK, PACK], BF16, "h1_grouped", after=f"y{EARLY - 2}_0"))
+        squares(1, LOW, after="y0_half1")
+        finish_pair(LOW, 1, masked[LOW, 1], damp[LOW, 1])
+        plain = held([P, 2, CHUNK], F32, "plain", after="y1_0")
+        for i, t in enumerate(HIGH):
+            nc.scalar.copy(plain[:, i, :], project(f"a{t}", wa_mx, 1, t)[:])
+        damping(1, HIGH, size_after="y0_half0")
         squares(1, HIGH)
-        finish_pair(HIGH, 1)
+        damped = held([P, 2, CHUNK], F32, "damped", after="masked0_1")
+        nc.gpsimd.tensor_tensor(damped[:], plain[:], damp[HIGH, 1][:], ALU.mult)
+        mask = held([P, 2, CHUNK], F32, "mask", after="y2_0")
+        nc.scalar.activation(mask[:], late[:, 1:3, :], ACT.Sign)
+        nc.scalar.activation(mask[:], mask[:], ACT.Relu)
+        finish_pair(HIGH, 1, damped, mask)
         quantize_h(1, slice(0, CHUNK))
-        y = held([P, CHUNK], F32, "y3_0", after="masked2_1")
-        embed(y[:], 3, 0)
-        place(y[:], 3, 0, CHUNK)
-        quantize_wo(4, after="y1_0_weighted", words_after="y3_0")
+        y = held([P, CHUNK], F32, "y_between", after="damped")
+        embed(y[:], EARLY - 1, 0)
+        place(y[:], EARLY - 1, 0, CHUNK)
+        quantize_wo(6, after="plain", words_after="y_between")
         for n in range(EARLY):
             y = held([P, CHUNK], F32, f"y{n}_1")
             embed(y[:], n, 1)

@@ -101,7 +101,6 @@ def tile_list_spill_damped_grad_kernel(tc, tab_words, tab_scales, offs, sT, wa, 
                 staged[first : first + SCALE_ROWS * PASSES, :].bitcast(I32),
             )
         open_window(after="picked_sc")
-        open_window(after="staged")
         s_rows = []
 
         def load_slot(t, after):
@@ -120,9 +119,9 @@ def tile_list_spill_damped_grad_kernel(tc, tab_words, tab_scales, offs, sT, wa, 
             wb_w_raw[:].rearrange("p a (m i t) -> p a m t i", t=PACK, i=WORDS_A_LINE),
         )
 
-        wa_raw.append(held([P, PACK, H], F32, "wa_raw1", after="wb_w_raw"))
+        wa_raw.append(held([P, PACK, H], F32, "wa_raw1", after="tab_w1"))
         nc.sync.dma_start(wa_raw[1][:], wa_by_pass[1])
-        load_slot(1, after="tab_w1")
+        open_window(after="wb_w_raw")
 
         wa_mx = {}
 
@@ -276,8 +275,9 @@ def tile_list_spill_damped_grad_kernel(tc, tab_words, tab_scales, offs, sT, wa, 
         halves = [slice(u * HALF, (u + 1) * HALF) for u in range(2)]
         for c in range(CHUNKS):
             pick_saved(0, c)
-        load_slot(2, after="s_rows0")
+        load_slot(1, after="s_rows0")
         quantize_wa(0)
+        load_slot(2, after="wa_raw0")
         load_slot(3, after="wa0_grouped")
         quantize_wa(1)
         open_window(after="wa1_grouped")

@@ -27,8 +27,8 @@ QUADRANT = 32
 SCALE_ROWS = 4
 LINE = 16
 WORDS_A_LINE = LINE // 4
-EARLY = 5
-WINDOWS = 5
+EARLY = 6
+WINDOWS = 6
 WO_PIECE = 256
 Y_TILES = 3
 LOW, HIGH = (0, 1), (2, 3)
@@ -122,6 +122,7 @@ def tile_list_spill_damped_grad_kernel(tc, tab_words, tab_scales, offs, sT, wa, 
         wa_raw.append(held([P, PACK, H], F32, "wa_raw1", after="tab_w1"))
         nc.sync.dma_start(wa_raw[1][:], wa_by_pass[1])
         open_window(after="wb_w_raw")
+        open_window(after="staged")
 
         wa_mx = {}
 
@@ -130,7 +131,8 @@ def tile_list_spill_damped_grad_kernel(tc, tab_words, tab_scales, offs, sT, wa, 
             into = grouped[:].rearrange("p (t m j) -> p m j t", t=PACK, j=PACK)
             rows = wa_raw[a][:].rearrange("p j (m t) -> p m j t", t=PACK)
             if a == 0:
-                nc.vector.tensor_copy(into, rows)
+                nc.vector.tensor_copy(into[:, :, :, 0:2], rows[:, :, :, 0:2])
+                nc.vector.tensor_copy(into[:, :, :, 2:4], rows[:, :, :, 2:4])
             else:
                 nc.vector.tensor_copy(into[:, :, :, 0:2], rows[:, :, :, 0:2])
                 nc.scalar.copy(into[:, :, :, 2:4], rows[:, :, :, 2:4])
@@ -206,9 +208,9 @@ def tile_list_spill_damped_grad_kernel(tc, tab_words, tab_scales, offs, sT, wa, 
 
         def finish_pair(pair, c, left, right, part=slice(0, CHUNK)):
             nc.gpsimd.tensor_tensor(
-                h_grouped[c][:, part, pair[0] : pair[1] + 1],
-                left[:, :, part].rearrange("p t c -> p c t"),
-                right[:, :, part].rearrange("p t c -> p c t"),
+                h_grouped[c][:, part, pair[0] : pair[1] + 1].rearrange("p (c i) t -> p c t i", i=WORDS_A_LINE),
+                left[:, :, part].rearrange("p t (c i) -> p c t i", i=WORDS_A_LINE),
+                right[:, :, part].rearrange("p t (c i) -> p c t i", i=WORDS_A_LINE),
                 ALU.mult,
             )
 

@@ -231,7 +231,7 @@ def tile_list_spill_damped_grad_kernel(tc, tab_words, tab_scales, offs, sT, wa, 
             for i in range(columns // P):
                 wo_mx[first_tile + i] = words[:, i * P : (i + 1) * P], scales[:, i * P : (i + 1) * P]
 
-        h_words = [held([P, CHUNK], U32, f"h{c}_words") for c in range(CHUNKS)]
+        h_words = {1: held([P, CHUNK], U32, "h1_words")}
         h_scales = [held([P, CHUNK], U8, f"h{c}_scales") for c in range(CHUNKS)]
 
         def quantize_h(c, part):
@@ -265,9 +265,9 @@ def tile_list_spill_damped_grad_kernel(tc, tab_words, tab_scales, offs, sT, wa, 
 
         def place_weighted(n, part, name, after=None):
             count = part.stop - part.start
-            y = held([P, count], F32, name)
+            y = held([P, count], F32, name, after)
             embed(y[:], n, 0, part)
-            weighted = held([P, count], F32, f"{name}_weighted", after)
+            weighted = held([P, count], F32, f"{name}_weighted")
             nc.gpsimd.tensor_tensor(weighted[:], y[:], gains[:, part], ALU.mult)
             nc.vector.tensor_copy(spots(n, part.start, count), weighted[:])
 
@@ -291,25 +291,28 @@ def tile_list_spill_damped_grad_kernel(tc, tab_words, tab_scales, offs, sT, wa, 
             for t in pair:
                 if t:
                     pick_saved(t, 0)
+                if t == HIGH[0]:
+                    pick_saved(t, 1)
                 masked_product(pair, 0, t, f"a{t}")
             for part in halves if pair == HIGH else [slice(0, CHUNK)]:
                 finish_pair(pair, 0, masked[pair, 0], damp[pair, 0], part)
         load_wo(0, 2, after="saved0_0")
-        gains = held([P, S], F32, "gains", after="saved1_0")
+        load_wo(2, 4, after="saved1_0")
+        gains = held([P, S], F32, "gains", after="saved2_0")
         nc.sync.dma_start(gains[:], wgo)
-        load_wo(2, 4, after="saved2_0")
         load_wo(6, 2, after="masked2_0")
         quantize_wo(0)
         damping(1, LOW, size_after="size2_0")
-        late = held([P, PACK - 1, CHUNK], F32, "late", after="saved3_0")
-        for t in range(1, PACK):
-            pick_saved(t, 1, late[:, t - 1, :])
+        late = held([P, 2, CHUNK], F32, "late", after="saved3_0")
+        for i, t in enumerate((LOW[1], HIGH[1])):
+            pick_saved(t, 1, late[:, i, :])
+        h_words[0] = held([P, CHUNK], U32, "h0_words", after="wo0_raw")
         for part in halves:
             quantize_h(0, part)
-        quantize_wo(2, words_after="h0_grouped")
+        quantize_wo(2)
         for u, part in enumerate(halves):
-            place_weighted(0, part, f"y0_half{u}", after=None if u else "wo2_grouped")
-        masked_product(LOW, 1, 0, "a0", after="damp2_0")
+            place_weighted(0, part, f"y0_half{u}", after=None if u else "wo2_raw")
+        masked_product(LOW, 1, 0, "a0", after="h0_grouped")
         masked_product(LOW, 1, 1, "a1")
         for n in range(1, EARLY - 1):
             place_weighted(n, slice(0, CHUNK), f"y{n}_0")
@@ -324,7 +327,8 @@ def tile_list_spill_damped_grad_kernel(tc, tab_words, tab_scales, offs, sT, wa, 
         damped = held([P, 2, CHUNK], F32, "damped", after="masked0_1")
         nc.gpsimd.tensor_tensor(damped[:], plain[:], damp[HIGH, 1][:], ALU.mult)
         mask = held([P, 2, CHUNK], F32, "mask", after="y2_0")
-        nc.scalar.activation(mask[:], late[:, 1:3, :], ACT.Sign)
+        for i, t in enumerate(HIGH):
+            nc.scalar.activation(mask[:, i, :], saved[t, 1], ACT.Sign)
         nc.scalar.activation(mask[:], mask[:], ACT.Relu)
         finish_pair(HIGH, 1, damped, mask)
         quantize_h(1, slice(0, CHUNK))

@@ -27,8 +27,8 @@ QUADRANT = 32
 SCALE_ROWS = 4
 LINE = 16
 WORDS_A_LINE = LINE // 4
-EARLY = 6
-WINDOWS = 6
+EARLY = 5
+WINDOWS = 5
 WO_PIECE = 256
 Y_TILES = 3
 LOW, HIGH = (0, 1), (2, 3)
@@ -107,22 +107,22 @@ def tile_list_spill_damped_grad_kernel(tc, tab_words, tab_scales, offs, sT, wa, 
             s_rows.append(held([P, T], F32, f"s_rows{t}", after))
             nc.sync.dma_start(s_rows[t][:], s_by_slot[t])
 
-        load_slot(0, after="tab_sc")
+        wa_raw = [held([P, PACK, H], F32, "wa_raw0", after="tab_sc")]
+        nc.sync.dma_start(wa_raw[0][:], wa_by_pass[0])
         v_w = [held([P, S], U32, f"v_w{a}") for a in range(PASSES)]
         for a in range(PASSES):
             nc.vector.tensor_copy(v_w[a][:], tab_w[a][:].bitcast(U32).indirect(picks[:]))
-        wa_raw = [held([P, PACK, H], F32, "wa_raw0", after="tab_w0")]
-        nc.sync.dma_start(wa_raw[0][:], wa_by_pass[0])
         wb_w = held([P, PASSES, H], I32, "wb_w")
         nc.vector.tensor_copy(
             wb_w[:].rearrange("p a (t m i) -> p a m t i", t=PACK, i=WORDS_A_LINE),
             wb_w_raw[:].rearrange("p a (m i t) -> p a m t i", t=PACK, i=WORDS_A_LINE),
         )
 
-        wa_raw.append(held([P, PACK, H], F32, "wa_raw1", after="tab_w1"))
+        wa_raw.append(held([P, PACK, H], F32, "wa_raw1", after="tab_w0"))
         nc.sync.dma_start(wa_raw[1][:], wa_by_pass[1])
+        load_slot(0, after="staged")
+        load_slot(1, after="tab_w1")
         open_window(after="wb_w_raw")
-        open_window(after="staged")
 
         wa_mx = {}
 
@@ -130,7 +130,7 @@ def tile_list_spill_damped_grad_kernel(tc, tab_words, tab_scales, offs, sT, wa, 
             grouped = held([P, H * PACK], BF16, f"wa{a}_grouped")
             into = grouped[:].rearrange("p (t m j) -> p m j t", t=PACK, j=PACK)
             rows = wa_raw[a][:].rearrange("p j (m t) -> p m j t", t=PACK)
-            if a == 0:
+            if a == 1:
                 nc.vector.tensor_copy(into[:, :, :, 0:2], rows[:, :, :, 0:2])
                 nc.vector.tensor_copy(into[:, :, :, 2:4], rows[:, :, :, 2:4])
             else:
@@ -214,17 +214,22 @@ def tile_list_spill_damped_grad_kernel(tc, tab_words, tab_scales, offs, sT, wa, 
                 ALU.mult,
             )
 
+        def finish_slot(t):
+            pair = LOW if t in LOW else HIGH
+            i = t - pair[0]
+            nc.gpsimd.tensor_tensor(h_grouped[0][:, :, t], masked[pair, 0][:, i, :], damp[pair, 0][:, i, :], ALU.mult)
+
         wo_mx = {}
 
-        def quantize_wo(first_tile, after=None, words_after=None):
-            rows = wo_raw[first_tile][:]
-            columns = rows.shape[2]
+        def quantize_wo(first_tile, tiles, after=None, words_after=None):
+            columns = tiles * P
             name = f"wo{first_tile}"
             grouped = held([P, columns, PACK], BF16, f"{name}_grouped", after)
-            nc.scalar.copy(
-                grouped[:].rearrange("p (c i) j -> p c j i", i=WORDS_A_LINE),
-                rows.rearrange("p j (c i) -> p c j i", i=WORDS_A_LINE),
-            )
+            for first in range(0, columns, WO_PIECE):
+                nc.scalar.copy(
+                    grouped[:, first : first + WO_PIECE, :].rearrange("p (c i) j -> p c j i", i=WORDS_A_LINE),
+                    wo_raw[first_tile + first // P][:].rearrange("p j (c i) -> p c j i", i=WORDS_A_LINE),
+                )
             words = held([P, columns], U32, f"{name}_words", words_after)
             scales = held([P, columns], U8, f"{name}_scales")
             nc.vector.quantize_mx(out=words[:].bitcast(E4M3), scales=scales[:], in_=grouped[:].rearrange("p c j -> p (c j)"))
@@ -238,7 +243,7 @@ def tile_list_spill_damped_grad_kernel(tc, tab_words, tab_scales, offs, sT, wa, 
             nc.vector.quantize_mx(
                 out=h_words[c][:, part].bitcast(E4M3),
                 scales=h_scales[c][:, part],
-                in_=h_grouped[c][:, part, :].rearrange("p c j -> p (c j)"),
+                in_=h_grouped[2 * c][:, part, :].rearrange("p c j -> p (c j)"),
             )
 
         filled = []
@@ -275,67 +280,74 @@ def tile_list_spill_damped_grad_kernel(tc, tab_words, tab_scales, offs, sT, wa, 
             nc.sync.dma_start(out[n * P : (n + 1) * P, :], windows[n % WINDOWS][:])
 
         halves = [slice(u * HALF, (u + 1) * HALF) for u in range(2)]
-        for c in range(CHUNKS):
-            pick_saved(0, c)
-        load_slot(1, after="s_rows0")
         quantize_wa(0)
-        load_slot(2, after="wa_raw0")
-        load_slot(3, after="wa0_grouped")
+        load_slot(2, after="wa0_grouped")
         quantize_wa(1)
+        load_slot(3, after="wa_raw1")
         open_window(after="wa1_grouped")
-        damping(0, LOW)
-        squares(0, LOW, after="wa_raw1")
-        damping(0, HIGH, size_after="size0_0")
+        damping(0, LOW, size_after="wa_raw0")
+        squares(0, LOW)
+        damping(0, HIGH)
         squares(0, HIGH)
         for pair in (LOW, HIGH):
             for t in pair:
-                if t:
-                    pick_saved(t, 0)
-                if t == HIGH[0]:
+                pick_saved(t, 0)
+                if t == 0:
                     pick_saved(t, 1)
                 masked_product(pair, 0, t, f"a{t}")
-            for part in halves if pair == HIGH else [slice(0, CHUNK)]:
-                finish_pair(pair, 0, masked[pair, 0], damp[pair, 0], part)
+                finish_slot(t)
         load_wo(0, 2, after="saved0_0")
-        load_wo(2, 4, after="saved1_0")
+        load_wo(2, 2, after="saved1_0")
+        load_wo(4, 2, after="size0_0")
         gains = held([P, S], F32, "gains", after="saved2_0")
         nc.sync.dma_start(gains[:], wgo)
         load_wo(6, 2, after="masked2_0")
-        quantize_wo(0)
-        damping(1, LOW, size_after="size2_0")
+        quantize_wo(0, 2)
+        damping(1, LOW)
+        squares(1, LOW)
         late = held([P, 2, CHUNK], F32, "late", after="saved3_0")
-        for i, t in enumerate((LOW[1], HIGH[1])):
+        for i, t in enumerate((1, 2)):
             pick_saved(t, 1, late[:, i, :])
         h_words[0] = held([P, CHUNK], U32, "h0_words", after="wo0_raw")
         for part in halves:
             quantize_h(0, part)
-        quantize_wo(2)
+        quantize_wo(2, 4)
+        latest = held([P, CHUNK], F32, "latest", after="h0_grouped")
+        pick_saved(3, 1, latest[:])
         for u, part in enumerate(halves):
-            place_weighted(0, part, f"y0_half{u}", after=None if u else "wo2_raw")
-        masked_product(LOW, 1, 0, "a0", after="h0_grouped")
-        masked_product(LOW, 1, 1, "a1")
+            place_weighted(0, part, f"y0_half{u}", after=None if u else "wo4_raw")
         for n in range(1, EARLY - 1):
             place_weighted(n, slice(0, CHUNK), f"y{n}_0")
-        h_grouped.append(held([P, CHUNK, PACK], BF16, "h1_grouped", after=f"y{EARLY - 2}_0"))
-        squares(1, LOW, after="y0_half1")
-        finish_pair(LOW, 1, masked[LOW, 1], damp[LOW, 1])
-        plain = held([P, 2, CHUNK], F32, "plain", after="y1_0")
-        for i, t in enumerate(HIGH):
-            nc.scalar.copy(plain[:, i, :], project(f"a{t}", wa_mx, 1, t)[:])
+        h_grouped.append(held([P, CHUNK, PACK], BF16, "h1_unmasked", after=f"y{EARLY - 2}_0"))
+
+        def plain_pair(pair, after):
+            plain = held([P, 2, CHUNK], F32, f"plain{pair[0]}", after)
+            for i, t in enumerate(pair):
+                nc.scalar.copy(plain[:, i, :], project(f"a{t}", wa_mx, 1, t)[:])
+            finish_pair(pair, 1, plain, damp[pair, 1])
+
+        plain_pair(LOW, after="wo2_raw")
         damping(1, HIGH, size_after="y0_half0")
         squares(1, HIGH)
-        damped = held([P, 2, CHUNK], F32, "damped", after="masked0_1")
-        nc.gpsimd.tensor_tensor(damped[:], plain[:], damp[HIGH, 1][:], ALU.mult)
-        mask = held([P, 2, CHUNK], F32, "mask", after="y2_0")
-        for i, t in enumerate(HIGH):
-            nc.scalar.activation(mask[:, i, :], saved[t, 1], ACT.Sign)
-        nc.scalar.activation(mask[:], mask[:], ACT.Relu)
-        finish_pair(HIGH, 1, damped, mask)
-        quantize_h(1, slice(0, CHUNK))
-        y = held([P, CHUNK], F32, "y_between", after="damped")
+        plain_pair(HIGH, after="y1_0")
+        signs = held([P, PACK, CHUNK], BF16, "signs", after="size2_1")
+        for t in range(PACK):
+            nc.scalar.activation(signs[:, t, :], saved[t, 1], ACT.Sign)
+        mask = held([P, CHUNK, PACK], BF16, "mask")
+        nc.scalar.activation(
+            mask[:].rearrange("p (c i) j -> p c j i", i=WORDS_A_LINE),
+            signs[:].rearrange("p j (c i) -> p c j i", i=WORDS_A_LINE),
+            ACT.Relu,
+        )
+        h_grouped.append(held([P, CHUNK, PACK], BF16, "h1_grouped"))
+        for part in halves:
+            nc.vector.tensor_tensor(h_grouped[2][:, part, :], h_grouped[1][:, part, :], mask[:, part, :], ALU.mult)
+        for part in halves:
+            quantize_h(1, part)
+        quantize_wo(6, 2, after="y2_0", words_after="plain2")
+        y = held([P, CHUNK], F32, "y_between", after="mask")
         embed(y[:], EARLY - 1, 0)
         place(y[:], EARLY - 1, 0, CHUNK)
-        quantize_wo(6, after="plain", words_after="y_between")
         for n in range(EARLY):
             y = held([P, CHUNK], F32, f"y{n}_1")
             embed(y[:], n, 1)

@@ -316,7 +316,8 @@ def tile_list_spill_damped_grad_kernel(tc, tab_words, tab_scales, offs, sT, wa, 
         pick_saved(3, 1, latest[:])
         for u, part in enumerate(halves):
             place_weighted(0, part, f"y0_half{u}", after=None if u else "wo4_raw")
-        for n in range(1, EARLY - 1):
+            place_weighted(1, part, f"y1_half{u}")
+        for n in range(2, EARLY - 1):
             place_weighted(n, slice(0, CHUNK), f"y{n}_0")
         h_grouped.append(held([P, CHUNK, PACK], BF16, "h1_unmasked", after=f"y{EARLY - 2}_0"))
 
@@ -329,7 +330,7 @@ def tile_list_spill_damped_grad_kernel(tc, tab_words, tab_scales, offs, sT, wa, 
         plain_pair(LOW, after="wo2_raw")
         damping(1, HIGH, size_after="y0_half0")
         squares(1, HIGH)
-        plain_pair(HIGH, after="y1_0")
+        plain_pair(HIGH, after="y1_half1")
         signs = held([P, PACK, CHUNK], BF16, "signs", after="size2_1")
         for t in range(PACK):
             nc.scalar.activation(signs[:, t, :], saved[t, 1], ACT.Sign)
@@ -344,8 +345,7 @@ def tile_list_spill_damped_grad_kernel(tc, tab_words, tab_scales, offs, sT, wa, 
             nc.vector.tensor_tensor(h_grouped[2][:, part, :], h_grouped[1][:, part, :], mask[:, part, :], ALU.mult)
         for part in halves:
             quantize_h(1, part)
-        quantize_wo(6, 2, after="y2_0", words_after="plain2")
-        y = held([P, CHUNK], F32, "y_between", after="mask")
+        y = held([P, CHUNK], F32, "y_between", after="signs")
         embed(y[:], EARLY - 1, 0)
         place(y[:], EARLY - 1, 0, CHUNK)
         for n in range(EARLY):
@@ -353,6 +353,8 @@ def tile_list_spill_damped_grad_kernel(tc, tab_words, tab_scales, offs, sT, wa, 
             embed(y[:], n, 1)
             place(y[:], n, CHUNK, CHUNK)
             store(n)
+            if n == 0:
+                quantize_wo(6, 2, after="mask", words_after="y_between")
         for n in range(EARLY, N // P):
             y = ring.tile([P, S], F32, name="y")
             for c in range(CHUNKS):

@@ -291,10 +291,18 @@ def tile_list_spill_damped_grad_kernel(tc, tab_words, tab_scales, offs, sT, wa, 
         squares(0, HIGH)
         for pair in (LOW, HIGH):
             for t in pair:
-                pick_saved(t, 0)
-                if t == 0:
-                    pick_saved(t, 1)
-                masked_product(pair, 0, t, f"a{t}")
+                if t == PACK - 1:
+                    a_acc = project(f"a{t}", wa_mx, 0, t)
+                    parts = [held([P, HALF], F32, f"saved3_half{u}") for u in range(2)]
+                    for part, into in zip(halves, parts):
+                        nc.vector.tensor_copy(into[:], s_rows[t][:].indirect(picks[:, entries(part.start, HALF)]))
+                    for part, picked in zip(halves, parts):
+                        nc.vector.scalar_tensor_tensor(masked[pair, 0][:, 1, part], picked[:], 0.0, a_acc[:, part], ALU.is_gt, ALU.mult)
+                else:
+                    pick_saved(t, 0)
+                    if t == 0:
+                        pick_saved(t, 1)
+                    masked_product(pair, 0, t, f"a{t}")
                 finish_slot(t)
         load_wo(0, 2, after="saved0_0")
         load_wo(2, 2, after="saved1_0")
@@ -305,7 +313,7 @@ def tile_list_spill_damped_grad_kernel(tc, tab_words, tab_scales, offs, sT, wa, 
         quantize_wo(0, 2)
         damping(1, LOW)
         squares(1, LOW)
-        late = held([P, 2, CHUNK], F32, "late", after="saved3_0")
+        late = held([P, 2, CHUNK], F32, "late", after="saved3_half0")
         for i, t in enumerate((1, 2)):
             pick_saved(t, 1, late[:, i, :])
         h_words[0] = held([P, CHUNK], U32, "h0_words", after="wo0_raw")

@@ -248,7 +248,7 @@ def tile_list_spill_damped_grad_kernel(tc, tab_words, tab_scales, offs, sT, wa, 
 
         filled = []
 
-        def embed(y, n, c, part=slice(0, CHUNK)):
+        def embed(y, n, c, part=slice(0, CHUNK), weigh=False):
             y_acc = psum.tile([P, CHUNK], F32, name=f"y{len(filled) % 2}")
             filled.append(n)
             nc.tensor.matmul_mx(
@@ -260,7 +260,10 @@ def tile_list_spill_damped_grad_kernel(tc, tab_words, tab_scales, offs, sT, wa, 
                 start=True,
                 stop=True,
             )
-            nc.scalar.copy(y, y_acc[:, part])
+            if weigh:
+                nc.vector.tensor_tensor(y, y_acc[:, part], gains[:, part], ALU.mult)
+            else:
+                nc.scalar.copy(y, y_acc[:, part])
 
         def spots(n, first, count):
             return windows[n % WINDOWS][:].indirect(places[:, entries(first, count)])
@@ -322,9 +325,12 @@ def tile_list_spill_damped_grad_kernel(tc, tab_words, tab_scales, offs, sT, wa, 
         quantize_wo(2, 4)
         latest = held([P, CHUNK], F32, "latest", after="h0_grouped")
         pick_saved(3, 1, latest[:])
-        for u, part in enumerate(halves):
-            place_weighted(0, part, f"y0_half{u}", after=None if u else "wo4_raw")
-            place_weighted(1, part, f"y1_half{u}")
+        y = held([P, HALF], F32, "y0_half0", after="wo4_raw")
+        embed(y[:], 0, 0, halves[0], weigh=True)
+        nc.vector.tensor_copy(spots(0, 0, HALF), y[:])
+        place_weighted(1, halves[0], "y1_half0")
+        place_weighted(0, halves[1], "y0_half1")
+        place_weighted(1, halves[1], "y1_half1")
         for n in range(2, EARLY - 1):
             place_weighted(n, slice(0, CHUNK), f"y{n}_0")
         h_grouped.append(held([P, CHUNK, PACK], BF16, "h1_unmasked", after=f"y{EARLY - 2}_0"))
@@ -336,7 +342,7 @@ def tile_list_spill_damped_grad_kernel(tc, tab_words, tab_scales, offs, sT, wa, 
             finish_pair(pair, 1, plain, damp[pair, 1])
 
         plain_pair(LOW, after="wo2_raw")
-        damping(1, HIGH, size_after="y0_half0")
+        damping(1, HIGH, size_after="y1_half0")
         squares(1, HIGH)
         plain_pair(HIGH, after="y1_half1")
         signs = held([P, PACK, CHUNK], BF16, "signs", after="size2_1")

@@ -168,6 +168,22 @@ def tile_list_spill_damped_grad_kernel(tc, tab_words, tab_scales, offs, sT, wa, 
                 )
             return acc
 
+        def project_pair(bank, weight, pair, part):
+            acc = psum.tile([P, 2, HALF], F32, name=bank)
+            for i, t in enumerate(pair):
+                for a in range(PASSES):
+                    words, scales = weight[a, t]
+                    nc.tensor.matmul_mx(
+                        out=acc[:, i, :],
+                        lhsT=words.bitcast(E4M3),
+                        lhsT_scale=scales,
+                        rhs=v_w[a][:, part].bitcast(E5M2),
+                        rhs_scale=planes_sc[:, a, part],
+                        start=(a == 0),
+                        stop=(a == PASSES - 1),
+                    )
+            return acc[:].rearrange("p t c -> p c t")
+
         wb_mx = {
             (a, t): (wb_w[:, a, t * P : (t + 1) * P], planes_sc[:, a, S + t * P : S + (t + 1) * P])
             for a in range(PASSES)
@@ -193,6 +209,16 @@ def tile_list_spill_damped_grad_kernel(tc, tab_words, tab_scales, offs, sT, wa, 
             damp[pair, c] = held([P, 2, CHUNK], F32, f"damp{pair[0]}_{c}", after)
             for i in range(2):
                 nc.scalar.activation(damp[pair, c][:, i, :], roots[pair, c][:, i, :], ACT.Square)
+
+        def damping_paired(pair, after=None):
+            size = held([P, CHUNK, 2], F32, f"size{pair[0]}_1", after)
+            damp[pair, 1] = held([P, CHUNK, 2], F32, f"damp{pair[0]}_1")
+            for u, part in enumerate(halves):
+                nc.scalar.activation(size[:, part, :], project_pair(f"b{u}", wb_mx, pair, second_halves[u]), ACT.Abs)
+            for part in halves:
+                nc.scalar.activation(size[:, part, :], size[:, part, :], ACT.Abs_reciprocal_sqrt, bias=1.0)
+            for part in halves:
+                nc.scalar.activation(damp[pair, 1][:, part, :], size[:, part, :], ACT.Square)
 
         def pick_saved(t, c, into=None):
             saved[t, c] = held([P, CHUNK], F32, f"saved{t}_{c}")[:] if into is None else into
@@ -283,6 +309,7 @@ def tile_list_spill_damped_grad_kernel(tc, tab_words, tab_scales, offs, sT, wa, 
             nc.sync.dma_start(out[n * P : (n + 1) * P, :], windows[n % WINDOWS][:])
 
         halves = [slice(u * HALF, (u + 1) * HALF) for u in range(2)]
+        second_halves = [slice(CHUNK + part.start, CHUNK + part.stop) for part in halves]
         quantize_wa(0)
         load_slot(2, after="wa0_grouped")
         quantize_wa(1)
@@ -314,8 +341,7 @@ def tile_list_spill_damped_grad_kernel(tc, tab_words, tab_scales, offs, sT, wa, 
         nc.sync.dma_start(gains[:], wgo)
         load_wo(6, 2, after="masked2_0")
         quantize_wo(0, 2)
-        damping(1, LOW)
-        squares(1, LOW)
+        damping_paired(LOW)
         late = held([P, 2, CHUNK], F32, "late", after="saved3_half0")
         for i, t in enumerate((1, 2)):
             pick_saved(t, 1, late[:, i, :])
@@ -336,14 +362,13 @@ def tile_list_spill_damped_grad_kernel(tc, tab_words, tab_scales, offs, sT, wa, 
         h_grouped.append(held([P, CHUNK, PACK], BF16, "h1_unmasked", after=f"y{EARLY - 2}_0"))
 
         def plain_pair(pair, after):
-            plain = held([P, 2, CHUNK], F32, f"plain{pair[0]}", after)
-            for i, t in enumerate(pair):
-                nc.scalar.copy(plain[:, i, :], project(f"a{t}", wa_mx, 1, t)[:])
-            finish_pair(pair, 1, plain, damp[pair, 1])
+            plain = held([P, CHUNK, 2], F32, f"plain{pair[0]}", after)
+            for u, part in enumerate(halves):
+                nc.scalar.copy(plain[:, part, :], project_pair(f"a{pair[0] + u}", wa_mx, pair, second_halves[u]))
+            nc.gpsimd.tensor_tensor(h_grouped[1][:, :, pair[0] : pair[1] + 1], plain[:], damp[pair, 1][:], ALU.mult)
 
         plain_pair(LOW, after="wo2_raw")
-        damping(1, HIGH, size_after="y1_half0")
-        squares(1, HIGH)
+        damping_paired(HIGH, after="y1_half0")
         plain_pair(HIGH, after="y1_half1")
         signs = held([P, PACK, CHUNK], BF16, "signs", after="size2_1")
         for t in range(PACK):

@@ -38,19 +38,23 @@ def tile_list_spill_damped_grad_kernel(tc, tab_words, tab_scales, offs, sT, wa, 
     nc = tc.nc
     with ExitStack() as ctx:
         keep = ctx.enter_context(tc.tile_pool(name="keep", bufs=1))
+        laid = ctx.enter_context(tc.tile_pool(name="laid", bufs=1))
         ring = ctx.enter_context(tc.tile_pool(name="ring", bufs=Y_TILES))
         psum = ctx.enter_context(tc.psum_pool(name="psum", bufs=1))
 
-        tags = {}
+        tags, spot = {}, {}
 
-        def held(shape, dtype, name, after=None):
+        def held(shape, dtype, name, after=None, at=None):
+            if at is not None or after in spot:
+                spot[name] = spot[after] if at is None else at
+                return laid.tile(shape, dtype, name=name, offset=spot[name], align_bytes=64)
             tags[name] = tags[after] if after else name
             return keep.tile(shape, dtype, name=name, tag=tags[name], align_bytes=64)
 
         picks = keep.tile([P, S // LIST_ROWS], U16, name="picks")
         places = keep.tile([P, S // LIST_ROWS], U16, name="places")
 
-        tab_sc = held([P, T], U8, "tab_sc")
+        tab_sc = held([P, T], U8, "tab_sc", at=2 * CHUNK)
         wb_sc_raw = held([P, H], U8, "wb_sc_raw")
         picked_sc = held([P, S], U8, "picked_sc")
         staged = held([P, S + H], U8, "staged")
@@ -240,22 +244,28 @@ def tile_list_spill_damped_grad_kernel(tc, tab_words, tab_scales, offs, sT, wa, 
                 ALU.mult,
             )
 
-        def finish_slot(t):
+        def finish_slot(t, part=slice(0, CHUNK)):
             pair = LOW if t in LOW else HIGH
             i = t - pair[0]
-            nc.gpsimd.tensor_tensor(h_grouped[0][:, :, t], masked[pair, 0][:, i, :], damp[pair, 0][:, i, :], ALU.mult)
+            nc.gpsimd.tensor_tensor(h_grouped[0][:, part, t], masked[pair, 0][:, i, part], damp[pair, 0][:, i, part], ALU.mult)
 
         wo_mx = {}
 
-        def quantize_wo(first_tile, tiles, after=None, words_after=None):
+        def cast_wo(first_tile, tiles, after=None):
             columns = tiles * P
-            name = f"wo{first_tile}"
-            grouped = held([P, columns, PACK], BF16, f"{name}_grouped", after)
+            grouped = held([P, columns, PACK], BF16, f"wo{first_tile}_grouped", after)
             for first in range(0, columns, WO_PIECE):
                 nc.scalar.copy(
                     grouped[:, first : first + WO_PIECE, :].rearrange("p (c i) j -> p c j i", i=WORDS_A_LINE),
                     wo_raw[first_tile + first // P][:].rearrange("p j (c i) -> p c j i", i=WORDS_A_LINE),
                 )
+            return grouped
+
+        def quantize_wo(first_tile, tiles, after=None, words_after=None):
+            quantize_cast(first_tile, cast_wo(first_tile, tiles, after), tiles, words_after)
+
+        def quantize_cast(first_tile, grouped, tiles, words_after=None):
+            columns, name = tiles * P, f"wo{first_tile}"
             words = held([P, columns], U32, f"{name}_words", words_after)
             scales = held([P, columns], U8, f"{name}_scales")
             nc.vector.quantize_mx(out=words[:].bitcast(E4M3), scales=scales[:], in_=grouped[:].rearrange("p c j -> p (c j)"))
@@ -328,12 +338,14 @@ def tile_list_spill_damped_grad_kernel(tc, tab_words, tab_scales, offs, sT, wa, 
                         nc.vector.tensor_copy(into[:], s_rows[t][:].indirect(picks[:, entries(part.start, HALF)]))
                     for part, picked in zip(halves, parts):
                         nc.vector.scalar_tensor_tensor(masked[pair, 0][:, 1, part], picked[:], 0.0, a_acc[:, part], ALU.is_gt, ALU.mult)
+                    for part in halves:
+                        finish_slot(t, part)
                 else:
                     pick_saved(t, 0)
                     if t == 0:
                         pick_saved(t, 1)
                     masked_product(pair, 0, t, f"a{t}")
-                finish_slot(t)
+                    finish_slot(t)
         load_wo(0, 2, after="saved0_0")
         load_wo(2, 2, after="saved1_0")
         load_wo(4, 2, after="size0_0")
@@ -345,13 +357,14 @@ def tile_list_spill_damped_grad_kernel(tc, tab_words, tab_scales, offs, sT, wa, 
         late = held([P, 2, CHUNK], F32, "late", after="saved3_half0")
         for i, t in enumerate((1, 2)):
             pick_saved(t, 1, late[:, i, :])
-        h_words[0] = held([P, CHUNK], U32, "h0_words", after="wo0_raw")
+        grouped = cast_wo(2, 4)
+        h_words[0] = held([P, CHUNK], U32, "h0_words", at=4 * CHUNK)
         for part in halves:
             quantize_h(0, part)
-        quantize_wo(2, 4)
-        latest = held([P, CHUNK], F32, "latest", after="h0_grouped")
+        quantize_cast(2, grouped, 4)
+        latest = held([P, CHUNK], F32, "latest", at=0)
         pick_saved(3, 1, latest[:])
-        y = held([P, HALF], F32, "y0_half0", after="wo4_raw")
+        y = held([P, HALF], F32, "y0_half0")
         embed(y[:], 0, 0, halves[0], weigh=True)
         nc.vector.tensor_copy(spots(0, 0, HALF), y[:])
         place_weighted(1, halves[0], "y1_half0")
@@ -359,15 +372,15 @@ def tile_list_spill_damped_grad_kernel(tc, tab_words, tab_scales, offs, sT, wa, 
         place_weighted(1, halves[1], "y1_half1")
         for n in range(2, EARLY - 1):
             place_weighted(n, slice(0, CHUNK), f"y{n}_0")
-        h_grouped.append(held([P, CHUNK, PACK], BF16, "h1_unmasked", after=f"y{EARLY - 2}_0"))
+        h_grouped.append(held([P, CHUNK, PACK], BF16, "h1_unmasked", after=f"y{EARLY - 3}_0"))
 
-        def plain_pair(pair, after):
-            plain = held([P, CHUNK, 2], F32, f"plain{pair[0]}", after)
+        def plain_pair(pair, after=None, at=None):
+            plain = held([P, CHUNK, 2], F32, f"plain{pair[0]}", after, at)
             for u, part in enumerate(halves):
                 nc.scalar.copy(plain[:, part, :], project_pair(f"a{pair[0] + u}", wa_mx, pair, second_halves[u]))
             nc.gpsimd.tensor_tensor(h_grouped[1][:, :, pair[0] : pair[1] + 1], plain[:], damp[pair, 1][:], ALU.mult)
 
-        plain_pair(LOW, after="wo2_raw")
+        plain_pair(LOW, at=8 * CHUNK)
         damping_paired(HIGH, after="y1_half0")
         plain_pair(HIGH, after="y1_half1")
         signs = held([P, PACK, CHUNK], BF16, "signs", after="size2_1")

@@ -54,10 +54,10 @@ def tile_list_spill_damped_grad_kernel(tc, tab_words, tab_scales, offs, sT, wa, 
         picks = keep.tile([P, S // LIST_ROWS], U16, name="picks")
         places = keep.tile([P, S // LIST_ROWS], U16, name="places")
 
-        tab_sc = held([P, T], U8, "tab_sc", at=2 * CHUNK)
+        tab_sc = held([P, T], U8, "tab_sc")
         wb_sc_raw = held([P, H], U8, "wb_sc_raw")
         picked_sc = held([P, S], U8, "picked_sc")
-        staged = held([P, S + H], U8, "staged")
+        staged = held([P, S + H], U8, "staged", at=24 * CHUNK)
         planes_sc = held([P, PASSES, S + H], U8, "planes_sc")
         warm = held([P, 8], F32, "warm")
         rest, last = slice(0, P - QUADRANT), slice(P - QUADRANT, P)
@@ -148,29 +148,13 @@ def tile_list_spill_damped_grad_kernel(tc, tab_words, tab_scales, offs, sT, wa, 
 
         wo_raw = {}
 
-        def load_wo(first_tile, tiles, after):
-            wo_raw[first_tile] = held([P, PACK, tiles * P], F32, f"wo{first_tile}_raw", after)
+        def load_wo(first_tile, tiles, after=None, at=None):
+            wo_raw[first_tile] = held([P, PACK, tiles * P], F32, f"wo{first_tile}_raw", after, at)
             nc.sync.dma_start(wo_raw[first_tile][:], wo_by_row[:, :, first_tile * P : (first_tile + tiles) * P])
 
 
         def entries(first, count):
             return slice(first // LIST_ROWS, (first + count) // LIST_ROWS)
-
-        def project(bank, weight, c, t):
-            acc = psum.tile([P, CHUNK], F32, name=bank)
-            cols = slice(c * CHUNK, (c + 1) * CHUNK)
-            for a in range(PASSES):
-                words, scales = weight[a, t]
-                nc.tensor.matmul_mx(
-                    out=acc[:],
-                    lhsT=words.bitcast(E4M3),
-                    lhsT_scale=scales,
-                    rhs=v_w[a][:, cols].bitcast(E5M2),
-                    rhs_scale=planes_sc[:, a, cols],
-                    start=(a == 0),
-                    stop=(a == PASSES - 1),
-                )
-            return acc
 
         def project_pair(bank, weight, pair, part):
             acc = psum.tile([P, 2, HALF], F32, name=bank)
@@ -193,61 +177,32 @@ def tile_list_spill_damped_grad_kernel(tc, tab_words, tab_scales, offs, sT, wa, 
             for a in range(PASSES)
             for t in range(PACK)
         }
-        sizes, roots, damp, saved, masked = {}, {}, {}, {}, {}
+        damp, saved = {}, {}
 
-        def damping(c, pair, size_after=None, root_after=None, later=False):
-            size = held([P, 2, CHUNK], F32, f"size{pair[0]}_{c}", size_after)
-            for i, t in enumerate(pair):
-                nc.scalar.activation(size[:, i, :], project(f"b{i}", wb_mx, c, t)[:], ACT.Abs)
-            sizes[pair, c] = size
-            if not later:
-                take_roots(c, pair, root_after)
+        def within(c, part):
+            return slice(c * CHUNK + part.start, c * CHUNK + part.stop)
 
-        def take_roots(c, pair, after):
-            size = sizes[pair, c]
-            roots[pair, c] = held([P, 2, CHUNK], F32, f"root{pair[0]}_{c}", after) if after else size
-            for i in range(2):
-                nc.scalar.activation(roots[pair, c][:, i, :], size[:, i, :], ACT.Abs_reciprocal_sqrt, bias=1.0)
-
-        def squares(c, pair, after=None):
-            damp[pair, c] = held([P, 2, CHUNK], F32, f"damp{pair[0]}_{c}", after)
-            for i in range(2):
-                nc.scalar.activation(damp[pair, c][:, i, :], roots[pair, c][:, i, :], ACT.Square)
-
-        def damping_paired(pair, after=None):
-            size = held([P, CHUNK, 2], F32, f"size{pair[0]}_1", after)
-            damp[pair, 1] = held([P, CHUNK, 2], F32, f"damp{pair[0]}_1")
+        def damping(c, pair, size, banks="b"):
+            damp[pair, c] = held([P, CHUNK, 2], F32, f"damp{pair[0]}_{c}")
             for u, part in enumerate(halves):
-                nc.scalar.activation(size[:, part, :], project_pair(f"b{u}", wb_mx, pair, second_halves[u]), ACT.Abs)
+                nc.scalar.activation(size[:, part, :], project_pair(f"{banks}{u}", wb_mx, pair, within(c, part)), ACT.Abs)
             for part in halves:
                 nc.scalar.activation(size[:, part, :], size[:, part, :], ACT.Abs_reciprocal_sqrt, bias=1.0)
             for part in halves:
-                nc.scalar.activation(damp[pair, 1][:, part, :], size[:, part, :], ACT.Square)
+                nc.scalar.activation(damp[pair, c][:, part, :], size[:, part, :], ACT.Square)
 
-        def pick_saved(t, c, into=None):
-            saved[t, c] = held([P, CHUNK], F32, f"saved{t}_{c}")[:] if into is None else into
-            nc.vector.tensor_copy(saved[t, c], s_rows[t][:].indirect(picks[:, entries(c * CHUNK, CHUNK)]))
+        def pick_saved(into, t, part):
+            nc.vector.tensor_copy(into, s_rows[t][:].indirect(picks[:, entries(part.start, part.stop - part.start)]))
 
-        def masked_product(pair, c, t, bank, after=None):
-            if (pair, c) not in masked:
-                masked[pair, c] = held([P, 2, CHUNK], F32, f"masked{t}_{c}", after)
-            a_acc = project(bank, wa_mx, c, t)
-            nc.vector.scalar_tensor_tensor(masked[pair, c][:, t - pair[0], :], saved[t, c], 0.0, a_acc[:], ALU.is_gt, ALU.mult)
+        def finish_pair(pair, picked):
+            masked = held([P, CHUNK, 2], F32, f"masked{pair[0]}")
+            for u, part in enumerate(halves):
+                a_acc = project_pair(f"a{pair[0] + u}", wa_mx, pair, part)
+                nc.vector.scalar_tensor_tensor(masked[:, part, :], picked[u].rearrange("p t c -> p c t"), 0.0, a_acc, ALU.is_gt, ALU.mult)
+            for part in halves:
+                nc.gpsimd.tensor_tensor(h_grouped[0][:, part, pair[0] : pair[1] + 1], masked[:, part, :], damp[pair, 0][:, part, :], ALU.mult)
 
         h_grouped = [held([P, CHUNK, PACK], BF16, "h0_grouped")]
-
-        def finish_pair(pair, c, left, right, part=slice(0, CHUNK)):
-            nc.gpsimd.tensor_tensor(
-                h_grouped[c][:, part, pair[0] : pair[1] + 1].rearrange("p (c i) t -> p c t i", i=WORDS_A_LINE),
-                left[:, :, part].rearrange("p t (c i) -> p c t i", i=WORDS_A_LINE),
-                right[:, :, part].rearrange("p t (c i) -> p c t i", i=WORDS_A_LINE),
-                ALU.mult,
-            )
-
-        def finish_slot(t, part=slice(0, CHUNK)):
-            pair = LOW if t in LOW else HIGH
-            i = t - pair[0]
-            nc.gpsimd.tensor_tensor(h_grouped[0][:, part, t], masked[pair, 0][:, i, part], damp[pair, 0][:, i, part], ALU.mult)
 
         wo_mx = {}
 
@@ -319,51 +274,44 @@ def tile_list_spill_damped_grad_kernel(tc, tab_words, tab_scales, offs, sT, wa, 
             nc.sync.dma_start(out[n * P : (n + 1) * P, :], windows[n % WINDOWS][:])
 
         halves = [slice(u * HALF, (u + 1) * HALF) for u in range(2)]
-        second_halves = [slice(CHUNK + part.start, CHUNK + part.stop) for part in halves]
+        second = slice(CHUNK, S)
         quantize_wa(0)
         load_slot(2, after="wa0_grouped")
         quantize_wa(1)
         load_slot(3, after="wa_raw1")
         open_window(after="wa1_grouped")
-        damping(0, LOW, size_after="wa_raw0")
-        squares(0, LOW)
-        damping(0, HIGH)
-        squares(0, HIGH)
-        for pair in (LOW, HIGH):
-            for t in pair:
-                if t == PACK - 1:
-                    a_acc = project(f"a{t}", wa_mx, 0, t)
-                    parts = [held([P, HALF], F32, f"saved3_half{u}") for u in range(2)]
-                    for part, into in zip(halves, parts):
-                        nc.vector.tensor_copy(into[:], s_rows[t][:].indirect(picks[:, entries(part.start, HALF)]))
-                    for part, picked in zip(halves, parts):
-                        nc.vector.scalar_tensor_tensor(masked[pair, 0][:, 1, part], picked[:], 0.0, a_acc[:, part], ALU.is_gt, ALU.mult)
-                    for part in halves:
-                        finish_slot(t, part)
-                else:
-                    pick_saved(t, 0)
-                    if t == 0:
-                        pick_saved(t, 1)
-                    masked_product(pair, 0, t, f"a{t}")
-                    finish_slot(t)
-        load_wo(0, 2, after="saved0_0")
-        load_wo(2, 2, after="saved1_0")
-        load_wo(4, 2, after="size0_0")
-        gains = held([P, S], F32, "gains", after="saved2_0")
+        sizes = held([P, 2, CHUNK, 2], F32, "sizes", after="wa_raw0")
+        damping(0, LOW, sizes[:, 0])
+        damping(0, HIGH, sizes[:, 1], banks="y")
+        low = held([P, 2, CHUNK], F32, "saved_low", at=2 * CHUNK)
+        for t in LOW:
+            pick_saved(low[:, t, :], t, slice(0, CHUNK))
+            saved[t] = held([P, CHUNK], F32, f"saved{t}")[:]
+            pick_saved(saved[t], t, second)
+        finish_pair(LOW, [low[:, :, part] for part in halves])
+        high = [held([P, 2, HALF], F32, f"saved_high{u}") for u in range(2)]
+        for i, t in enumerate(HIGH):
+            for u, part in enumerate(halves):
+                pick_saved(high[u][:, i, :], t, part)
+        finish_pair(HIGH, [picked[:] for picked in high])
+        load_wo(0, 2, after="s_rows0")
+        load_wo(2, 2, at=32 * CHUNK)
+        load_wo(4, 2, after="saved_low")
+        gains = held([P, S], F32, "gains", after="masked0")
         nc.sync.dma_start(gains[:], wgo)
-        load_wo(6, 2, after="masked2_0")
+        load_wo(6, 2, after="masked2")
         quantize_wo(0, 2)
-        damping_paired(LOW)
-        late = held([P, 2, CHUNK], F32, "late", after="saved3_half0")
-        for i, t in enumerate((1, 2)):
-            pick_saved(t, 1, late[:, i, :])
+        damping(1, LOW, held([P, CHUNK, 2], F32, "size0_1"))
+        late = held([P, CHUNK + HALF], F32, "late", after="saved_high0")
+        pick_saved(late[:, :CHUNK], 2, second)
+        pick_saved(late[:, CHUNK:], 3, within(1, halves[0]))
         grouped = cast_wo(2, 4)
         h_words[0] = held([P, CHUNK], U32, "h0_words", at=4 * CHUNK)
         for part in halves:
             quantize_h(0, part)
         quantize_cast(2, grouped, 4)
-        latest = held([P, CHUNK], F32, "latest", at=0)
-        pick_saved(3, 1, latest[:])
+        latest = held([P, HALF], F32, "latest", at=2 * CHUNK)
+        pick_saved(latest[:], 3, within(1, halves[1]))
         y = held([P, HALF], F32, "y0_half0")
         embed(y[:], 0, 0, halves[0], weigh=True)
         nc.vector.tensor_copy(spots(0, 0, HALF), y[:])
@@ -377,15 +325,18 @@ def tile_list_spill_damped_grad_kernel(tc, tab_words, tab_scales, offs, sT, wa, 
         def plain_pair(pair, after=None, at=None):
             plain = held([P, CHUNK, 2], F32, f"plain{pair[0]}", after, at)
             for u, part in enumerate(halves):
-                nc.scalar.copy(plain[:, part, :], project_pair(f"a{pair[0] + u}", wa_mx, pair, second_halves[u]))
+                nc.scalar.copy(plain[:, part, :], project_pair(f"a{pair[0] + u}", wa_mx, pair, within(1, part)))
             nc.gpsimd.tensor_tensor(h_grouped[1][:, :, pair[0] : pair[1] + 1], plain[:], damp[pair, 1][:], ALU.mult)
 
         plain_pair(LOW, at=8 * CHUNK)
-        damping_paired(HIGH, after="y1_half0")
+        damping(1, HIGH, held([P, CHUNK, 2], F32, "size2_1", after="y1_half0"))
         plain_pair(HIGH, after="y1_half1")
         signs = held([P, PACK, CHUNK], BF16, "signs", after="size2_1")
-        for t in range(PACK):
-            nc.scalar.activation(signs[:, t, :], saved[t, 1], ACT.Sign)
+        for t in LOW:
+            nc.scalar.activation(signs[:, t, :], saved[t], ACT.Sign)
+        high_signs = signs[:, 2:, :].rearrange("p t c -> p (t c)")
+        nc.scalar.activation(high_signs[:, : CHUNK + HALF], late[:], ACT.Sign)
+        nc.scalar.activation(high_signs[:, CHUNK + HALF :], latest[:], ACT.Sign)
         mask = held([P, CHUNK, PACK], BF16, "mask")
         nc.scalar.activation(
             mask[:].rearrange("p (c i) j -> p c j i", i=WORDS_A_LINE),

@@ -27,8 +27,8 @@ QUADRANT = 32
 SCALE_ROWS = 4
 LINE = 16
 WORDS_A_LINE = LINE // 4
-EARLY = 5
-WINDOWS = 5
+EARLY = 6
+WINDOWS = 6
 WO_PIECE = 256
 Y_TILES = 3
 LOW, HIGH = (0, 1), (2, 3)
@@ -134,12 +134,8 @@ def tile_list_spill_damped_grad_kernel(tc, tab_words, tab_scales, offs, sT, wa, 
             grouped = held([P, H * PACK], BF16, f"wa{a}_grouped")
             into = grouped[:].rearrange("p (t m j) -> p m j t", t=PACK, j=PACK)
             rows = wa_raw[a][:].rearrange("p j (m t) -> p m j t", t=PACK)
-            if a == 1:
-                nc.vector.tensor_copy(into[:, :, :, 0:2], rows[:, :, :, 0:2])
-                nc.vector.tensor_copy(into[:, :, :, 2:4], rows[:, :, :, 2:4])
-            else:
-                nc.vector.tensor_copy(into[:, :, :, 0:2], rows[:, :, :, 0:2])
-                nc.scalar.copy(into[:, :, :, 2:4], rows[:, :, :, 2:4])
+            nc.vector.tensor_copy(into[:, :, :, 0:2], rows[:, :, :, 0:2])
+            nc.scalar.copy(into[:, :, :, 2:4], rows[:, :, :, 2:4])
             words = held([P, H], U32, f"wa{a}_words")
             scales = held([P, H], U8, f"wa{a}_scales")
             nc.vector.quantize_mx(out=words[:].bitcast(E4M3), scales=scales[:], in_=grouped[:])
@@ -182,8 +178,8 @@ def tile_list_spill_damped_grad_kernel(tc, tab_words, tab_scales, offs, sT, wa, 
         def within(c, part):
             return slice(c * CHUNK + part.start, c * CHUNK + part.stop)
 
-        def damping(c, pair, size, banks="b"):
-            damp[pair, c] = held([P, CHUNK, 2], F32, f"damp{pair[0]}_{c}")
+        def damping(c, pair, size, banks="b", at=None):
+            damp[pair, c] = held([P, CHUNK, 2], F32, f"damp{pair[0]}_{c}", at=at)
             for u, part in enumerate(halves):
                 nc.scalar.activation(size[:, part, :], project_pair(f"{banks}{u}", wb_mx, pair, within(c, part)), ACT.Abs)
             for part in halves:
@@ -276,14 +272,14 @@ def tile_list_spill_damped_grad_kernel(tc, tab_words, tab_scales, offs, sT, wa, 
         halves = [slice(u * HALF, (u + 1) * HALF) for u in range(2)]
         second = slice(CHUNK, S)
         quantize_wa(0)
-        load_slot(2, after="wa0_grouped")
+        load_slot(2, after="wa_raw0")
         quantize_wa(1)
-        load_slot(3, after="wa_raw1")
+        load_slot(3, after="wa0_grouped")
         open_window(after="wa1_grouped")
-        sizes = held([P, 2, CHUNK, 2], F32, "sizes", after="wa_raw0")
+        sizes = held([P, 2, CHUNK, 2], F32, "sizes", after="wa_raw1")
         damping(0, LOW, sizes[:, 0])
         damping(0, HIGH, sizes[:, 1], banks="y")
-        low = held([P, 2, CHUNK], F32, "saved_low", at=2 * CHUNK)
+        low = held([P, 2, CHUNK], F32, "saved_low", at=8 * CHUNK)
         for t in LOW:
             pick_saved(low[:, t, :], t, slice(0, CHUNK))
             saved[t] = held([P, CHUNK], F32, f"saved{t}")[:]
@@ -301,16 +297,15 @@ def tile_list_spill_damped_grad_kernel(tc, tab_words, tab_scales, offs, sT, wa, 
         nc.sync.dma_start(gains[:], wgo)
         load_wo(6, 2, after="masked2")
         quantize_wo(0, 2)
-        damping(1, LOW, held([P, CHUNK, 2], F32, "size0_1"))
         late = held([P, CHUNK + HALF], F32, "late", after="saved_high0")
         pick_saved(late[:, :CHUNK], 2, second)
         pick_saved(late[:, CHUNK:], 3, within(1, halves[0]))
         grouped = cast_wo(2, 4)
-        h_words[0] = held([P, CHUNK], U32, "h0_words", at=4 * CHUNK)
+        h_words[0] = held([P, CHUNK], U32, "h0_words", at=11 * CHUNK)
         for part in halves:
             quantize_h(0, part)
         quantize_cast(2, grouped, 4)
-        latest = held([P, HALF], F32, "latest", at=2 * CHUNK)
+        latest = held([P, HALF], F32, "latest", at=9 * CHUNK)
         pick_saved(latest[:], 3, within(1, halves[1]))
         y = held([P, HALF], F32, "y0_half0")
         embed(y[:], 0, 0, halves[0], weigh=True)
@@ -328,9 +323,11 @@ def tile_list_spill_damped_grad_kernel(tc, tab_words, tab_scales, offs, sT, wa, 
                 nc.scalar.copy(plain[:, part, :], project_pair(f"a{pair[0] + u}", wa_mx, pair, within(1, part)))
             nc.gpsimd.tensor_tensor(h_grouped[1][:, :, pair[0] : pair[1] + 1], plain[:], damp[pair, 1][:], ALU.mult)
 
-        plain_pair(LOW, at=8 * CHUNK)
+        damping(1, LOW, held([P, CHUNK, 2], F32, "size0_1", at=CHUNK))
+        plain_pair(LOW, at=15 * CHUNK)
         damping(1, HIGH, held([P, CHUNK, 2], F32, "size2_1", after="y1_half0"))
         plain_pair(HIGH, after="y1_half1")
+        open_window(after="plain2")
         signs = held([P, PACK, CHUNK], BF16, "signs", after="size2_1")
         for t in LOW:
             nc.scalar.activation(signs[:, t, :], saved[t], ACT.Sign)

@@ -178,13 +178,13 @@ def tile_list_spill_damped_grad_kernel(tc, tab_words, tab_scales, offs, sT, wa, 
         def within(c, part):
             return slice(c * CHUNK + part.start, c * CHUNK + part.stop)
 
-        def damping(c, pair, size, banks="b", at=None):
-            damp[pair, c] = held([P, CHUNK, 2], F32, f"damp{pair[0]}_{c}", at=at)
+        def damping(c, pair, size, banks="b", parts=None):
+            damp[pair, c] = held([P, CHUNK, 2], F32, f"damp{pair[0]}_{c}")
             for u, part in enumerate(halves):
                 nc.scalar.activation(size[:, part, :], project_pair(f"{banks}{u}", wb_mx, pair, within(c, part)), ACT.Abs)
-            for part in halves:
+            for part in parts or halves:
                 nc.scalar.activation(size[:, part, :], size[:, part, :], ACT.Abs_reciprocal_sqrt, bias=1.0)
-            for part in halves:
+            for part in parts or halves:
                 nc.scalar.activation(damp[pair, c][:, part, :], size[:, part, :], ACT.Square)
 
         def pick_saved(into, t, part):
@@ -277,8 +277,8 @@ def tile_list_spill_damped_grad_kernel(tc, tab_words, tab_scales, offs, sT, wa, 
         load_slot(3, after="wa0_grouped")
         open_window(after="wa1_grouped")
         sizes = held([P, 2, CHUNK, 2], F32, "sizes", after="wa_raw1")
-        damping(0, LOW, sizes[:, 0])
-        damping(0, HIGH, sizes[:, 1], banks="y")
+        damping(0, LOW, sizes[:, 0], parts=[slice(0, CHUNK)])
+        damping(0, HIGH, sizes[:, 1], banks="y", parts=[slice(0, CHUNK)])
         low = held([P, 2, CHUNK], F32, "saved_low", at=8 * CHUNK)
         for t in LOW:
             pick_saved(low[:, t, :], t, slice(0, CHUNK))
@@ -327,25 +327,25 @@ def tile_list_spill_damped_grad_kernel(tc, tab_words, tab_scales, offs, sT, wa, 
         plain_pair(LOW, at=15 * CHUNK)
         damping(1, HIGH, held([P, CHUNK, 2], F32, "size2_1", after="y1_half0"))
         plain_pair(HIGH, after="y1_half1")
-        open_window(after="plain2")
+        open_window(after="plain0")
         signs = held([P, PACK, CHUNK], BF16, "signs", after="size2_1")
         for t in LOW:
             nc.scalar.activation(signs[:, t, :], saved[t], ACT.Sign)
         high_signs = signs[:, 2:, :].rearrange("p t c -> p (t c)")
         nc.scalar.activation(high_signs[:, : CHUNK + HALF], late[:], ACT.Sign)
         nc.scalar.activation(high_signs[:, CHUNK + HALF :], latest[:], ACT.Sign)
-        mask = held([P, CHUNK, PACK], BF16, "mask")
-        nc.scalar.activation(
-            mask[:].rearrange("p (c i) j -> p c j i", i=WORDS_A_LINE),
-            signs[:].rearrange("p j (c i) -> p c j i", i=WORDS_A_LINE),
-            ACT.Relu,
-        )
         h_grouped.append(held([P, CHUNK, PACK], BF16, "h1_grouped"))
-        for part in halves:
-            nc.vector.tensor_tensor(h_grouped[2][:, part, :], h_grouped[1][:, part, :], mask[:, part, :], ALU.mult)
+        for u, (part, engine) in enumerate(zip(halves, (nc.gpsimd, nc.vector))):
+            mask = held([P, HALF, PACK], BF16, f"mask{u}")
+            nc.scalar.activation(
+                mask[:].rearrange("p (c i) j -> p c j i", i=WORDS_A_LINE),
+                signs[:, :, part].rearrange("p j (c i) -> p c j i", i=WORDS_A_LINE),
+                ACT.Relu,
+            )
+            engine.tensor_tensor(h_grouped[2][:, part, :], h_grouped[1][:, part, :], mask[:], ALU.mult)
         for part in halves:
             quantize_h(1, part)
-        y = held([P, CHUNK], F32, "y_between", after="signs")
+        y = held([P, CHUNK], F32, "y_between", after="mask0")
         embed(y[:], EARLY - 1, 0)
         place(y[:], EARLY - 1, 0, CHUNK)
         for n in range(EARLY):
@@ -354,7 +354,7 @@ def tile_list_spill_damped_grad_kernel(tc, tab_words, tab_scales, offs, sT, wa, 
             place(y[:], n, CHUNK, CHUNK)
             store(n)
             if n == 0:
-                quantize_wo(6, 2, after="mask", words_after="y_between")
+                quantize_wo(6, 2, after="mask1", words_after="y_between")
         for n in range(EARLY, N // P):
             y = ring.tile([P, S], F32, name="y")
             for c in range(CHUNKS):

@@ -116,10 +116,10 @@ def tile_list_spill_damped_grad_kernel(tc, tab_words, tab_scales, offs, sT, wa, 
         v_w = [held([P, S], U32, f"v_w{a}") for a in range(PASSES)]
         for a in range(PASSES):
             nc.vector.tensor_copy(v_w[a][:], tab_w[a][:].bitcast(U32).indirect(picks[:]))
-        wb_w = held([P, PASSES, H], I32, "wb_w")
-        nc.vector.tensor_copy(
+        wb_w = held([P, PASSES, H], U32, "wb_w")
+        nc.scalar.copy(
             wb_w[:].rearrange("p a (t m i) -> p a m t i", t=PACK, i=WORDS_A_LINE),
-            wb_w_raw[:].rearrange("p a (m i t) -> p a m t i", t=PACK, i=WORDS_A_LINE),
+            wb_w_raw[:].bitcast(U32).rearrange("p a (m i t) -> p a m t i", t=PACK, i=WORDS_A_LINE),
         )
 
         wa_raw.append(held([P, PACK, H], F32, "wa_raw1", after="tab_w0"))

from contextlib import ExitStack

import concourse.mybir as mybir

K, H, N, T, S, T2 = 1024, 512, 1024, 2048, 1024, 2048
FLOPS = 2 * (2 * K * H * S + H * N * S)

F32 = mybir.dt.float32
BF16 = mybir.dt.bfloat16
I32 = mybir.dt.int32
U32 = mybir.dt.uint32
U16 = mybir.dt.uint16
U8 = mybir.dt.uint8
E4M3 = mybir.dt.float8_e4m3fn_x4
E5M2 = mybir.dt.float8_e5m2_x4
ACT = mybir.ActivationFunctionType
ALU = mybir.AluOpType

P = 128
PACK = 4
PASSES = K // (P * PACK)
CHUNK = 512
CHUNKS = S // CHUNK
HALF = CHUNK // 2
LIST_ROWS = 16
QUADRANT = 32
SCALE_ROWS = 4
LINE = 16
WORDS_A_LINE = LINE // 4
EARLY = 6
WINDOWS = 6
WO_PIECE = 256
Y_TILES = 3
LOW, HIGH = (0, 1), (2, 3)


def tile_list_spill_damped_grad_kernel(tc, tab_words, tab_scales, offs, sT, wa, wb_words, wb_scales, wo, wgo, offs2, out):
    nc = tc.nc
    with ExitStack() as ctx:
        keep = ctx.enter_context(tc.tile_pool(name="keep", bufs=1))
        laid = ctx.enter_context(tc.tile_pool(name="laid", bufs=1))
        ring = ctx.enter_context(tc.tile_pool(name="ring", bufs=Y_TILES))
        psum = ctx.enter_context(tc.psum_pool(name="psum", bufs=1))

        tags, spot = {}, {}

        def held(shape, dtype, name, after=None, at=None):
            if at is not None or after in spot:
                spot[name] = spot[after] if at is None else at
                return laid.tile(shape, dtype, name=name, offset=spot[name], align_bytes=64)
            tags[name] = tags[after] if after else name
            return keep.tile(shape, dtype, name=name, tag=tags[name], align_bytes=64)

        picks = keep.tile([P, S // LIST_ROWS], U16, name="picks")
        places = keep.tile([P, S // LIST_ROWS], U16, name="places")

        tab_sc = held([P, T], U8, "tab_sc")
        wb_sc_raw = held([P, H], U8, "wb_sc_raw")
        picked_sc = held([P, S], U8, "picked_sc")
        staged = held([P, S + H], U8, "staged", at=24 * CHUNK)
        planes_sc = held([P, PASSES, S + H], U8, "planes_sc")
        warm = held([P, 8], F32, "warm")
        rest, last = slice(0, P - QUADRANT), slice(P - QUADRANT, P)

        nc.gpsimd.memset(tab_sc[rest, :].bitcast(I32), 0)
        nc.gpsimd.memset(wb_sc_raw[rest, :].bitcast(I32), 0)
        nc.gpsimd.memset(planes_sc[:].rearrange("p a c -> p (a c)").bitcast(I32), 0)

        nc.vector.memset(warm[:], 0.0)
        nc.scalar.activation(warm[:], warm[:], ACT.Abs_reciprocal_sqrt, bias=1.0)

        tab_w = [held([P, T], I32, f"tab_w{a}") for a in range(PASSES)]
        wb_w_raw = held([P, PASSES, H], I32, "wb_w_raw")
        s_by_slot = sT.rearrange("(p t) c -> t p c", t=PACK)
        wa_by_pass = wa.rearrange("(a p j) c -> a p j c", a=PASSES, j=PACK)
        wo_by_row = wo.rearrange("(p j) c -> p j c", j=PACK)

        nc.sync.dma_start(picks[:], offs)
        nc.sync.dma_start(tab_sc[last, :].bitcast(I32), tab_scales.rearrange("a q c -> q a c").bitcast(I32))
        nc.sync.dma_start(wb_sc_raw[last, :].bitcast(I32), wb_scales.rearrange("a q c -> q a c").bitcast(I32))
        nc.sync.dma_start(tab_w[0][:], tab_words[0].rearrange("p c i -> p (c i)").bitcast(I32))
        nc.sync.dma_start(wb_w_raw[:], wb_words.rearrange("a p c i -> p a (c i)").bitcast(I32))
        nc.sync.dma_start(tab_w[1][:], tab_words[1].rearrange("p c i -> p (c i)").bitcast(I32))
        nc.sync.dma_start(places[:], offs2)

        windows = []

        def open_window(after=None):
            window = held([P, T2], F32, f"window{len(windows)}", after)
            nc.gpsimd.memset(window[:].bitcast(I32), 0)
            windows.append(window)

        open_window()
        open_window()
        nc.vector.tensor_copy(picked_sc[:], tab_sc[:].indirect(picks[:]))
        nc.vector.tensor_copy(
            staged[:, S:].rearrange("p (t m i) -> p m t i", t=PACK, i=LINE),
            wb_sc_raw[:].rearrange("p (m i t) -> p m t i", t=PACK, i=LINE),
        )
        nc.vector.tensor_copy(staged[last, 0:S].bitcast(I32), picked_sc[last, :].bitcast(I32))
        for q in range(P // QUADRANT):
            first = last.start + q * SCALE_ROWS * PASSES
            nc.scalar.dma_start(
                planes_sc[QUADRANT * q : QUADRANT * q + SCALE_ROWS, :, :].bitcast(I32),
                staged[first : first + SCALE_ROWS * PASSES, :].bitcast(I32),
            )
        open_window(after="picked_sc")
        s_rows = []

        def load_slot(t, after):
            s_rows.append(held([P, T], F32, f"s_rows{t}", after))
            nc.sync.dma_start(s_rows[t][:], s_by_slot[t])

        wa_raw = [held([P, PACK, H], F32, "wa_raw0", after="tab_sc")]
        nc.sync.dma_start(wa_raw[0][:], wa_by_pass[0])
        v_w = [held([P, S], U32, f"v_w{a}") for a in range(PASSES)]
        for a in range(PASSES):
            nc.vector.tensor_copy(v_w[a][:], tab_w[a][:].bitcast(U32).indirect(picks[:]))
        wb_w = held([P, PASSES, H], U32, "wb_w")
        nc.scalar.copy(
            wb_w[:].rearrange("p a (t m i) -> p a m t i", t=PACK, i=WORDS_A_LINE),
            wb_w_raw[:].bitcast(U32).rearrange("p a (m i t) -> p a m t i", t=PACK, i=WORDS_A_LINE),
        )

        wa_raw.append(held([P, PACK, H], F32, "wa_raw1", after="tab_w0"))
        nc.sync.dma_start(wa_raw[1][:], wa_by_pass[1])
        load_slot(0, after="staged")
        load_slot(1, after="tab_w1")
        open_window(after="wb_w_raw")

        wa_mx = {}

        def quantize_wa(a):
            grouped = held([P, H * PACK], BF16, f"wa{a}_grouped")
            into = grouped[:].rearrange("p (t m j) -> p m j t", t=PACK, j=PACK)
            rows = wa_raw[a][:].rearrange("p j (m t) -> p m j t", t=PACK)
            nc.vector.tensor_copy(into[:, :, :, 0:2], rows[:, :, :, 0:2])
            nc.scalar.copy(into[:, :, :, 2:4], rows[:, :, :, 2:4])
            words = held([P, H], U32, f"wa{a}_words")
            scales = held([P, H], U8, f"wa{a}_scales")
            nc.vector.quantize_mx(out=words[:].bitcast(E4M3), scales=scales[:], in_=grouped[:])
            for t in range(PACK):
                wa_mx[a, t] = words[:, t * P : (t + 1) * P], scales[:, t * P : (t + 1) * P]

        wo_raw = {}

        def load_wo(first_tile, tiles, after=None, at=None):
            wo_raw[first_tile] = held([P, PACK, tiles * P], F32, f"wo{first_tile}_raw", after, at)
            nc.sync.dma_start(wo_raw[first_tile][:], wo_by_row[:, :, first_tile * P : (first_tile + tiles) * P])


        def entries(first, count):
            return slice(first // LIST_ROWS, (first + count) // LIST_ROWS)

        def project_pair(bank, weight, pair, part):
            acc = psum.tile([P, 2, HALF], F32, name=bank)
            for i, t in enumerate(pair):
                for a in range(PASSES):
                    words, scales = weight[a, t]
                    nc.tensor.matmul_mx(
                        out=acc[:, i, :],
                        lhsT=words.bitcast(E4M3),
                        lhsT_scale=scales,
                        rhs=v_w[a][:, part].bitcast(E5M2),
                        rhs_scale=planes_sc[:, a, part],
                        start=(a == 0),
                        stop=(a == PASSES - 1),
                    )
            return acc[:].rearrange("p t c -> p c t")

        wb_mx = {
            (a, t): (wb_w[:, a, t * P : (t + 1) * P], planes_sc[:, a, S + t * P : S + (t + 1) * P])
            for a in range(PASSES)
            for t in range(PACK)
        }
        damp, saved = {}, {}

        def within(c, part):
            return slice(c * CHUNK + part.start, c * CHUNK + part.stop)

        def damping(c, pair, size, banks="b", parts=None):
            damp[pair, c] = held([P, CHUNK, 2], F32, f"damp{pair[0]}_{c}")
            for u, part in enumerate(halves):
                nc.scalar.activation(size[:, part, :], project_pair(f"{banks}{u}", wb_mx, pair, within(c, part)), ACT.Abs)
            for part in parts or halves:
                nc.scalar.activation(size[:, part, :], size[:, part, :], ACT.Abs_reciprocal_sqrt, bias=1.0)
            for part in parts or halves:
                nc.scalar.activation(damp[pair, c][:, part, :], size[:, part, :], ACT.Square)

        def pick_saved(into, t, part):
            nc.vector.tensor_copy(into, s_rows[t][:].indirect(picks[:, entries(part.start, part.stop - part.start)]))

        def finish_pair(pair, picked):
            masked = held([P, CHUNK, 2], F32, f"masked{pair[0]}")
            for u, part in enumerate(halves):
                a_acc = project_pair(f"a{pair[0] + u}", wa_mx, pair, part)
                nc.vector.scalar_tensor_tensor(masked[:, part, :], picked[u].rearrange("p t c -> p c t"), 0.0, a_acc, ALU.is_gt, ALU.mult)
            for part in halves:
                nc.gpsimd.tensor_tensor(h_grouped[0][:, part, pair[0] : pair[1] + 1], masked[:, part, :], damp[pair, 0][:, part, :], ALU.mult)

        h_grouped = [held([P, CHUNK, PACK], BF16, "h0_grouped")]

        wo_mx = {}

        def cast_wo(first_tile, tiles, after=None):
            columns = tiles * P
            grouped = held([P, columns, PACK], BF16, f"wo{first_tile}_grouped", after)
            for first in range(0, columns, WO_PIECE):
                nc.scalar.copy(
                    grouped[:, first : first + WO_PIECE, :].rearrange("p (c i) j -> p c j i", i=WORDS_A_LINE),
                    wo_raw[first_tile + first // P][:].rearrange("p j (c i) -> p c j i", i=WORDS_A_LINE),
                )
            return grouped

        def quantize_wo(first_tile, tiles, after=None, words_after=None):
            quantize_cast(first_tile, cast_wo(first_tile, tiles, after), tiles, words_after)

        def quantize_cast(first_tile, grouped, tiles, words_after=None):
            columns, name = tiles * P, f"wo{first_tile}"
            words = held([P, columns], U32, f"{name}_words", words_after)
            scales = held([P, columns], U8, f"{name}_scales")
            nc.vector.quantize_mx(out=words[:].bitcast(E4M3), scales=scales[:], in_=grouped[:].rearrange("p c j -> p (c j)"))
            for i in range(columns // P):
                wo_mx[first_tile + i] = words[:, i * P : (i + 1) * P], scales[:, i * P : (i + 1) * P]

        h_words = {1: held([P, CHUNK], U32, "h1_words")}
        h_scales = [held([P, CHUNK], U8, f"h{c}_scales") for c in range(CHUNKS)]

        def quantize_h(c, part):
            nc.vector.quantize_mx(
                out=h_words[c][:, part].bitcast(E4M3),
                scales=h_scales[c][:, part],
                in_=h_grouped[2 * c][:, part, :].rearrange("p c j -> p (c j)"),
            )

        filled = []

        def embed(y, n, c, part=slice(0, CHUNK), weigh=False):
            y_acc = psum.tile([P, CHUNK], F32, name=f"y{len(filled) % 2}")
            filled.append(n)
            nc.tensor.matmul_mx(
                out=y_acc[:, part],
                lhsT=wo_mx[n][0].bitcast(E4M3),
                lhsT_scale=wo_mx[n][1],
                rhs=h_words[c][:, part].bitcast(E4M3),
                rhs_scale=h_scales[c][:, part],
                start=True,
                stop=True,
            )
            if weigh:
                nc.vector.tensor_tensor(y, y_acc[:, part], gains[:, part], ALU.mult)
            else:
                nc.scalar.copy(y, y_acc[:, part])

        def spots(n, first, count):
            return windows[n % WINDOWS][:].indirect(places[:, entries(first, count)])

        def place(y, n, first, count):
            nc.vector.tensor_tensor(spots(n, first, count), y, gains[:, first : first + count], ALU.mult)

        def place_weighted(n, part, name, after=None):
            count = part.stop - part.start
            y = held([P, count], F32, name, after)
            embed(y[:], n, 0, part)
            weighted = held([P, count], F32, f"{name}_weighted")
            nc.gpsimd.tensor_tensor(weighted[:], y[:], gains[:, part], ALU.mult)
            nc.vector.tensor_copy(spots(n, part.start, count), weighted[:])

        def store(n):
            nc.sync.dma_start(out[n * P : (n + 1) * P, :], windows[n % WINDOWS][:])

        halves = [slice(u * HALF, (u + 1) * HALF) for u in range(2)]
        second = slice(CHUNK, S)
        quantize_wa(0)
        load_slot(2, after="wa_raw0")
        quantize_wa(1)
        load_slot(3, after="wa0_grouped")
        open_window(after="wa1_grouped")
        sizes = held([P, 2, CHUNK, 2], F32, "sizes", after="wa_raw1")
        damping(0, LOW, sizes[:, 0], parts=[slice(0, CHUNK)])
        damping(0, HIGH, sizes[:, 1], banks="y", parts=[slice(0, CHUNK)])
        low = held([P, 2, CHUNK], F32, "saved_low", at=8 * CHUNK)
        for t in LOW:
            pick_saved(low[:, t, :], t, slice(0, CHUNK))
            saved[t] = held([P, CHUNK], F32, f"saved{t}")[:]
            pick_saved(saved[t], t, second)
        finish_pair(LOW, [low[:, :, part] for part in halves])
        high = [held([P, 2, HALF], F32, f"saved_high{u}") for u in range(2)]
        for i, t in enumerate(HIGH):
            for u, part in enumerate(halves):
                pick_saved(high[u][:, i, :], t, part)
        finish_pair(HIGH, [picked[:] for picked in high])
        load_wo(0, 2, after="s_rows0")
        load_wo(2, 2, at=32 * CHUNK)
        load_wo(4, 2, after="saved_low")
        gains = held([P, S], F32, "gains", after="masked0")
        nc.sync.dma_start(gains[:], wgo)
        load_wo(6, 2, after="masked2")
        quantize_wo(0, 2)
        late = held([P, CHUNK + HALF], F32, "late", after="saved_high0")
        pick_saved(late[:, :CHUNK], 2, second)
        pick_saved(late[:, CHUNK:], 3, within(1, halves[0]))
        grouped = cast_wo(2, 4)
        h_words[0] = held([P, CHUNK], U32, "h0_words", at=11 * CHUNK)
        for part in halves:
            quantize_h(0, part)
        quantize_cast(2, grouped, 4)
        latest = held([P, HALF], F32, "latest", at=9 * CHUNK)
        pick_saved(latest[:], 3, within(1, halves[1]))
        y = held([P, HALF], F32, "y0_half0")
        embed(y[:], 0, 0, halves[0], weigh=True)
        nc.vector.tensor_copy(spots(0, 0, HALF), y[:])
        place_weighted(1, halves[0], "y1_half0")
        place_weighted(0, halves[1], "y0_half1")
        place_weighted(1, halves[1], "y1_half1")
        for n in range(2, EARLY - 1):
            place_weighted(n, slice(0, CHUNK), f"y{n}_0")
        h_grouped.append(held([P, CHUNK, PACK], BF16, "h1_unmasked", after=f"y{EARLY - 3}_0"))

        def plain_pair(pair, after=None, at=None):
            plain = held([P, CHUNK, 2], F32, f"plain{pair[0]}", after, at)
            for u, part in enumerate(halves):
                nc.scalar.copy(plain[:, part, :], project_pair(f"a{pair[0] + u}", wa_mx, pair, within(1, part)))
            nc.gpsimd.tensor_tensor(h_grouped[1][:, :, pair[0] : pair[1] + 1], plain[:], damp[pair, 1][:], ALU.mult)

        damping(1, LOW, held([P, CHUNK, 2], F32, "size0_1", at=CHUNK))
        plain_pair(LOW, at=15 * CHUNK)
        damping(1, HIGH, held([P, CHUNK, 2], F32, "size2_1", after="y1_half0"))
        plain_pair(HIGH, after="y1_half1")
        open_window(after="plain0")
        signs = held([P, PACK, CHUNK], BF16, "signs", after="size2_1")
        for t in LOW:
            nc.scalar.activation(signs[:, t, :], saved[t], ACT.Sign)
        high_signs = signs[:, 2:, :].rearrange("p t c -> p (t c)")
        nc.scalar.activation(high_signs[:, : CHUNK + HALF], late[:], ACT.Sign)
        nc.scalar.activation(high_signs[:, CHUNK + HALF :], latest[:], ACT.Sign)
        h_grouped.append(held([P, CHUNK, PACK], BF16, "h1_grouped"))
        for u, (part, engine) in enumerate(zip(halves, (nc.gpsimd, nc.vector))):
            mask = held([P, HALF, PACK], BF16, f"mask{u}")
            nc.scalar.activation(
                mask[:].rearrange("p (c i) j -> p c j i", i=WORDS_A_LINE),
                signs[:, :, part].rearrange("p j (c i) -> p c j i", i=WORDS_A_LINE),
                ACT.Relu,
            )
            engine.tensor_tensor(h_grouped[2][:, part, :], h_grouped[1][:, part, :], mask[:], ALU.mult)
        for part in halves:
            quantize_h(1, part)
        y = held([P, CHUNK], F32, "y_between", after="mask0")
        embed(y[:], EARLY - 1, 0)
        place(y[:], EARLY - 1, 0, CHUNK)
        for n in range(EARLY):
            y = held([P, CHUNK], F32, f"y{n}_1")
            embed(y[:], n, 1)
            place(y[:], n, CHUNK, CHUNK)
            store(n)
            if n == 0:
                quantize_wo(6, 2, after="mask1", words_after="y_between")
        for n in range(EARLY, N // P):
            y = ring.tile([P, S], F32, name="y")
            for c in range(CHUNKS):
                embed(y[:, c * CHUNK : (c + 1) * CHUNK], n, c)
            place(y[:], n, 0, S)
            store(n)
